import numpy as np, ml_dtypes
CORES = [8,136,40,168]
N = 4
BF = ml_dtypes.bfloat16
def gentries(a):
    return np.ascontiguousarray(a.reshape(8, 16, -1).transpose(0, 2, 1)).reshape(8, -1)
def gtable(e):
    e = np.asarray(e); return np.ascontiguousarray(e.reshape(8, -1, 16).transpose(0, 2, 1)).reshape(128, -1).astype(np.int32)
SO, RO, CR, CL, CF, TR = 384, 640, 384, 176, 80, 4
S, R = N * SO, N * RO
TH = 24
EPS = np.float32(0.125); UNDER = np.nextafter(EPS, np.float32(0)); LEAST = np.float32(0.00390625)
def expo(rng, lo, hi, *shape):
    return np.exp2(lo + (hi - lo) * rng.random(shape)).astype(np.float32)
def mark(rng, cnt):
    return np.argsort(rng.random((N, 8, 16, SO)), axis=2) < cnt[:, :, None, :]
def rows(rng, cnt):
    hi = np.maximum(expo(rng, -3, 0, N, 8, 16, SO), EPS); lo = np.minimum(expo(rng, -8, -3.1, N, 8, 16, SO), UNDER)
    return np.where(mark(rng, cnt), hi, lo)
def alive(cnt):
    return 2 * cnt + np.roll(cnt, -1, axis=1) >= TH
def lanes(rng, n):
    v = rng.random((N, 8, SO)); v[1::2, :, SO - 1] = -1.0
    return np.where(np.argsort(np.argsort(v, axis=2), axis=2) < n[:, :, None], 16, 0)
def react(rng, live, n):
    a = rng.integers(0, S, (N, 8, RO)); b = rng.integers(0, S, (N, 8, RO))
    for g in range(8):
        lv = np.flatnonzero(live[:, g]); dd = np.flatnonzero(~live[:, g])
        if lv.size == 0 or dd.size == 0: continue
        for q in range(N):
            v = rng.random(RO)
            if q % 2: v[RO - 1] = -1.0
            s = np.argsort(v)[:int(n[q, g])]; x = rng.choice(dd, (2, RO))
            x[0, s] = rng.choice(lv, len(s)); x[1, s] = rng.integers(0, S, len(s))
            x[1] = np.where(rng.random(RO) < 0.1, x[0], x[1]); sw = rng.random(RO) < 0.5
            a[q, g] = np.where(sw, x[1], x[0]); b[q, g] = np.where(sw, x[0], x[1])
    return a, b
def parts(rng):
    c = expo(rng, -0.5, 0.5, N, 8, 1, SO) * expo(rng, -0.25, 0.25, N, 8, 16, SO)
    share = rng.choice(np.array([0.3, 0.45, 0.6, 0.75]), (N, 8, 1))
    cnt = np.where(rng.random((N, 8, SO)) < share, rng.integers(9, 17, (N, 8, SO)), rng.integers(0, 8, (N, 8, SO)))
    e = rows(rng, cnt)
    goal = (rng.random((N, 8, 1, SO)) < 0.05) & (rng.random((N, 8, 16, SO)) < 0.75)
    tau = np.where(goal, np.float32(1), expo(rng, -8, -4, N, 8, 16, SO))
    hot = ((1.0 + 0.25 * rng.permutation(8)) * 0.0625).reshape(1, 8, 1, 1)
    k = np.where(rng.random((N, 8, 1, RO)) < hot, expo(rng, -0.75, 0.5, N, 8, 1, RO), expo(rng, -5, -3, N, 8, 1, RO)) * expo(rng, -0.5, 0.5, N, 8, 16, RO)
    return [c, e, tau, k, rng.integers(0, S, (N, 8, RO)), rng.integers(0, S, (N, 8, RO)), rng.integers(0, R, (N, 8, SO, 16)), rng.integers(0, S, (N, 8, SO, 16))]
def pack(c, e, tau, k, a, b, rx, ot):
    fl = lambda x, lo, hi: np.ascontiguousarray(np.clip(x.astype(np.float32), np.float32(lo), np.float32(hi)).reshape(N, 128, -1))
    ls = lambda x: np.stack([gtable(v.reshape(8, -1)) for v in x])
    return {"cin": fl(c, 0.125, 8), "ein": fl(e, 0.00390625, 1), "tau": fl(tau, 0.00390625, 1), "kin": fl(k, 0.015625, 2), "ra": ls(a), "rb": ls(b), "rx": ls(rx), "ot": ls(ot)}
def setup_inputs(rng):
    return pack(*parts(rng))
def setup_inputs_spread(rng):
    p = parts(rng)
    p[0] = np.clip(expo(rng, -3, 3, N, 8, 1, SO) * expo(rng, -0.5, 0.5, N, 8, 16, SO), 0.125, 8)
    p[3] = np.clip(expo(rng, -6, -1, N, 8, 1, RO) * expo(rng, -0.5, 0.5, N, 8, 16, RO), 0.015625, 2)
    return pack(*p)
def atend(rng, x, top, share):
    return np.where(rng.random(x.shape) < 0.72, np.where(rng.random(x.shape) < share, top, 0), x)
def setup_inputs_ends(rng):
    c, e, tau, k, a, b, rx, ot = parts(rng); q = N - 1
    n = rng.choice(np.array([CL // 2, CL - 1, CL, CL + 1, SO // 2, SO - CF]), (N, 8)); n[q] = CL - 1
    cnt = lanes(rng, n); mix = rng.random((N, 8, SO)) < 0.2; mix[q] = False
    cnt = np.where(mix, rng.choice(np.array([1, 7, 8, 11, 12, 15]), (N, 8, SO)), cnt)
    cnt[0, 7, :2] = 16; cnt[q, 7, SO - 2:] = 16
    e = np.where(mark(rng, cnt), np.float32(1), LEAST)
    ch = lambda w, share, hi, lo: rng.random((N, 8, 16, w)) < np.where(rng.random((N, 8, 1, w)) < share, hi, lo)
    c = np.where(ch(SO, 0.15, 0.9, 0.05), 8.0, 0.125); k = np.where(ch(RO, 0.25, 0.9, 0.08), 2.0, 0.015625); tau = np.where(ch(SO, 0.06, 0.9, 0.01), np.float32(1), LEAST)
    a = atend(rng, a, S - 1, 0.5); b = atend(rng, b, S - 1, 0.5); ot = atend(rng, ot, S - 1, 0.5)
    rx = atend(rng, rx, R - 1, np.where(rng.random((N, 8, SO, 1)) < 0.3, 0.5, 0.02))
    a[0, :, 0] = 0; b[0, :, 0] = 0; k[0, :, :, 0] = 0.015625; c[0, :, :, 0] = 0.125
    a[q, :, RO - 1] = S - 1; b[q, :, RO - 1] = S - 1; k[q, :, :, RO - 1] = 2.0; c[q, :, :, SO - 1] = 8.0
    rx[q, :, SO - 1, :8] = R - 1; rx[q, :, SO - 1, 8:] = 0; rx[q, :, SO - 2, :8] = 0; rx[q, :, SO - 2, 8:] = R - 1
    rx[0, :, 0, :8] = 0; rx[0, :, 0, 8:] = R - 1; rx[0, :, 1, :8] = R - 1; rx[0, :, 1, 8:] = 0
    c[q, 7, :, SO - 2] = 8.0; c[0, 7, :, 1] = 0.125
    a[q, :, RO - 17:RO - 1] = S - 1; b[q, :, RO - 17:RO - 1] = S - 1; k[q, :, :, RO - 17:RO - 1] = 2.0 - 0.03125 * rng.random((8, 16, 16))
    for g in range(8):
        h = rng.permutation(np.flatnonzero(cnt[q, g, :SO - 2] == 16))[:8]
        c[q, g][:, h] = 4.0; rx[q, g, h] = R - 17 + np.argsort(rng.random((len(h), 16)), axis=1)
    return pack(c, e, tau, k, a, b, rx, ot)
def setup_inputs_corners(rng):
    p = parts(rng); q = N - 1
    menu = np.array([0, 1, CL - 1, CL, CL + 1, SO, SO - CF, SO - CF + 1, SO - CF - 1, SO - 1, SO // 2]); n = rng.choice(menu, (N, 8))
    n[0] = menu[:8]; n[1] = rng.permutation(menu)[:8]; n[q] = np.where(np.arange(8) % 2 == 1, CL, SO - CF)
    m = np.array([0, 1, CR - 1, CR, CR + 1, RO, RO - 1, CR]); rn = rng.choice(m, (N, 8)); rn[0] = rng.permutation(m); rn[q] = m
    cnt = lanes(rng, n); p[1] = rows(rng, cnt); p[4], p[5] = react(rng, alive(cnt), rn)
    own = (np.arange(N)[:, None] * SO + np.arange(SO)[None, :])[:, None, :, None]
    z = rng.random((N, 8, SO, 16)); p[7] = np.where(z < 0.1, own, np.where(z < 0.15, 0, np.where(z < 0.2, S - 1, p[7])))
    z = rng.random((N, 8, SO, 16)); p[6] = np.where(z < 0.05, 0, np.where(z < 0.1, R - 1, p[6]))
    return pack(*p)
def setup_inputs_crowd(rng):
    c, e, tau, k, a, b, rx, ot = parts(rng)
    for g in range(8):
        x, y = int(rng.integers(0, S)), int(rng.integers(0, R))
        if g == 0: x, y = S - 1, R - 1
        if g == 1: x, y = 0, 0
        e[x // SO, g, :, x % SO] = 1.0 if g < 4 else LEAST; tau[x // SO, g, :, x % SO] = 1.0 if g < 4 else LEAST
        if g % 4 == 0: a[:, g] = x; b[:, g] = x; rx[:, g] = y; ot[:, g] = x
        if g % 4 == 1:
            j = int(rng.integers(0, RO)); a[:, g, :j] = x; a[:, g, j + 1:] = x; b[:, g, :j] = x; b[:, g, j + 1:] = x
            rx[:, g, :, :15] = y; ot[:, g, :, :15] = x
        if g % 4 == 2:
            sp = np.array([x, (x + 1) % S, (x + SO) % S]); rc = np.array([y, (y + 1) % R, (y + RO) % R])
            a[:, g] = rng.choice(sp, (N, RO)); b[:, g] = rng.choice(sp, (N, RO)); rx[:, g] = rng.choice(rc, (N, SO, 16)); ot[:, g] = rng.choice(sp, (N, SO, 16))
        if g % 4 == 3: a[:, g] = x; rx[:, g, :, :8] = y
    return pack(c, e, tau, k, a, b, rx, ot)
def setup_inputs_calm(rng):
    p = parts(rng); i = 3 * np.arange(N)[:, None] + np.arange(8)[None, :]; q = N - 1
    n = np.array([0, 1, 2, 3, SO - 1, SO, CL, CL + 1])[i % 8]; n[1, 4:] = CL
    cnt = lanes(rng, n); keep = np.array(cnt[1, 4:])
    cnt[1::2] = rng.choice(np.array([0, 1, 2, 7, 8, 11, 12, 15, 16]), cnt[1::2].shape)
    v = rng.permutation(SO // 4); z, u = int(v[0]), int(v[1]); chain = v[2:7]; lapse = v[7:15]; rise = v[15:23]
    gg = SO // 4 + rng.permutation(CL - SO // 4)[:8]
    cnt[1, 4:] = keep; cnt[1, :2] = 16; cnt[1][:2, chain] = 0; cnt[1, 2] = 0; cnt[1, 3] = 16
    cnt[q][:, gg] = 16; cnt[q][:, z] = 16; cnt[q][:, u] = 0
    half = rng.random((N, 8, 16, SO)) < 0.5
    p[2] = np.where(mark(rng, cnt), np.where(half, EPS, np.float32(1)), np.where(half, UNDER, expo(rng, -8, -6, N, 8, 16, SO))); p[1] = np.array(p[2])
    p[0] = expo(rng, -1, 0.5, N, 8, 1, SO) * expo(rng, -0.25, 0.25, N, 8, 16, SO); p[3] = expo(rng, -6, -5.5, N, 8, 16, RO)
    lv = alive(cnt); p[4], p[5] = react(rng, lv, np.array([0, 1, 2, 3, RO - 1, RO, CR - 1, CR])[(i + 2) % 8])
    c, e, tau, k, a, b, rx, ot = p
    for x in (a, b):
        x[:, 2] = np.where(np.isin(x[:, 2], SO + lapse), q * SO + u, x[:, 2]); x[:, 3] = np.where(np.isin(x[:, 3], SO + rise), q * SO + z, x[:, 3])
        x[1, 2] = SO + rng.choice(lapse, RO)
    e[1, 2][:, lapse] = 1.0; tau[1, 2][:, lapse] = LEAST
    e[1, 3][:, rise] = LEAST
    for g in range(8):
        d = 2.0 ** -int(rng.integers(13, 20)); y, y2 = [int(x) for x in rng.permutation(RO)[:2]]; s = int(rng.integers(0, 16))
        flat = lv[:, g].reshape(-1)
        for j, rate in ((y, 0.5 * (1.0 - d)), (y2, 0.875)):
            x = q * SO + (z if flat[a[q, g, j]] or flat[b[q, g, j]] else u)
            a[q, g, j] = x; b[q, g, j] = x; k[q, g, :, j] = rate
        rx[:, g] = np.where((rx[:, g] == q * RO + y) | (rx[:, g] == q * RO + y2), rx[:, g] - q * RO, rx[:, g])
        c[q, g][:, [z, u]] = 1.0; rx[q, g, z, 8:] = rx[q, g, z, :8]
        e[q, g, :, z] = 0.25 * (1.0 + d); tau[q, g, :, z] = 0.25 * (1.0 + d)
        tau[q, g][:, gg] = LEAST; e[q, g][:, gg] = EPS; rx[q, g, gg, s] = q * RO + y; ot[q, g, gg, s] = q * SO + z
        if g < 2:
            src = q * SO + int(gg[0])
            for x in chain:
                e[1, g, :, x] = LEAST; tau[1, g, :, x] = LEAST; rx[1, g, x] = q * RO + y2; ot[1, g, x] = src; src = SO + int(x)
        if g >= 4:
            ot[1, g] = q * SO + rng.integers(0, SO, (SO, 16)); ot[1, g, SO - 1, 15] = q * SO + z; rx[1, g, SO - 1, 15] = q * RO + y
            tau[1, g, :, SO - 1] = LEAST; e[1, g, :, SO - 1] = EPS; c[1, g, :, SO - 1] = 1.0
    return pack(c, e, tau, k, a, b, rx, ot)
def check_inputs(d):
    bad = []
    for k, lo, hi in (("cin", 0.125, 8), ("ein", 0.00390625, 1), ("tau", 0.00390625, 1), ("kin", 0.015625, 2), ("ra", 0, S - 1), ("rb", 0, S - 1), ("rx", 0, R - 1), ("ot", 0, S - 1)):
        if not (np.min(d[k]) >= lo and np.max(d[k]) <= hi): bad.append("range of " + k)
    return bad
def first(flag, start, cap):
    f = np.roll(flag, -start, axis=2).astype(np.int64); before = np.add.accumulate(f, axis=2) - f
    return np.roll((f == 1) & (before < cap), start, axis=2)
def reference(cin, ein, tau, kin, ra, rb, rx, ot):
    F = np.float32
    glue = lambda x: np.array(x.astype(F).reshape(N, 8, 16, -1).transpose(1, 2, 0, 3), order="C").reshape(8, 16, -1)
    lst = lambda x: np.stack([gentries(v) for v in x]).astype(np.int64).transpose(1, 0, 2).reshape(8, -1)
    C, E, low, k = glue(cin), glue(ein), glue(tau), glue(kin)
    A, B = lst(ra), lst(rb); RX, OT = lst(rx).reshape(8, S, 16), lst(ot).reshape(8, S, 16)
    w = np.stack([(k[g] * C[g][:, A[g]]) * C[g][:, B[g]] for g in range(8)])
    for t in range(TR):
        cnt = np.add.reduce((E >= EPS).astype(np.int64), axis=1)
        live = 2 * cnt + np.roll(cnt, -1, axis=0) >= TH
        act = np.take_along_axis(live, A, 1) | np.take_along_axis(live, B, 1)
        mr = first(act.reshape(8, N, RO), (t * (RO // 4)) % RO, CR).reshape(8, R)
        ml = first(live.reshape(8, N, SO), (t * (SO // 4)) % SO, CL).reshape(8, S)
        mf = first(~live.reshape(8, N, SO), (t * (SO // 4)) % SO, CF).reshape(8, S)
        for g in range(8):
            j = np.flatnonzero(mr[g]); w[g][:, j] = (k[g][:, j] * C[g][:, A[g, j]]) * C[g][:, B[g, j]]
        for sweep in range(2):
            for g in range(8):
                s = np.flatnonzero(ml[g] | mf[g])
                p = E[g][:, OT[g, s].reshape(-1)] * np.minimum(w[g][:, RX[g, s].reshape(-1)], F(1))
                E[g][:, s] = np.maximum(low[g][:, s], np.max(p.reshape(16, len(s), 16), axis=2))
        for g in range(8):
            s = np.flatnonzero(ml[g]); x = w[g][:, RX[g, s].reshape(-1)].reshape(16, len(s), 16)
            for level in range(3): x = x[:, :, 0::2] + x[:, :, 1::2]
            C[g][:, s] = np.minimum(np.maximum(C[g][:, s] + (x[:, :, 0] - x[:, :, 1]) * F(0.125), F(0.125)), F(8))
    back = lambda x: np.ascontiguousarray(x.reshape(8, 16, N, -1).transpose(2, 0, 1, 3)).reshape(N, 128, -1)
    return {"yc": back(C), "ye": back(E), "yw": back(w)}

@@ -1,0 +1,527 @@
+from concourse.mybir import AluOpType, ActivationFunctionType
+
+N, SO, RO, TR = 4, 384, 640, 4
+CH1 = [(0, 32), (32, 96), (96, 176), (176, 256)]
+CH2 = [(0, 64), (64, 128)]
+CH3 = [(128, 192), (192, 256)]
+HY = 128
+F, B, I, U = "float32", "bfloat16", "int32", "uint16"
+SCRATCH = {
+    "ps": ("psum", [128, 4096], F),
+    "sa": ("sbuf", [128, 3 * 384], F), "la": ("sbuf", [128, 4 * 384], F), "sab": ("sbuf", [128, 4 * 80], I),
+    "sb": ("sbuf", [128, 384], F), "si": ("sbuf", [128, 384], I), "sj": ("sbuf", [128, 384], I), "stau": ("sbuf", [128, 288], F),
+    "sk": ("sbuf", [128, 384], F), "lb": ("dram", [4, 128, 96], F), "lc": ("dram", [4, 128, 96], F),
+    "ew": ("sbuf", [128, 1536], F), "cw": ("sbuf", [128, 1536], F), "wr": ("sbuf", [128, 2560], F), "wm": ("sbuf", [128, 2560], F),
+    "kab": ("sbuf", [128, 720], F), "tau_o": ("sbuf", [128, 384], F), "pkf": ("sbuf", [128, 384], F), "pk": ("sbuf", [128, 384], I),
+    "co": ("sbuf", [128, 384], F), "ct": ("sbuf", [128, 384], F), "wb0": ("sbuf", [128, 1280], F), "wb1": ("sbuf", [128, 1280], F),
+    "wt": ("sbuf", [128, 640], F), "ec0": ("sbuf", [128, 4480], F), "ec1": ("sbuf", [128, 4480], F), "et": ("sbuf", [128, 384], F),
+    "dw": ("sbuf", [128, 640], F), "pm": ("sbuf", [128, 640], F), "taum": ("sbuf", [128, 384], F), "lst": ("sbuf", [128, 640], I),
+    "lo_i": ("sbuf", [128, 256], I), "rx16": ("sbuf", [128, 256], U), "ot16": ("sbuf", [128, 256], U),
+    "wg": ("sbuf", [128, 4096], F), "prod": ("sbuf", [128, 4096], F), "msk": ("sbuf", [128, 1280], B), "eg": ("sbuf", [128, 2048], F),
+    "pe16": ("sbuf", [128, 24], U), "mz": ("sbuf", [128, 640], B),
+    "xg": ("sbuf", [128, 2816], F), "y1": ("sbuf", [128, 704], F), "z1": ("sbuf", [128, 352], F), "p1": ("sbuf", [128, 176], F),
+    "ind": ("sbuf", [128, 384], B), "nw": ("sbuf", [128, 96], B), "nr": ("sbuf", [128, 96], B), "ll": ("sbuf", [128, 128], B),
+    "xab": ("sbuf", [128, 1280], B), "oh": ("sbuf", [128, 1280], B), "act": ("sbuf", [128, 40], B), "csr": ("sbuf", [128, 40], B),
+    "css": ("sbuf", [128, 24], B), "sm": ("sbuf", [128, 10, 40], F), "wo16": ("sbuf", [128, 40], U), "pos16": ("sbuf", [128, 24], U),
+    "abi": ("sbuf", [128, 80], I), "abt": ("sbuf", [128, 160], I), "ab16": ("sbuf", [128, 80], U), "abd16": ("sbuf", [128, 80], U), "abm16": ("sbuf", [128, 80], U),
+    "iv": ("sbuf", [128, 640], F), "agi": ("sbuf", [128, 640], F), "ma": ("sbuf", [128, 640], B), "mb": ("sbuf", [128, 640], B), "mt": ("sbuf", [128, 640], B),
+    "we": ("sbuf", [128, 2048], B), "blk": ("sbuf", [128, 128], B), "trn": ("sbuf", [128, 128], B), "trn2": ("sbuf", [128, 128], B),
+    "ci": ("sbuf", [128, 4], I), "cf": ("sbuf", [128, 8], F), "io2": ("sbuf", [128, 200], F), "g8": ("sbuf", [128, 8], B), "idg": ("sbuf", [128, 16], F),
+    "j40": ("sbuf", [128, 40], F), "dump": ("sbuf", [128, 24], F), "k1": ("sbuf", [128, 96], F), "k2": ("sbuf", [128, 96], F), "one": ("sbuf", [128, 40], B),
+    "so": ("sbuf", [128, 3 * 256], F), "lo": ("sbuf", [128, 4 * 256], F), "se": ("sbuf", [128, 3 * 96], F), "le": ("sbuf", [128, 4 * 96], F),
+}
+SEMAPHORES = (["qv", "qs", "qp", "qg", "rl", "lbo", "lco", "lbt", "lbp", "ldb", "ldi", "st"]
+              + ["%s%d" % (n, k) for n in ("lda", "ldab", "ara", "arb", "arc", "arn", "aro", "are", "pko") for k in range(4)])
+SHAPES = {n: v[1] for n, v in SCRATCH.items()}
+A = AluOpType
+ACT = ActivationFunctionType
+XCH = [(0, 64), (64, 128), (128, 176)]
+
+
+def rank_program(g, core, T, topo):
+    r = T.rank_of(core)
+    if r is None:
+        return
+    Q = {"g": g, "v": g.vector, "s": g.scalar, "p": g.tensor, "y": g.sync}
+    cnt = {"qv": 0, "qs": 0, "qp": 0, "qg": 0}
+    known = {q: {} for q in Q}
+    log = {}
+
+    def ap(name, *idx):
+        shape = SHAPES[name]
+        idx = list(idx) + [slice(None)] * (len(shape) - len(idx))
+        lo, hi, stride, rng = 0, 0, 1, []
+        for k in range(len(shape) - 1, -1, -1):
+            ix = idx[k]
+            rr = range(shape[k])[ix] if isinstance(ix, slice) else range(ix, ix + 1)
+            if k == 0:
+                rng = [rr[0], rr[-1] + 1]
+            else:
+                lo += rr[0] * stride
+                hi += rr[-1] * stride
+                stride *= shape[k]
+        if name == "ps":
+            reg = (name, 0, 128, lo // 512 * 512, hi // 512 * 512 + 512, (lo, hi + 1))
+        elif SCRATCH[name][0] == "dram":
+            reg = (name, rng[0], rng[1], 0, 1, (0, 1))
+        else:
+            reg = (name, rng[0], rng[1], lo, hi + 1, (lo, hi + 1))
+        return {"ap": T[name][tuple(idx)], "regs": [reg], "offs": []}
+
+    def c(name, a, b, step=None, p=None):
+        ps_ = slice(None) if p is None else slice(p[0], p[1])
+        return ap(name, ps_, slice(a, b, step))
+
+    def ind(win, off):
+        return {"ap": win["ap"].indirect(off["ap"]), "regs": win["regs"], "offs": off["regs"]}
+
+    def wait(q, tok):
+        sem, val, clock = tok
+        if val is None:
+            val = cnt[sem]
+        if known[q].get(sem, 0) >= val:
+            return
+        Q[q].wait_ge(T.sem[sem], val)
+        for s_, v_ in list(clock.items()) + [(sem, val)]:
+            if known[q].get(s_, 0) < v_:
+                known[q][s_] = v_
+
+    def order(q, reads, writes, tok_of, comp=False):
+        acc = [(x, False) for a_ in reads for x in a_["regs"] + a_["offs"]]
+        acc += [(x, True) for a_ in writes for x in a_["regs"]] + [(x, False) for a_ in writes for x in a_["offs"]]
+        need = []
+        for (name, p0, p1, c0, c1, p0x), wr in acc:
+            for e in log.get(name, []):
+                if e[0] < p1 and p0 < e[1] and e[2] < c1 and c0 < e[3]:
+                    if name != "ps":
+                        if wr or e[4]:
+                            need.append(e[6])
+                    elif e[5] != q:
+                        need.append(e[6])
+                    elif q != "p" and (wr or e[4]) and e[0] < p1 and e[7] < p0x[1] and p0x[0] < e[8]:
+                        need.append(e[6])
+        need.sort(key=lambda t_: -(t_[1] or 0))
+        for t_ in need:
+            wait(q, t_)
+        tok = tok_of()
+        for (name, p0, p1, c0, c1, p0x), wr in acc:
+            old = log.get(name, [])
+            if name == "ps":
+                old = [e for e in old if not (c0 <= e[2] and e[3] <= c1 and (e[5] != q or q == "p"))]
+            elif wr:
+                old = [e for e in old if not (p0 <= e[0] and e[1] <= p1 and c0 <= e[2] and e[3] <= c1)]
+            log[name] = old + [[p0, p1, c0, c1, wr, q, tok, p0x[0], p0x[1]]]
+        return tok
+
+    def op(q, fn, reads, writes):
+        def emit():
+            sem = "q" + q
+            fn().then_inc(T.sem[sem], 1)
+            cnt[sem] += 1
+            return (sem, cnt[sem], dict(known[q]))
+        return order(q, reads, writes, emit, True)
+
+    def dma(q, out, in_, sem):
+        def emit():
+            Q[q].dma_start(out["ap"], in_["ap"]).then_inc(T.sem[sem], 16)
+            cnt[sem] = cnt.get(sem, 0) + 16
+            return (sem, None, dict(known[q]))
+        return order(q, [in_], [out], emit)
+
+    def ext(a_):
+        return {"ap": a_, "regs": [], "offs": []}
+
+    def engines(d):
+        return topo.engines(core, T.cores[d])
+
+    def send(d, out, in_, sem):
+        def emit():
+            rid, pid = topo.addr(T.cores[d], core)
+            g.remote_dma(out["ap"], in_["ap"], T.sem[sem], T.sem.rl, pid, rid, topo.mask(core, T.cores[d]))
+            cnt["rl"] = cnt.get("rl", 0) + len(engines(d))
+            return ("rl", None, {})
+        return order("g", [in_], [], emit)
+
+    def lands(a_, sem, n):
+        cnt[sem] = n
+        for name, p0, p1, c0, c1, _ in a_["regs"]:
+            log.setdefault(name, []).append([p0, p1, c0, c1, True, "far", (sem, n, {}), c0, c1])
+
+    def sc_(x):
+        return x["ap"] if isinstance(x, dict) else x
+
+    def tt(out, a_, b_, o):
+        return op("v", lambda: g.vector.tensor_tensor(out["ap"], a_["ap"], b_["ap"], o), [a_, b_], [out])
+
+    def ts(out, a_, s1, o1, s2=None, o2=None):
+        rd = [a_] + [x for x in (s1, s2) if isinstance(x, dict)]
+        if o2 is None:
+            return op("v", lambda: g.vector.tensor_scalar(out["ap"], a_["ap"], sc_(s1), None, o1), rd, [out])
+        return op("v", lambda: g.vector.tensor_scalar(out["ap"], a_["ap"], sc_(s1), sc_(s2), o1, o2), rd, [out])
+
+    def cp(q, out, a_, scale=None):
+        if q == "v":
+            return op("v", lambda: g.vector.tensor_copy(out["ap"], a_["ap"]), [a_], [out])
+        if scale is None:
+            return op("s", lambda: g.scalar.activation(out["ap"], a_["ap"], ACT.Copy), [a_], [out])
+        return op("s", lambda: g.scalar.activation(out["ap"], a_["ap"], ACT.Copy, scale=scale), [a_], [out])
+
+    def ms(out, val):
+        return op("v", lambda: g.vector.memset(out["ap"], val), [], [out])
+
+    def scan(out, a_, b_, init, o1, o2):
+        rd = [a_, b_] + ([init] if isinstance(init, dict) else [])
+        return op("v", lambda: g.vector.tensor_tensor_scan(out["ap"], a_["ap"], b_["ap"], sc_(init), o1, o2), rd, [out])
+
+    def mm(out, lhs, rhs, start=True, stop=True):
+        return op("p", lambda: g.tensor.matmul(out["ap"], lhs["ap"], rhs["ap"], start, stop), [lhs, rhs], [out])
+
+    def iota(out, pat, base, cm, flt=True):
+        if flt:
+            return op("g", lambda: g.iota(out["ap"], pat, base, cm, allow_small_or_imprecise_dtypes=True), [], [out])
+        return op("g", lambda: g.iota(out["ap"], pat, base, cm), [], [out])
+
+    def blkp(q):
+        return (32 * q, 32 * q + 32)
+
+    def bank(b, a_=0, n=512):
+        return c("ps", 512 * b + a_, 512 * b + a_ + n)
+
+    ne = len(engines((r + 1) % N))
+    others = [(r + k) % N for k in (1, 2, 3)]
+    for s in others:
+        lands(c("la", 384 * s, 384 * s + 384), "ara%d" % s, ne)
+        lands(ap("lb", s), "arb%d" % s, ne)
+        lands(ap("lc", s), "arc%d" % s, ne)
+        lands(c("lo", 256 * s, 256 * s + 256), "aro%d" % s, ne)
+    for t in range(TR):
+        lands(c("nr", 24 * t, 24 * t + 24), "arn%d" % t, ne)
+
+    def pack(d, a_, b_, p=None):
+        k = others.index(d) if d != r else None
+        return c("la", 384 * r + a_, 384 * r + b_, p=p) if d == r else c("sa", 384 * k + a_, 384 * k + b_, p=p)
+
+    for d in others + [r]:
+        rows = slice(32 * d, 32 * d + 32)
+        dma("y", c("sab", 80 * d, 80 * d + 40, p=blkp(3)), ext(T.ra[rows, :]), "ldab%d" % d)
+        dma("s", c("sab", 80 * d + 40, 80 * d + 80, p=blkp(3)), ext(T.rb[rows, :]), "ldab%d" % d)
+        dma("y", pack(d, 0, 384, blkp(0)), ext(T.ein[rows, :]), "lda%d" % d)
+        dma("s", pack(d, 0, 384, blkp(1)), ext(T.cin[rows, :]), "lda%d" % d)
+        dma("y", pack(d, 0, 384, blkp(2)), ext(T.kin[rows, 0:384]), "lda%d" % d)
+        dma("s", pack(d, 0, 256, blkp(3)), ext(T.kin[rows, 384:640]), "lda%d" % d)
+    for d in others + [r]:
+        rows = slice(32 * d, 32 * d + 32)
+        dma("y", c("si", 96 * d, 96 * d + 96), ext(T.rx[rows, :]), "ldi")
+        dma("s", c("sj", 96 * d, 96 * d + 96), ext(T.ot[rows, :]), "ldi")
+    for k, d in enumerate(others):
+        dma("y", c("stau", 96 * k, 96 * k + 96), ext(T.tau[32 * d:32 * d + 32, :]), "ldb")
+    dma("y", ap("lc", r), ext(T.tau[32 * r:32 * r + 32, :]), "lco")
+
+    iota(c("ci", 0, 1), [[0, 1]], 0, 1, False)
+    iota(c("io2", 0, 128), [[16, 8], [0, 16]], 0, 0)
+    iota(c("iv", 0, 512), [[-32, 4], [0, 4], [-1, 32]], 0, 1)
+    iota(c("iv", 512, 640), [[-1, 128]], 0, 1)
+    for d in others + [r]:
+        ms(pack(d, 336, 384, blkp(3)), 0.0)
+    ms(c("we", 0, 2048), 0.0)
+    ts(c("ci", 1, 2), c("ci", 0, 1), 112, A.bitwise_and)
+    ts(c("ci", 2, 3), c("ci", 0, 1), 15, A.bitwise_and)
+    ts(c("ci", 3, 4), c("ci", 0, 1), 16, A.bitwise_and)
+    cp("v", c("cf", 0, 4), c("ci", 0, 4))
+    kg16, pmod = c("cf", 1, 2), c("cf", 2, 3)
+    ts(c("g8", 0, 8), c("io2", 0, 128, 16), kg16, A.is_equal)
+    for e in range(16):
+        cp("s", c("we", 128 * e + e, 128 * e + 128, 16), c("g8", 0, 8))
+    for d in others + [r]:
+        cp("v", pack(d, 256, 336, blkp(3)), c("sab", 80 * d, 80 * d + 80, p=blkp(3)))
+        if d != r:
+            send(d, c("la", 384 * r, 384 * r + 384), pack(d, 0, 384), "ara%d" % r)
+        if d == others[0]:
+            iota(c("io2", 128, 144), [[1, 16]], 0, 0)
+            iota(c("io2", 144, 184), [[16, 40]], 0, 1)
+            ts(c("agi", 0, 640), c("iv", 0, 640), 0.0, A.is_equal)
+        if d == others[1]:
+            ts(c("blk", 0, 128), c("io2", 0, 128), kg16, A.is_equal)
+            ts(c("trn2", 0, 128), c("io2", 0, 128), kg16, A.is_equal, -1.0, A.mult)
+            ms(c("mz", 0, 640), 0.0)
+            ms(c("lst", 0, 640), 0)
+            cp("s", c("mt", 0, 640), c("agi", 0, 640), 2.0)
+
+    def asel(out, a_, pat, cmp_, fill, base):
+        return op("g", lambda: g.affine_select(out["ap"], a_["ap"], pat, cmp_, fill, base, 1), [a_], [out])
+
+    def live_sel(x):
+        o, st, b0 = 128 * x, (-32 if x == 4 else 0), (0 if x == 4 else -32 * x)
+        asel(c("ma", o, o + 128), c("mt", o, o + 128), [[st, 4], [1000, 2], [-1, 16]], A.not_equal, 1.0, b0 - 16)
+        asel(c("mb", o, o + 128), c("mz", o, o + 128), [[st, 4], [-1000, 2], [-1, 16]], A.not_equal, 1.0, b0 + 1000)
+
+    live_sel(4)
+    asel(c("trn", 0, 128), c("trn2", 0, 128), [[-1, 128]], A.is_gt, 0.0, 0)
+    asel(c("trn2", 0, 128), c("trn", 0, 128), [[-1, 128]], A.not_equal, -1024.0, 0)
+
+    def consts(k):
+        if k == 0:
+            ts(c("sk", 0, 384), c("si", 0, 384), 4096.0, A.mult)
+            tt(c("sb", 0, 384), c("sk", 0, 384), c("sj", 0, 384), A.add)
+            for d in others:
+                send(d, ap("lb", r), c("sb", 96 * d, 96 * d + 96), "arb%d" % r)
+            dma("y", ap("lb", r), c("sb", 96 * r, 96 * r + 96), "lbo")
+            cp("s", c("dw", 0, 640), c("iv", 0, 640), 0.0)
+        if k == 1:
+            ts(c("j40", 0, 40), c("io2", 144, 184), kg16, A.subtract)
+            ts(c("idg", 0, 16), c("io2", 128, 144), pmod, A.is_equal)
+            ms(c("one", 0, 40), 1.0)
+            ts(c("dump", 0, 24), c("j40", 0, 24), 256.0, A.add)
+            for t in range(4):
+                ts(c("k1", 30 * t, 24 * t + 24), c("j40", 6 * t, 24), -96.0 * t, A.add)
+                if t:
+                    ts(c("k1", 24 * t, 30 * t), c("j40", 0, 6 * t), 384.0 - 96.0 * t, A.add)
+            ms(c("pm", 0, 256), 1.0)
+            ts(c("k2", 0, 96), c("k1", 0, 96), -1.0, A.mult, 79.0, A.add)
+            cp("s", c("pm", 256, 640), c("iv", 256, 640), 0.0)
+        if k == 2:
+            ms(c("msk", 0, 1280), 1.0)
+            ms(c("msk", 0, 1280, 16), 0.0)
+
+    def agm(q):
+        return c("agi", 128 * q, 128 * q + 128)
+
+    for k, s in enumerate([r] + others[::-1]):
+        o = 384 * s
+        mm(bank(k, 0, 384), agm(1), c("la", o, o + 384))
+        cp("v", c("ec0", 4096, 4480, p=blkp(s)), c("la", o, o + 384, p=blkp(0)))
+        cp("s", c("kab", 384, 720, p=blkp(s)), c("la", o, o + 336, p=blkp(3)))
+        cp("s", c("kab", 0, 384, p=blkp(s)), c("la", o, o + 384, p=blkp(2)))
+        if k < 3:
+            mm(bank(4 + k, 0, 384), agm(0), c("la", o, o + 384))
+            cp("v", c("cw", o, o + 384), bank(k, 0, 384))
+            cp("s", c("co", 0, 384, p=blkp(s)), c("la", o, o + 384, p=blkp(1)))
+            cp("s", c("ew", o, o + 384), bank(4 + k, 0, 384))
+            consts(k)
+    dma("y", c("pkf", 0, 384), ap("lb"), "lbp")
+    dma("y", c("tau_o", 0, 384), ap("lc"), "lbt")
+
+    def gather_all(src, width, b0, lo=0, hi=None):
+        a_ = lo
+        while a_ < (hi or 4 * width):
+            q = a_ // width
+            b_ = min((q + 1) * width, (a_ // 512 + 1) * 512)
+            mm(c("ps", 512 * b0 + a_, 512 * b0 + b_), agm(q), src(a_ - q * width, b_ - q * width))
+            a_ = b_
+
+    def new_rates(out):
+        tt(c("wt", 0, 640), ind(c("cw", 0, 1536), c("ab16", 0, 40)), c("kab", 0, 640), A.mult)
+        tt(out, ind(c("cw", 0, 1536), c("ab16", 40, 80)), c("wt", 0, 640), A.mult)
+
+    def cyc_scan(out, src, n, p):
+        scan(c(out, p, n), src(p, n), c("one", p, n), 0.0, A.add, A.mult)
+        if p:
+            scan(c(out, 0, p), src(0, p), c("one", 0, p), c(out, n - 1, n), A.add, A.mult)
+
+    def sm(k, n=24):
+        return ap("sm", slice(None), k, slice(0, n))
+
+    def products(a_, b_):
+        tt(c("prod", 16 * a_, 16 * b_), ind(c("ew", 0, 1536), c("ot16", a_, b_)), c("wg", 16 * a_, 16 * b_), A.mult)
+
+    def maxima(ec, a_, b_):
+        scan(c(ec, 16 * a_, 16 * b_), c("msk", 0, 16 * (b_ - a_)), c("prod", 16 * a_, 16 * b_), 0.0, A.mult, A.max)
+
+    def spread(ec, out):
+        tt(out, ind(c(ec, 0, 4480), c("pe16", 0, 24)), c("taum", 0, 384), A.max)
+
+    for t in range(TR):
+        ec, ecn = "ec%d" % (t % 2), "ec%d" % ((t + 1) % 2)
+        wb, wbo = "wb%d" % (t % 2), "wb%d" % ((t + 1) % 2)
+        nw, nr = c("nw", 24 * t, 24 * t + 24), c("nr", 24 * t, 24 * t + 24)
+        ts(c("ind", 0, 384), c(ec, 4096, 4480), 0.125, A.is_ge)
+        for e in range(16):
+            mm(bank(5, 0, 24), c("we", 128 * e, 128 * e + 128), c("ind", e, 384, 16), e == 0, e == 15)
+        if t == 0:
+            s = others[0]
+            mm(bank(7, 0, 384), agm(0), c("la", 384 * s, 384 * s + 384))
+            cp("v", c("cw", 384 * s, 384 * s + 384), bank(3, 0, 384))
+            cp("v", c("ab16", 0, 80), c("kab", 640, 720))
+        cp("v", nw, bank(5, 0, 24))
+        send((r - 1) % N, nr, nw, "arn%d" % t)
+        if t == 0:
+            for x, d in enumerate(others):
+                send(d, ap("lc", r), c("stau", 96 * x, 96 * x + 96), "arc%d" % r)
+            for x in range(N):
+                live_sel(x)
+            new_rates(c(wb, 0, 640))
+            cp("s", c("ew", 384 * s, 384 * s + 384), bank(7, 0, 384))
+            cp("s", c("co", 0, 384, p=blkp(s)), c("la", 384 * s, 384 * s + 384, p=blkp(1)))
+            gather_all(lambda a_, b_: c(wb, a_, b_), 640, 0, 0, 1024)
+        else:
+            gather_all(lambda a_, b_: c(ec, 4096 + a_, 4096 + b_), 384, 0)
+            for b in range(3):
+                cp("s", c("ew", 512 * b, 512 * b + 512), bank(b))
+            new_rates(c(wbo, 640, 1280))
+            for q in range(N):
+                mm(bank(6, 24 * q, 24), c("ma", 128 * q, 128 * q + 128), nw, True, False)
+                mm(bank(6, 24 * q, 24), c("mb", 128 * q, 128 * q + 128), nr, False, True)
+
+        def wcopy(b):
+            ts(c("wm", 512 * b, 512 * b + 512), bank(b), 1.0, A.min)
+            if b < 4:
+                cp("s", c("wr", 512 * b, 512 * b + 512), bank(b))
+        mm(bank(6, 96, 24), c("ma", 512, 640), nw, True, False)
+        mm(bank(6, 96, 24), c("mb", 512, 640), nr, False, True)
+        if t == 0:
+            gather_all(lambda a_, b_: c(wb, a_, b_), 640, 0, 1024, 1536)
+            wcopy(0)
+        a0 = 0 if t else 96
+        ts(c("ll", a0, 120), bank(6, a0, 120 - a0), 23.5, A.is_ge)
+        lw = c("ll", 96, 120)
+        if t:
+            for h in range(2):
+                tt(c("xab", 640 * h, 640 * h + 640), ind(c("ll", 0, 96), c("abd16", 40 * h, 40 * h + 40)),
+                   c("oh", 640 * h, 640 * h + 640), A.mult)
+                for e in range(16):
+                    mm(bank(7, 0, 40), c("we", 128 * e, 128 * e + 128), c("xab", 640 * h + e, 640 * h + 640, 16),
+                       h == 0 and e == 0, h == 1 and e == 15)
+        cyc_scan("css", lambda a_, b_: c("ll", 96 + a_, 96 + b_), 24, 6 * t)
+        tt(sm(0), lw, c("k1", 24 * t, 24 * t + 24), A.mult)
+        if t:
+            ts(c("act", 0, 40), bank(7, 0, 40), 0.5, A.is_ge)
+            tt(sm(1), sm(0), c("k2", 24 * t, 24 * t + 24), A.add)
+            cyc_scan("csr", lambda a_, b_: c("act", a_, b_), 40, 10 * t)
+            mm(bank(5, 32, 40), c("blk", 0, 128), c("csr", 0, 40), True, False)
+            mm(bank(5, 32, 40), c("trn2", 0, 128), c("act", 0, 40), False, True)
+        else:
+            tt(sm(1), sm(0), c("k2", 24 * t, 24 * t + 24), A.add)
+        mm(bank(6, 128, 24), c("blk", 0, 128), c("css", 0, 24), True, False)
+        mm(bank(6, 128, 24), c("trn", 0, 128), lw, False, True)
+        if t == 0:
+            gather_all(lambda a_, b_: c(wb, a_, b_), 640, 0, 1536)
+            wcopy(1)
+        tt(sm(2), sm(1), c("dump", 0, 24), A.subtract)
+        if t:
+            ts(sm(8, 40), bank(5, 32, 40), -640.0, A.is_le, 640.0, A.mult)
+        tt(sm(3), bank(6, 128, 24), sm(1), A.add)
+        if t:
+            tt(sm(9, 40), sm(8, 40), c("j40", 0, 40), A.add)
+        tt(sm(4), bank(6, 128, 24), sm(2), A.add)
+        if t:
+            cp("v", c("wo16", 0, 40), sm(9, 40))
+        ts(sm(5), sm(3), 0.0, A.max, 255.0, A.min)
+        if t:
+            cp("s", c(wb, 0, 640), ind(c(wbo, 0, 1280), c("wo16", 0, 40)))
+            gather_all(lambda a_, b_: c(wb, a_, b_), 640, 0)
+        tt(sm(6), sm(5), sm(3), A.is_equal)
+        tt(sm(7), sm(6), sm(4), A.mult)
+        tt(sm(0), sm(7), c("dump", 0, 24), A.add)
+        cp("v", c("pos16", 0, 24), sm(0))
+        if t == TR - 1:
+            for k, d in enumerate(others):
+                dma("y", c("so", 256 * k, 256 * k + 160), c(wb, 0, 640, p=blkp(d)), "pko%d" % d)
+            dma("y", ext(T.yw[32 * r:32 * r + 32, :]), c(wb, 0, 640, p=blkp(r)), "st")
+        if t == 0:
+            wcopy(2)
+            wcopy(3)
+            cp("v", c("pk", 0, 384), c("pkf", 0, 384))
+        cp("v", ind(c("lst", 0, 640), c("pos16", 0, 24)), c("pk", 0, 384))
+        if t:
+            wcopy(0)
+            wcopy(1)
+        ts(c("rx16", 0, 256), c("lst", 0, 256), 2.0 ** -12, A.mult)
+        if t:
+            wcopy(2)
+        ts(c("lo_i", 0, 256), c("lst", 0, 256), 4095, A.bitwise_and)
+        if t:
+            wcopy(3)
+            cp("v", c("ot16", 0, 256), c("lo_i", 0, 256))
+        wcopy(4)
+        if t == 0:
+            cp("v", c("ot16", 0, 256), c("lo_i", 0, 256))
+        for a_, b_ in CH1:
+            cp("s", c("wg", 16 * a_, 16 * b_), ind(c("wm", 0, 2560), c("rx16", a_, b_)))
+        cp("s", c("wr", 2048, 2560), bank(4))
+        for x, (a_, b_) in enumerate(XCH):
+            cp("s", c("xg", 16 * a_, 16 * b_), ind(c("wr", 0, 2560), c("rx16", 80 + a_, 80 + b_)), 0.125)
+            if x < 2:
+                mm(bank(3 + x), c("agi", 512, 640), c("xg", 16 * a_ + 1, 16 * b_, 2))
+        ts(sm(1), sm(0), 16.0, A.mult, 15.0, A.add)
+        ts(sm(2), sm(0), 3840.0, A.add)
+        if t:
+            tt(c("taum", 0, 384), ind(c("pm", 0, 640), c("pos16", 0, 24)), c("tau_o", 0, 384), A.mult)
+        products(*CH1[0])
+        tt(sm(3), sm(1), sm(2), A.min)
+        if t == 0:
+            tt(c("taum", 0, 384), ind(c("pm", 0, 640), c("pos16", 0, 24)), c("tau_o", 0, 384), A.mult)
+        cp("v", c("pe16", 0, 24), sm(3))
+        for x in range(1, len(CH1)):
+            maxima(ec, *CH1[x - 1])
+            products(*CH1[x])
+        maxima(ec, *CH1[-1])
+        spread(ec, c("et", 0, 384))
+        gather_all(lambda a_, b_: c("et", a_, b_), 384, 0, 0, 512)
+        mm(bank(7, 0, 384), c("agi", 512, 640), c("xg", 2049, 2816, 2))
+        gather_all(lambda a_, b_: c("et", a_, b_), 384, 0, 512)
+        for x in range(2):
+            a_, b_ = XCH[x]
+            tt(c("y1", 4 * a_, 4 * b_), c("xg", 16 * a_, 16 * b_, 4), c("ps", 512 * (3 + x), 512 * (4 + x), 2), A.add)
+            tt(c("ps", 2560 + 4 * a_, 2560 + 4 * b_), c("xg", 16 * a_ + 2, 16 * b_, 4), c("ps", 512 * (3 + x) + 1, 512 * (4 + x), 2), A.add)
+        cp("s", c("ew", 0, 512), bank(0))
+        a_, b_ = XCH[2]
+        tt(c("y1", 4 * a_, 4 * b_), c("xg", 16 * a_, 16 * b_, 4), c("ps", 3584, 3968, 2), A.add)
+        tt(c("ps", 2560 + 4 * a_, 2560 + 4 * b_), c("xg", 16 * a_ + 2, 16 * b_, 4), c("ps", 3585, 3968, 2), A.add)
+        cp("s", c("ew", 512, 1024), bank(1))
+        cp("s", c("ew", 1024, 1536), bank(2))
+        tt(c("z1", 0, 352), c("y1", 0, 704, 2), c("ps", 2560, 3264, 2), A.add)
+        tt(bank(7, 0, 352), c("y1", 1, 704, 2), c("ps", 2561, 3264, 2), A.add)
+        tt(c("p1", 0, 176), c("z1", 0, 352, 2), c("ps", 3584, 3936, 2), A.add)
+        tt(bank(3, 0, 176), c("z1", 1, 352, 2), c("ps", 3585, 3936, 2), A.add)
+        tt(c("dw", 80, 256), c("p1", 0, 176), bank(3, 0, 176), A.subtract)
+        tt(c("ct", 0, 384), ind(c("dw", 0, 640), c("pos16", 0, 24)), c("co", 0, 384), A.add)
+        ts(c("co", 0, 384), c("ct", 0, 384), 0.125, A.max, 8.0, A.min)
+        nh = 16 * (256 - HY)
+        for a_, b_ in CH3:
+            cp("s", c("eg", 16 * (a_ - HY), 16 * (b_ - HY)), ind(c("ew", 0, 1536), c("ot16", a_, b_)))
+        for o in range(0, nh, 512):
+            mm(c("ps", o, o + 512), c("agi", 512, 640), c("wg", 16 * HY + o, 16 * HY + o + 512))
+        if t < TR - 1:
+            gather_all(lambda a_, b_: c("co", a_, b_), 384, 4)
+            for b in range(3):
+                cp("s", c("cw", 512 * b, 512 * b + 512), bank(4 + b))
+        else:
+            for k, d in enumerate(others):
+                dma("y", c("so", 256 * k + 160, 256 * k + 256), c("co", 0, 384, p=blkp(d)), "pko%d" % d)
+            dma("y", ext(T.yc[32 * r:32 * r + 32, :]), c("co", 0, 384, p=blkp(r)), "st")
+            for k, d in enumerate(others):
+                send(d, c("lo", 256 * r, 256 * r + 256), c("so", 256 * k, 256 * k + 256), "aro%d" % r)
+            for s in others[::-1]:
+                dma("y", ext(T.yw[32 * s:32 * s + 32, :]), c("lo", 256 * s, 256 * s + 160), "st")
+                dma("y", ext(T.yc[32 * s:32 * s + 32, :]), c("lo", 256 * s + 160, 256 * s + 256), "st")
+        if t == 0:
+            cp("v", c("abi", 0, 80), c("kab", 640, 720))
+        for a_, b_ in CH2:
+            products(a_, b_)
+        for a_, b_ in CH2:
+            maxima(ec, a_, b_)
+        for a_, b_ in CH3:
+            tt(c("prod", 16 * a_, 16 * b_), c("eg", 16 * (a_ - HY), 16 * (b_ - HY)), c("ps", 16 * (a_ - HY), 16 * (b_ - HY)), A.mult)
+        if t == 0:
+            ts(c("abt", 0, 80), c("abi", 0, 80), 4, A.arith_shift_right)
+            ts(c("abt", 80, 160), c("abi", 0, 80), 15, A.bitwise_and)
+            cp("v", c("abd16", 0, 80), c("abt", 0, 80))
+            cp("v", c("abm16", 0, 80), c("abt", 80, 160))
+            cp("s", c("oh", 0, 1280), ind(c("idg", 0, 16), c("abm16", 0, 80)))
+        for a_, b_ in CH3:
+            maxima(ec, a_, b_)
+        spread(ec, c(ecn, 4096, 4480))
+
+    ef = "ec%d" % (TR % 2)
+    dma("y", ext(T.ye[32 * r:32 * r + 32, :]), c(ef, 4096, 4480, p=blkp(r)), "st")
+    for k, d in enumerate(others):
+        for u in range(4):
+            cp("vs"[u % 2], c("se", 96 * k, 96 * k + 96, p=blkp(u)), c(ef, 4096 + 96 * u, 4192 + 96 * u, p=blkp(d)))
+        send(d, c("le", 96 * r, 96 * r + 96), c("se", 96 * k, 96 * k + 96), "are%d" % r)
+    for s in others[::-1]:
+        lands(c("le", 96 * s, 96 * s + 96), "are%d" % s, ne)
+        for u in range(4):
+            dma("ys"[u % 2], ext(T.ye[32 * s:32 * s + 32, 96 * u:96 * u + 96]), c("le", 96 * s, 96 * s + 96, p=blkp(u)), "st")
+    for sem in cnt:
+        if cnt[sem]:
+            wait("g", (sem, cnt[sem], {}))

@@ -14,7 +14,7 @@ SCRATCH = {
     "ew": ("sbuf", [128, 1536], F), "cw": ("sbuf", [128, 1536], F), "wr": ("sbuf", [128, 2560], F), "wm": ("sbuf", [128, 2560], F),
     "kab": ("sbuf", [128, 720], F), "tau_o": ("sbuf", [128, 384], F), "pkf": ("sbuf", [128, 384], F), "pk": ("sbuf", [128, 384], I),
     "co": ("sbuf", [128, 384], F), "ct": ("sbuf", [128, 384], F), "wb0": ("sbuf", [128, 1280], F), "wb1": ("sbuf", [128, 1280], F),
-    "wt": ("sbuf", [128, 640], F), "ec0": ("sbuf", [128, 4480], F), "ec1": ("sbuf", [128, 4480], F), "et": ("sbuf", [128, 384], F),
+    "wt": ("sbuf", [128, 640], F), "wbm": ("sbuf", [128, 640], F), "ec0": ("sbuf", [128, 4480], F), "ec1": ("sbuf", [128, 4480], F), "et": ("sbuf", [128, 384], F),
     "dw": ("sbuf", [128, 640], F), "pm": ("sbuf", [128, 640], F), "taum": ("sbuf", [128, 384], F), "lst": ("sbuf", [128, 640], I),
     "lo_i": ("sbuf", [128, 256], I), "rx16": ("sbuf", [128, 256], U), "ot16": ("sbuf", [128, 256], U),
     "wg": ("sbuf", [128, 4096], F), "prod": ("sbuf", [128, 4096], F), "msk": ("sbuf", [128, 1280], B), "eg": ("sbuf", [128, 2048], F),
@@ -31,7 +31,7 @@ SCRATCH = {
     "so": ("sbuf", [128, 3 * 256], F), "lo": ("sbuf", [128, 4 * 256], F), "se": ("sbuf", [128, 3 * 96], F), "le": ("sbuf", [128, 4 * 96], F),
 }
 SEMAPHORES = (["qv", "qs", "qp", "qg", "rl", "lbo", "lco", "lbt", "lbp", "ldb", "ldi", "st"]
-              + ["%s%d" % (n, k) for n in ("lda", "ldab", "ara", "arb", "arc", "arn", "aro", "are", "pko") for k in range(4)])
+              + ["%s%d" % (n, k) for n in ("lda", "ldab", "ara", "arb", "arc", "arn", "aro", "are", "pko", "wr") for k in range(4)])
 SHAPES = {n: v[1] for n, v in SCRATCH.items()}
 A = AluOpType
 ACT = ActivationFunctionType
@@ -299,7 +299,6 @@ def rank_program(g, core, T, topo):
             cp("s", c("ew", o, o + 384), bank(4 + k, 0, 384))
             consts(k)
     dma("y", c("pkf", 0, 384), ap("lb"), "lbp")
-    dma("y", c("tau_o", 0, 384), ap("lc"), "lbt")
 
     def gather_all(src, width, b0, lo=0, hi=None):
         a_ = lo
@@ -352,7 +351,6 @@ def rank_program(g, core, T, topo):
             new_rates(c(wb, 0, 640))
             cp("s", c("ew", 384 * s, 384 * s + 384), bank(7, 0, 384))
             cp("s", c("co", 0, 384, p=blkp(s)), c("la", 384 * s, 384 * s + 384, p=blkp(1)))
-            gather_all(lambda a_, b_: c(wb, a_, b_), 640, 0, 0, 1024)
         else:
             gather_all(lambda a_, b_: c(ec, 4096 + a_, 4096 + b_), 384, 0)
             for b in range(3):
@@ -363,13 +361,30 @@ def rank_program(g, core, T, topo):
                 mm(bank(6, 24 * q, 24), c("mb", 128 * q, 128 * q + 128), nr, False, True)
 
         def wcopy(b):
-            ts(c("wm", 512 * b, 512 * b + 512), bank(b), 1.0, A.min)
             if b < 4:
-                cp("s", c("wr", 512 * b, 512 * b + 512), bank(b))
+                n = min(512, 1920 - 512 * b)
+                cp("s", c("wm", 512 * b, 512 * b + n), bank(b, 0, n))
+
+        def wshift(q, x):
+            cp(q, c("wm", 1920, 2560, p=blkp(x)), c("wbm", 0, 640, p=blkp(3)))
+
+        def wraw():
+            for x in range(N):
+                for y in range(N):
+                    dma("y", c("wr", 640 * x, 640 * x + 640, p=blkp(y)), c(wb, 0, 640, p=blkp(x)), "wr%d" % t)
+        if t == 0:
+            ts(c("wbm", 0, 640), c(wb, 0, 640), 1.0, A.min)
+            gather_all(lambda a_, b_: c("wbm", a_, b_), 640, 0, 0, 1024)
+            wraw()
+            dma("y", c("tau_o", 0, 384), ap("lc"), "lbt")
+            wshift("s", 0)
+            wshift("v", 2)
+            wshift("s", 1)
+            wshift("v", 3)
         mm(bank(6, 96, 24), c("ma", 512, 640), nw, True, False)
         mm(bank(6, 96, 24), c("mb", 512, 640), nr, False, True)
         if t == 0:
-            gather_all(lambda a_, b_: c(wb, a_, b_), 640, 0, 1024, 1536)
+            gather_all(lambda a_, b_: c("wbm", a_, b_), 640, 0, 1024, 1536)
             wcopy(0)
         a0 = 0 if t else 96
         ts(c("ll", a0, 120), bank(6, a0, 120 - a0), 23.5, A.is_ge)
@@ -394,7 +409,7 @@ def rank_program(g, core, T, topo):
         mm(bank(6, 128, 24), c("blk", 0, 128), c("css", 0, 24), True, False)
         mm(bank(6, 128, 24), c("trn", 0, 128), lw, False, True)
         if t == 0:
-            gather_all(lambda a_, b_: c(wb, a_, b_), 640, 0, 1536)
+            gather_all(lambda a_, b_: c("wbm", a_, b_), 640, 0, 1536, 1920)
             wcopy(1)
         tt(sm(2), sm(1), c("dump", 0, 24), A.subtract)
         if t:
@@ -408,7 +423,11 @@ def rank_program(g, core, T, topo):
         ts(sm(5), sm(3), 0.0, A.max, 255.0, A.min)
         if t:
             cp("s", c(wb, 0, 640), ind(c(wbo, 0, 1280), c("wo16", 0, 40)))
-            gather_all(lambda a_, b_: c(wb, a_, b_), 640, 0)
+            ts(c("wbm", 0, 640), ind(c(wbo, 0, 1280), c("wo16", 0, 40)), 1.0, A.min)
+            gather_all(lambda a_, b_: c("wbm", a_, b_), 640, 0, 0, 1920)
+            wraw()
+            wshift("s", 0)
+            wshift("s", 1)
         tt(sm(6), sm(5), sm(3), A.is_equal)
         tt(sm(7), sm(6), sm(4), A.mult)
         tt(sm(0), sm(7), c("dump", 0, 24), A.add)
@@ -423,26 +442,21 @@ def rank_program(g, core, T, topo):
             cp("v", c("pk", 0, 384), c("pkf", 0, 384))
         cp("v", ind(c("lst", 0, 640), c("pos16", 0, 24)), c("pk", 0, 384))
         if t:
-            wcopy(0)
-            wcopy(1)
+            for b in range(4):
+                wcopy(b)
         ts(c("rx16", 0, 256), c("lst", 0, 256), 2.0 ** -12, A.mult)
         if t:
-            wcopy(2)
+            wshift("v", 2)
+            wshift("v", 3)
         ts(c("lo_i", 0, 256), c("lst", 0, 256), 4095, A.bitwise_and)
-        if t:
-            wcopy(3)
-            cp("v", c("ot16", 0, 256), c("lo_i", 0, 256))
-        wcopy(4)
-        if t == 0:
-            cp("v", c("ot16", 0, 256), c("lo_i", 0, 256))
+        ts(sm(1), sm(0), 16.0, A.mult, 15.0, A.add)
+        cp("v", c("ot16", 0, 256), c("lo_i", 0, 256))
         for a_, b_ in CH1:
             cp("s", c("wg", 16 * a_, 16 * b_), ind(c("wm", 0, 2560), c("rx16", a_, b_)))
-        cp("s", c("wr", 2048, 2560), bank(4))
         for x, (a_, b_) in enumerate(XCH):
             cp("s", c("xg", 16 * a_, 16 * b_), ind(c("wr", 0, 2560), c("rx16", 80 + a_, 80 + b_)), 0.125)
             if x < 2:
                 mm(bank(3 + x), c("agi", 512, 640), c("xg", 16 * a_ + 1, 16 * b_, 2))
-        ts(sm(1), sm(0), 16.0, A.mult, 15.0, A.add)
         ts(sm(2), sm(0), 3840.0, A.add)
         if t:
             tt(c("taum", 0, 384), ind(c("pm", 0, 640), c("pos16", 0, 24)), c("tau_o", 0, 384), A.mult)
@@ -456,9 +470,8 @@ def rank_program(g, core, T, topo):
             products(*CH1[x])
         maxima(ec, *CH1[-1])
         spread(ec, c("et", 0, 384))
-        gather_all(lambda a_, b_: c("et", a_, b_), 384, 0, 0, 512)
         mm(bank(7, 0, 384), c("agi", 512, 640), c("xg", 2049, 2816, 2))
-        gather_all(lambda a_, b_: c("et", a_, b_), 384, 0, 512)
+        gather_all(lambda a_, b_: c("et", a_, b_), 384, 0)
         for x in range(2):
             a_, b_ = XCH[x]
             tt(c("y1", 4 * a_, 4 * b_), c("xg", 16 * a_, 16 * b_, 4), c("ps", 512 * (3 + x), 512 * (4 + x), 2), A.add)

@@ -1,41 +1,43 @@
 from concourse.mybir import AluOpType, ActivationFunctionType
 
 N, SO, RO, TR = 4, 384, 640, 4
-CH1 = [(0, 32), (32, 96), (96, 176), (176, 256)]
-CH2 = [(0, 64), (64, 128)]
-CH3 = [(128, 192), (192, 256)]
-HY = 128
+CH1 = [(0, 16), (16, 48), (48, 104), (104, 176), (176, 256)]
+CH2 = [(0, 48)]
+CH3 = [(48, 112), (112, 184), (184, 256)]
+XCH = [(0, 64), (64, 128), (128, 176)]
+HY = CH3[0][0]
+LIFT = 2.0 ** 20
+S0 = 432
 F, B, I, U = "float32", "bfloat16", "int32", "uint16"
 SCRATCH = {
     "ps": ("psum", [128, 4096], F),
-    "sa": ("sbuf", [128, 3 * 384], F), "la": ("sbuf", [128, 4 * 384], F), "sab": ("sbuf", [128, 4 * 80], I),
+    "sa": ("sbuf", [128, 3 * 384], F), "la": ("sbuf", [128, 4 * 384], F), "sab": ("sbuf", [128, 80], I), "sar": ("sbuf", [128, 160], F),
     "sb": ("sbuf", [128, 384], F), "si": ("sbuf", [128, 384], I), "sj": ("sbuf", [128, 384], I), "stau": ("sbuf", [128, 288], F),
-    "sk": ("sbuf", [128, 384], F), "lb": ("dram", [4, 128, 96], F), "lc": ("dram", [4, 128, 96], F),
-    "ew": ("sbuf", [128, 1536], F), "cw": ("sbuf", [128, 1536], F), "wr": ("sbuf", [128, 2560], F), "wm": ("sbuf", [128, 2560], F),
-    "kab": ("sbuf", [128, 720], F), "tau_o": ("sbuf", [128, 384], F), "pkf": ("sbuf", [128, 384], F), "pk": ("sbuf", [128, 384], I),
-    "co": ("sbuf", [128, 384], F), "ct": ("sbuf", [128, 384], F), "wb0": ("sbuf", [128, 1280], F), "wb1": ("sbuf", [128, 1280], F),
-    "wt": ("sbuf", [128, 640], F), "wbm": ("sbuf", [128, 640], F), "ec0": ("sbuf", [128, 4480], F), "ec1": ("sbuf", [128, 4480], F), "et": ("sbuf", [128, 384], F),
-    "dw": ("sbuf", [128, 640], F), "pm": ("sbuf", [128, 640], F), "taum": ("sbuf", [128, 384], F), "lst": ("sbuf", [128, 640], I),
+    "sk": ("sbuf", [128, 384], F), "sp": ("sbuf", [128, 288], F), "lb": ("sbuf", [128, 384], F), "lc": ("dram", [4, 128, 96], F),
+    "ea": ("sbuf", [128, 5640], F), "eb": ("sbuf", [128, 5640], F), "cw": ("sbuf", [128, 1536], F), "wm": ("sbuf", [128, 2560], F),
+    "w0": ("sbuf", [128, 3200], F), "w1": ("sbuf", [128, 3200], F),
+    "kab": ("sbuf", [128, 720], F), "tau_o": ("sbuf", [128, 384], F), "pk": ("sbuf", [128, 384], F),
+    "ct": ("sbuf", [128, 384], F), "wt": ("sbuf", [128, 640], F), "et": ("sbuf", [128, 384], F),
+    "dw": ("sbuf", [128, 896], F), "pm": ("sbuf", [128, 896], F), "taum": ("sbuf", [128, 384], F), "lst": ("sbuf", [128, 896], I),
     "lo_i": ("sbuf", [128, 256], I), "rx16": ("sbuf", [128, 256], U), "ot16": ("sbuf", [128, 256], U),
-    "wg": ("sbuf", [128, 4096], F), "prod": ("sbuf", [128, 4096], F), "msk": ("sbuf", [128, 1280], B), "eg": ("sbuf", [128, 2048], F),
-    "pe16": ("sbuf", [128, 24], U), "mz": ("sbuf", [128, 640], B),
+    "wg": ("sbuf", [128, 4096], F), "prod": ("sbuf", [128, 4096], F), "msk": ("sbuf", [128, 1792], B), "eg": ("sbuf", [128, 16 * (256 - HY)], F),
+    "pe16": ("sbuf", [128, 24], U), "mz": ("sbuf", [128, 128], B),
     "xg": ("sbuf", [128, 2816], F), "y1": ("sbuf", [128, 704], F), "z1": ("sbuf", [128, 352], F), "p1": ("sbuf", [128, 176], F),
     "ind": ("sbuf", [128, 384], B), "nw": ("sbuf", [128, 96], B), "nr": ("sbuf", [128, 96], B), "ll": ("sbuf", [128, 128], B),
     "xab": ("sbuf", [128, 1280], B), "oh": ("sbuf", [128, 1280], B), "act": ("sbuf", [128, 40], B), "csr": ("sbuf", [128, 40], B),
     "css": ("sbuf", [128, 24], B), "sm": ("sbuf", [128, 10, 40], F), "wo16": ("sbuf", [128, 40], U), "pos16": ("sbuf", [128, 24], U),
     "abi": ("sbuf", [128, 80], I), "abt": ("sbuf", [128, 160], I), "ab16": ("sbuf", [128, 80], U), "abd16": ("sbuf", [128, 80], U), "abm16": ("sbuf", [128, 80], U),
-    "iv": ("sbuf", [128, 640], F), "agi": ("sbuf", [128, 640], F), "ma": ("sbuf", [128, 640], B), "mb": ("sbuf", [128, 640], B), "mt": ("sbuf", [128, 640], B),
-    "we": ("sbuf", [128, 2048], B), "blk": ("sbuf", [128, 128], B), "trn": ("sbuf", [128, 128], B), "trn2": ("sbuf", [128, 128], B),
+    "iv": ("sbuf", [128, 256], F), "agi": ("sbuf", [128, 256], F), "ma": ("sbuf", [128, 224], B), "mb": ("sbuf", [128, 224], B), "mt": ("sbuf", [128, 128], B),
+    "we": ("sbuf", [128, 2048], B), "blk": ("sbuf", [128, 128], B), "trn": ("sbuf", [128, 128], B), "trn2": ("sbuf", [128, 128], B), "trn0": ("sbuf", [128, 128], B),
     "ci": ("sbuf", [128, 4], I), "cf": ("sbuf", [128, 8], F), "io2": ("sbuf", [128, 200], F), "g8": ("sbuf", [128, 8], B), "idg": ("sbuf", [128, 16], F),
-    "j40": ("sbuf", [128, 40], F), "dump": ("sbuf", [128, 24], F), "k1": ("sbuf", [128, 96], F), "k2": ("sbuf", [128, 96], F), "one": ("sbuf", [128, 40], B),
+    "j40": ("sbuf", [128, 40], F), "dump": ("sbuf", [128, 24], F), "k2": ("sbuf", [128, 96], F), "one": ("sbuf", [128, 40], B),
     "so": ("sbuf", [128, 3 * 256], F), "lo": ("sbuf", [128, 4 * 256], F), "se": ("sbuf", [128, 3 * 96], F), "le": ("sbuf", [128, 4 * 96], F),
 }
-SEMAPHORES = (["qv", "qs", "qp", "qg", "rl", "lbo", "lco", "lbt", "lbp", "ldb", "ldi", "st"]
-              + ["%s%d" % (n, k) for n in ("lda", "ldab", "ara", "arb", "arc", "arn", "aro", "are", "pko", "wr") for k in range(4)])
+SEMAPHORES = (["qv", "qs", "qp", "qg", "rl", "lco", "lbt", "ldb", "ldi", "ldab", "st"]
+              + ["%s%d" % (n, k) for n in ("lda", "ara", "arb", "arc", "arn", "aro", "arw", "are", "pko", "pkc", "wr", "cg") for k in range(4)])
 SHAPES = {n: v[1] for n, v in SCRATCH.items()}
 A = AluOpType
 ACT = ActivationFunctionType
-XCH = [(0, 64), (64, 128), (128, 176)]
 
 
 def rank_program(g, core, T, topo):
@@ -86,7 +88,7 @@ def rank_program(g, core, T, topo):
             if known[q].get(s_, 0) < v_:
                 known[q][s_] = v_
 
-    def order(q, reads, writes, tok_of, comp=False):
+    def order(q, reads, writes, tok_of):
         acc = [(x, False) for a_ in reads for x in a_["regs"] + a_["offs"]]
         acc += [(x, True) for a_ in writes for x in a_["regs"]] + [(x, False) for a_ in writes for x in a_["offs"]]
         need = []
@@ -119,7 +121,7 @@ def rank_program(g, core, T, topo):
             fn().then_inc(T.sem[sem], 1)
             cnt[sem] += 1
             return (sem, cnt[sem], dict(known[q]))
-        return order(q, reads, writes, emit, True)
+        return order(q, reads, writes, emit)
 
     def dma(q, out, in_, sem):
         def emit():
@@ -161,6 +163,8 @@ def rank_program(g, core, T, topo):
 
     def cp(q, out, a_, scale=None):
         if q == "v":
+            if scale is not None:
+                return ts(out, a_, scale, A.mult)
             return op("v", lambda: g.vector.tensor_copy(out["ap"], a_["ap"]), [a_], [out])
         if scale is None:
             return op("s", lambda: g.scalar.activation(out["ap"], a_["ap"], ACT.Copy), [a_], [out])
@@ -181,19 +185,29 @@ def rank_program(g, core, T, topo):
             return op("g", lambda: g.iota(out["ap"], pat, base, cm, allow_small_or_imprecise_dtypes=True), [], [out])
         return op("g", lambda: g.iota(out["ap"], pat, base, cm), [], [out])
 
+    def asel(out, a_, pat, cmp_, fill, base):
+        return op("g", lambda: g.affine_select(out["ap"], a_["ap"], pat, cmp_, fill, base, 1), [a_], [out])
+
     def blkp(q):
         return (32 * q, 32 * q + 32)
 
     def bank(b, a_=0, n=512):
         return c("ps", 512 * b + a_, 512 * b + a_ + n)
 
+    def sm(k, n=24):
+        return ap("sm", slice(None), k, slice(0, n))
+
+    def turn(m):
+        return c("agi", 32 * m, 32 * m + 128)
+
     ne = len(engines((r + 1) % N))
     others = [(r + k) % N for k in (1, 2, 3)]
     for s in others:
         lands(c("la", 384 * s, 384 * s + 384), "ara%d" % s, ne)
-        lands(ap("lb", s), "arb%d" % s, ne)
+        lands(c("lb", 96 * s, 96 * s + 96), "arb%d" % s, ne)
         lands(ap("lc", s), "arc%d" % s, ne)
-        lands(c("lo", 256 * s, 256 * s + 256), "aro%d" % s, ne)
+        lands(c("lo", 256 * s, 256 * s + 160), "arw%d" % s, ne)
+        lands(c("lo", 256 * s + 160, 256 * s + 256), "aro%d" % s, ne)
     for t in range(TR):
         lands(c("nr", 24 * t, 24 * t + 24), "arn%d" % t, ne)
 
@@ -201,336 +215,293 @@ def rank_program(g, core, T, topo):
         k = others.index(d) if d != r else None
         return c("la", 384 * r + a_, 384 * r + b_, p=p) if d == r else c("sa", 384 * k + a_, 384 * k + b_, p=p)
 
+    dma("y", c("sab", 0, 40), ext(T.ra[:, :]), "ldab")
+    dma("s", c("sab", 40, 80), ext(T.rb[:, :]), "ldab")
     for d in others + [r]:
         rows = slice(32 * d, 32 * d + 32)
-        dma("y", c("sab", 80 * d, 80 * d + 40, p=blkp(3)), ext(T.ra[rows, :]), "ldab%d" % d)
-        dma("s", c("sab", 80 * d + 40, 80 * d + 80, p=blkp(3)), ext(T.rb[rows, :]), "ldab%d" % d)
         dma("y", pack(d, 0, 384, blkp(0)), ext(T.ein[rows, :]), "lda%d" % d)
         dma("s", pack(d, 0, 384, blkp(1)), ext(T.cin[rows, :]), "lda%d" % d)
         dma("y", pack(d, 0, 384, blkp(2)), ext(T.kin[rows, 0:384]), "lda%d" % d)
         dma("s", pack(d, 0, 256, blkp(3)), ext(T.kin[rows, 384:640]), "lda%d" % d)
-    for d in others + [r]:
-        rows = slice(32 * d, 32 * d + 32)
-        dma("y", c("si", 96 * d, 96 * d + 96), ext(T.rx[rows, :]), "ldi")
-        dma("s", c("sj", 96 * d, 96 * d + 96), ext(T.ot[rows, :]), "ldi")
+    dma("y", c("si", 0, 384), ext(T.rx[:, :]), "ldi")
+    dma("s", c("sj", 0, 384), ext(T.ot[:, :]), "ldi")
     for k, d in enumerate(others):
         dma("y", c("stau", 96 * k, 96 * k + 96), ext(T.tau[32 * d:32 * d + 32, :]), "ldb")
     dma("y", ap("lc", r), ext(T.tau[32 * r:32 * r + 32, :]), "lco")
 
     iota(c("ci", 0, 1), [[0, 1]], 0, 1, False)
     iota(c("io2", 0, 128), [[16, 8], [0, 16]], 0, 0)
-    iota(c("iv", 0, 512), [[-32, 4], [0, 4], [-1, 32]], 0, 1)
-    iota(c("iv", 512, 640), [[-1, 128]], 0, 1)
+    iota(c("iv", 0, 256), [[0, 2], [-1, 128]], 0, 1)
     for d in others + [r]:
         ms(pack(d, 336, 384, blkp(3)), 0.0)
     ms(c("we", 0, 2048), 0.0)
     ts(c("ci", 1, 2), c("ci", 0, 1), 112, A.bitwise_and)
     ts(c("ci", 2, 3), c("ci", 0, 1), 15, A.bitwise_and)
-    ts(c("ci", 3, 4), c("ci", 0, 1), 16, A.bitwise_and)
-    cp("v", c("cf", 0, 4), c("ci", 0, 4))
+    cp("v", c("cf", 0, 3), c("ci", 0, 3))
     kg16, pmod = c("cf", 1, 2), c("cf", 2, 3)
     ts(c("g8", 0, 8), c("io2", 0, 128, 16), kg16, A.is_equal)
     for e in range(16):
         cp("s", c("we", 128 * e + e, 128 * e + 128, 16), c("g8", 0, 8))
+    ts(c("sar", 0, 80), c("sab", 0, 80), float(SO * r), A.is_lt, float(N * SO), A.mult)
+    tt(c("sar", 80, 160), c("sar", 0, 80), c("sab", 0, 80), A.add)
     for d in others + [r]:
-        cp("v", pack(d, 256, 336, blkp(3)), c("sab", 80 * d, 80 * d + 80, p=blkp(3)))
+        ts(pack(d, 256, 336, blkp(3)), c("sar", 80, 160, p=blkp(d)), -float(SO * r), A.add)
         if d != r:
             send(d, c("la", 384 * r, 384 * r + 384), pack(d, 0, 384), "ara%d" % r)
-        if d == others[0]:
-            iota(c("io2", 128, 144), [[1, 16]], 0, 0)
-            iota(c("io2", 144, 184), [[16, 40]], 0, 1)
-            ts(c("agi", 0, 640), c("iv", 0, 640), 0.0, A.is_equal)
-        if d == others[1]:
-            ts(c("blk", 0, 128), c("io2", 0, 128), kg16, A.is_equal)
-            ts(c("trn2", 0, 128), c("io2", 0, 128), kg16, A.is_equal, -1.0, A.mult)
-            ms(c("mz", 0, 640), 0.0)
-            ms(c("lst", 0, 640), 0)
-            cp("s", c("mt", 0, 640), c("agi", 0, 640), 2.0)
+    ts(c("agi", 0, 256), c("iv", 0, 256), 0.0, A.is_equal)
+    ts(c("blk", 0, 128), c("io2", 0, 128), kg16, A.is_equal, 2.0 ** -9, A.mult)
+    ts(c("trn0", 0, 128), c("io2", 0, 128), kg16, A.is_equal, -2.0 ** -9, A.mult)
+    ms(c("mz", 0, 128), 0.0)
+    cp("s", c("mt", 0, 128), c("agi", 0, 128), 2.0)
+    ms(c("lst", 0, 896), 0)
+    ms(c("dw", 0, 896), 0.0)
+    ts(bank(0, 0, 384), c("si", 0, 384), 4096.0, A.mult, -4096.0 * RO * r - SO * r, A.add)
+    ts(bank(1, 0, 384), c("si", 0, 384), float(RO * r), A.is_lt, 4096.0 * N * RO, A.mult)
+    ts(bank(2, 0, 384), c("sj", 0, 384), float(SO * r), A.is_lt, float(N * SO), A.mult)
+    tt(c("sk", 0, 384), c("sj", 0, 384), bank(0, 0, 384), A.add)
+    tt(c("sb", 0, 384), c("sk", 0, 384), bank(1, 0, 384), A.add)
+    tt(c("sk", 0, 384), c("sb", 0, 384), bank(2, 0, 384), A.add)
+    for k, d in enumerate(others):
+        for u in range(4):
+            cp("vs"[u % 2], c("sp", 96 * k, 96 * k + 96, p=blkp(u)), c("sk", 96 * u, 96 * u + 96, p=blkp(d)))
+        send(d, c("lb", 96 * r, 96 * r + 96), c("sp", 96 * k, 96 * k + 96), "arb%d" % r)
+    cp("s", c("pk", 0, 384, p=blkp(r)), c("sk", 0, 384, p=blkp(r)))
 
-    def asel(out, a_, pat, cmp_, fill, base):
-        return op("g", lambda: g.affine_select(out["ap"], a_["ap"], pat, cmp_, fill, base, 1), [a_], [out])
+    iota(c("io2", 128, 144), [[1, 16]], 0, 0)
+    iota(c("io2", 144, 184), [[16, 40]], 0, 1)
+    asel(c("ma", 0, 128), c("mt", 0, 128), [[-32, 4], [1000, 2], [-1, 16]], A.not_equal, 1.0, -16)
+    asel(c("mb", 0, 128), c("mz", 0, 128), [[-32, 4], [-1000, 2], [-1, 16]], A.not_equal, 1.0, 1000)
+    asel(c("trn", 0, 128), c("trn0", 0, 128), [[-1, 128]], A.is_ge, 0.0, 0)
+    asel(c("trn2", 0, 128), c("trn", 0, 128), [[-1, 128]], A.not_equal, -2.0, 0)
+    cp("s", c("pm", 0, 896), c("dw", 0, 896))
+    ms(c("pm", S0, S0 + 256), LIFT)
+    ms(c("msk", 0, 1792), 1.0)
+    ms(c("msk", 0, 1792, 16), 0.0)
 
-    def live_sel(x):
-        o, st, b0 = 128 * x, (-32 if x == 4 else 0), (0 if x == 4 else -32 * x)
-        asel(c("ma", o, o + 128), c("mt", o, o + 128), [[st, 4], [1000, 2], [-1, 16]], A.not_equal, 1.0, b0 - 16)
-        asel(c("mb", o, o + 128), c("mz", o, o + 128), [[st, 4], [-1000, 2], [-1, 16]], A.not_equal, 1.0, b0 + 1000)
-
-    live_sel(4)
-    asel(c("trn", 0, 128), c("trn2", 0, 128), [[-1, 128]], A.is_gt, 0.0, 0)
-    asel(c("trn2", 0, 128), c("trn", 0, 128), [[-1, 128]], A.not_equal, -1024.0, 0)
-
-    def consts(k):
-        if k == 0:
-            ts(c("sk", 0, 384), c("si", 0, 384), 4096.0, A.mult)
-            tt(c("sb", 0, 384), c("sk", 0, 384), c("sj", 0, 384), A.add)
-            for d in others:
-                send(d, ap("lb", r), c("sb", 96 * d, 96 * d + 96), "arb%d" % r)
-            dma("y", ap("lb", r), c("sb", 96 * r, 96 * r + 96), "lbo")
-            cp("s", c("dw", 0, 640), c("iv", 0, 640), 0.0)
-        if k == 1:
-            ts(c("j40", 0, 40), c("io2", 144, 184), kg16, A.subtract)
-            ts(c("idg", 0, 16), c("io2", 128, 144), pmod, A.is_equal)
-            ms(c("one", 0, 40), 1.0)
-            ts(c("dump", 0, 24), c("j40", 0, 24), 256.0, A.add)
-            for t in range(4):
-                ts(c("k1", 30 * t, 24 * t + 24), c("j40", 6 * t, 24), -96.0 * t, A.add)
-                if t:
-                    ts(c("k1", 24 * t, 30 * t), c("j40", 0, 6 * t), 384.0 - 96.0 * t, A.add)
-            ms(c("pm", 0, 256), 1.0)
-            ts(c("k2", 0, 96), c("k1", 0, 96), -1.0, A.mult, 79.0, A.add)
-            cp("s", c("pm", 256, 640), c("iv", 256, 640), 0.0)
-        if k == 2:
-            ms(c("msk", 0, 1280), 1.0)
-            ms(c("msk", 0, 1280, 16), 0.0)
-
-    def agm(q):
-        return c("agi", 128 * q, 128 * q + 128)
+    def late_constants():
+        ts(c("j40", 0, 40), c("io2", 144, 184), kg16, A.subtract)
+        ts(c("idg", 0, 16), c("io2", 128, 144), pmod, A.is_equal)
+        ms(c("one", 0, 40), 1.0)
+        ts(c("dump", 0, 24), c("j40", 0, 24), 4096.0, A.add)
+        for t in range(TR):
+            ts(c("k2", 30 * t, 24 * t + 24), c("j40", 6 * t, 24), -1.0, A.mult, 511.0 + 96.0 * t, A.add)
+            if t:
+                ts(c("k2", 24 * t, 30 * t), c("j40", 0, 6 * t), -1.0, A.mult, 127.0 + 96.0 * t, A.add)
+        cp("s", c("ma", 128, 224), c("ma", 0, 96))
+        cp("s", c("mb", 128, 224), c("mb", 0, 96))
 
     for k, s in enumerate([r] + others[::-1]):
         o = 384 * s
-        mm(bank(k, 0, 384), agm(1), c("la", o, o + 384))
-        cp("v", c("ec0", 4096, 4480, p=blkp(s)), c("la", o, o + 384, p=blkp(0)))
+        if k == 2:
+            late_constants()
+        cp("v", c("ea", 4096, 4480, p=blkp(s)), c("la", o, o + 384, p=blkp(0)), LIFT)
+        if k == 3:
+            ts(c("ind", 0, 384), c("ea", 4096, 4480), 0.125 * LIFT, A.is_ge)
         cp("s", c("kab", 384, 720, p=blkp(s)), c("la", o, o + 336, p=blkp(3)))
+        for y in range(N):
+            m = (s - y) % N
+            cp("vs"[y % 2], c("cw", 384 * m, 384 * m + 384, p=blkp(y)), c("la", o, o + 384, p=blkp(1)))
         cp("s", c("kab", 0, 384, p=blkp(s)), c("la", o, o + 384, p=blkp(2)))
-        if k < 3:
-            mm(bank(4 + k, 0, 384), agm(0), c("la", o, o + 384))
-            cp("v", c("cw", o, o + 384), bank(k, 0, 384))
-            cp("s", c("co", 0, 384, p=blkp(s)), c("la", o, o + 384, p=blkp(1)))
-            cp("s", c("ew", o, o + 384), bank(4 + k, 0, 384))
-            consts(k)
-    dma("y", c("pkf", 0, 384), ap("lb"), "lbp")
 
-    def gather_all(src, width, b0, lo=0, hi=None):
-        a_ = lo
-        while a_ < (hi or 4 * width):
-            q = a_ // width
-            b_ = min((q + 1) * width, (a_ // 512 + 1) * 512)
-            mm(c("ps", 512 * b0 + a_, 512 * b0 + b_), agm(q), src(a_ - q * width, b_ - q * width))
-            a_ = b_
+    def turn_pe(buf, base, width, at, ms_):
+        for k, m in enumerate(ms_):
+            a_ = 0
+            while a_ < width:
+                o = at[k] + a_
+                b_ = min(width, a_ + 512 - o % 512)
+                mm(c("ps", o, o + b_ - a_), turn(m), c(buf, base + a_, base + b_))
+                a_ = b_
+
+    def turn_out(q, buf, base, width, at, m):
+        cp(q, c(buf, base + m * width, base + (m + 1) * width), c("ps", at, at + width))
+
+    def turn_half(q, buf, base, width, h):
+        cp(q, c(buf, base + 2 * width, base + 3 * width, p=(64 * h, 64 * h + 64)), c(buf, base, base + width, p=(64 - 64 * h, 128 - 64 * h)))
+
+    def turn_dma(buf, base, width, sem):
+        for m in (1, 2, 3):
+            o = base + m * width
+            dma("y", c(buf, o, o + width, p=(0, 128 - 32 * m)), c(buf, base, base + width, p=(32 * m, 128)), sem)
+            dma("y", c(buf, o, o + width, p=(128 - 32 * m, 128)), c(buf, base, base + width, p=(0, 32 * m)), sem)
+
+    def e_window(buf):
+        turn_pe(buf, 4096, 384, (2560, 3072, 3584), (1, 2, 3))
+
+    def e_out(buf, ms_):
+        for m in ms_:
+            turn_out("s", buf, 4096, 384, 2048 + 512 * m, m)
 
     def new_rates(out):
         tt(c("wt", 0, 640), ind(c("cw", 0, 1536), c("ab16", 0, 40)), c("kab", 0, 640), A.mult)
         tt(out, ind(c("cw", 0, 1536), c("ab16", 40, 80)), c("wt", 0, 640), A.mult)
 
-    def cyc_scan(out, src, n, p):
-        scan(c(out, p, n), src(p, n), c("one", p, n), 0.0, A.add, A.mult)
-        if p:
-            scan(c(out, 0, p), src(0, p), c("one", 0, p), c(out, n - 1, n), A.add, A.mult)
+    def products(e_, a_, b_):
+        tt(c("prod", 16 * a_, 16 * b_), ind(c(e_, 4096, 5632), c("ot16", a_, b_)), c("wg", 16 * a_, 16 * b_), A.mult)
 
-    def sm(k, n=24):
-        return ap("sm", slice(None), k, slice(0, n))
+    def maxima(e_, a_, b_):
+        scan(c(e_, 16 * a_, 16 * b_), c("msk", 0, 16 * (b_ - a_)), c("prod", 16 * a_, 16 * b_), 0.0, A.mult, A.max)
 
-    def products(a_, b_):
-        tt(c("prod", 16 * a_, 16 * b_), ind(c("ew", 0, 1536), c("ot16", a_, b_)), c("wg", 16 * a_, 16 * b_), A.mult)
-
-    def maxima(ec, a_, b_):
-        scan(c(ec, 16 * a_, 16 * b_), c("msk", 0, 16 * (b_ - a_)), c("prod", 16 * a_, 16 * b_), 0.0, A.mult, A.max)
-
-    def spread(ec, out):
-        tt(out, ind(c(ec, 0, 4480), c("pe16", 0, 24)), c("taum", 0, 384), A.max)
+    def spread(e_, to):
+        tt(c(to, 4096, 4480), ind(c(e_, 0, 4480), c("pe16", 0, 24)), c("taum", 0, 384), A.max)
 
     for t in range(TR):
-        ec, ecn = "ec%d" % (t % 2), "ec%d" % ((t + 1) % 2)
-        wb, wbo = "wb%d" % (t % 2), "wb%d" % ((t + 1) % 2)
+        wn, wo = "w%d" % (t % 2), "w%d" % ((t + 1) % 2)
         nw, nr = c("nw", 24 * t, 24 * t + 24), c("nr", 24 * t, 24 * t + 24)
-        ts(c("ind", 0, 384), c(ec, 4096, 4480), 0.125, A.is_ge)
+        if t:
+            ts(c("ind", 0, 384), c("ea", 4096, 4480), 0.125 * LIFT, A.is_ge)
         for e in range(16):
-            mm(bank(5, 0, 24), c("we", 128 * e, 128 * e + 128), c("ind", e, 384, 16), e == 0, e == 15)
+            mm(bank(4, 0, 24), c("we", 128 * e, 128 * e + 128), c("ind", e, 384, 16), e == 0, e == 15)
         if t == 0:
-            s = others[0]
-            mm(bank(7, 0, 384), agm(0), c("la", 384 * s, 384 * s + 384))
-            cp("v", c("cw", 384 * s, 384 * s + 384), bank(3, 0, 384))
             cp("v", c("ab16", 0, 80), c("kab", 640, 720))
-        cp("v", nw, bank(5, 0, 24))
+        cp("v", nw, bank(4, 0, 24))
         send((r - 1) % N, nr, nw, "arn%d" % t)
+        e_window("ea")
         if t == 0:
             for x, d in enumerate(others):
                 send(d, ap("lc", r), c("stau", 96 * x, 96 * x + 96), "arc%d" % r)
-            for x in range(N):
-                live_sel(x)
-            new_rates(c(wb, 0, 640))
-            cp("s", c("ew", 384 * s, 384 * s + 384), bank(7, 0, 384))
-            cp("s", c("co", 0, 384, p=blkp(s)), c("la", 384 * s, 384 * s + 384, p=blkp(1)))
+            new_rates(c(wn, 640, 1280))
+            for s in others[::-1]:
+                for u in range(4):
+                    cp("s", c("pk", 96 * u, 96 * u + 96, p=blkp(s)), c("lb", 96 * s, 96 * s + 96, p=blkp(u)))
         else:
-            gather_all(lambda a_, b_: c(ec, 4096 + a_, 4096 + b_), 384, 0)
-            for b in range(3):
-                cp("s", c("ew", 512 * b, 512 * b + 512), bank(b))
-            new_rates(c(wbo, 640, 1280))
-            for q in range(N):
-                mm(bank(6, 24 * q, 24), c("ma", 128 * q, 128 * q + 128), nw, True, False)
-                mm(bank(6, 24 * q, 24), c("mb", 128 * q, 128 * q + 128), nr, False, True)
+            new_rates(c(wo, 0, 640))
+        e_out("ea", (1, 2, 3))
 
-        def wcopy(b):
-            if b < 4:
-                n = min(512, 1920 - 512 * b)
-                cp("s", c("wm", 512 * b, 512 * b + n), bank(b, 0, n))
-
-        def wshift(q, x):
-            cp(q, c("wm", 1920, 2560, p=blkp(x)), c("wbm", 0, 640, p=blkp(3)))
-
-        def wraw():
-            for x in range(N):
-                for y in range(N):
-                    dma("y", c("wr", 640 * x, 640 * x + 640, p=blkp(y)), c(wb, 0, 640, p=blkp(x)), "wr%d" % t)
+        def w_window():
+            parts = [(m, h) for m in (1, 3) for h in (0, 320)]
+            for b, (m, h) in enumerate(parts):
+                mm(bank(b, 128, 320), turn(m), c("wm", h, h + 320))
+            turn_half("s", "wm", 0, 640, 0)
+            turn_half("s", "wm", 0, 640, 1)
+            for b, (m, h) in enumerate(parts):
+                cp("s", c("wm", 640 * m + h, 640 * m + h + 320), bank(b, 128, 320))
         if t == 0:
-            ts(c("wbm", 0, 640), c(wb, 0, 640), 1.0, A.min)
-            gather_all(lambda a_, b_: c("wbm", a_, b_), 640, 0, 0, 1024)
-            wraw()
+            ts(c("wm", 0, 640), c(wn, 640, 1280), 1.0, A.min)
+            w_window()
+            turn_dma(wn, 640, 640, "wr%d" % t)
             dma("y", c("tau_o", 0, 384), ap("lc"), "lbt")
-            wshift("s", 0)
-            wshift("v", 2)
-            wshift("s", 1)
-            wshift("v", 3)
-        mm(bank(6, 96, 24), c("ma", 512, 640), nw, True, False)
-        mm(bank(6, 96, 24), c("mb", 512, 640), nr, False, True)
-        if t == 0:
-            gather_all(lambda a_, b_: c("wbm", a_, b_), 640, 0, 1024, 1536)
-            wcopy(0)
-        a0 = 0 if t else 96
-        ts(c("ll", a0, 120), bank(6, a0, 120 - a0), 23.5, A.is_ge)
-        lw = c("ll", 96, 120)
+        for m in ([0, 1, 2, 3] if t else [0]) + [-1]:
+            x = 32 * max(m, 0)
+            mm(bank(4, 64 + 24 * m, 24), c("ma", x, x + 128), nw, True, False)
+            mm(bank(4, 64 + 24 * m, 24), c("mb", x, x + 128), nr, False, True)
+        n = 120 if t else 48
+        ts(c("ll", 8, 8 + n), bank(4, 40, n), 23.5, A.is_ge, 512.0, A.mult)
+        lw = c("ll", 32, 56)
+        p = 6 * t
         if t:
             for h in range(2):
-                tt(c("xab", 640 * h, 640 * h + 640), ind(c("ll", 0, 96), c("abd16", 40 * h, 40 * h + 40)),
+                tt(c("xab", 640 * h, 640 * h + 640), ind(c("ll", 32, 128), c("abd16", 40 * h, 40 * h + 40)),
                    c("oh", 640 * h, 640 * h + 640), A.mult)
                 for e in range(16):
-                    mm(bank(7, 0, 40), c("we", 128 * e, 128 * e + 128), c("xab", 640 * h + e, 640 * h + 640, 16),
+                    mm(bank(3, 0, 40), c("we", 128 * e, 128 * e + 128), c("xab", 640 * h + e, 640 * h + 640, 16),
                        h == 0 and e == 0, h == 1 and e == 15)
-        cyc_scan("css", lambda a_, b_: c("ll", 96 + a_, 96 + b_), 24, 6 * t)
-        tt(sm(0), lw, c("k1", 24 * t, 24 * t + 24), A.mult)
+        scan(c("css", 0, 24), c("ll", 8 + p, 32 + p), c("one", 0, 24), 0.0, A.add, A.mult)
+        tt(sm(0), lw, c("k2", 24 * t, 24 * t + 24), A.max)
+        mm(bank(4, 256, 24), c("trn", 0, 128), lw, True, False)
+        mm(bank(4, 256 + p, 24 - p), c("blk", 0, 128), c("css", 0, 24 - p), False, False)
+        if p:
+            mm(bank(4, 256, p), c("blk", 0, 128), c("css", 24 - p, 24), False, False)
+        mm(bank(4, 256, 24), turn(0), sm(0), False, True)
         if t:
-            ts(c("act", 0, 40), bank(7, 0, 40), 0.5, A.is_ge)
-            tt(sm(1), sm(0), c("k2", 24 * t, 24 * t + 24), A.add)
-            cyc_scan("csr", lambda a_, b_: c("act", a_, b_), 40, 10 * t)
-            mm(bank(5, 32, 40), c("blk", 0, 128), c("csr", 0, 40), True, False)
-            mm(bank(5, 32, 40), c("trn2", 0, 128), c("act", 0, 40), False, True)
-        else:
-            tt(sm(1), sm(0), c("k2", 24 * t, 24 * t + 24), A.add)
-        mm(bank(6, 128, 24), c("blk", 0, 128), c("css", 0, 24), True, False)
-        mm(bank(6, 128, 24), c("trn", 0, 128), lw, False, True)
-        if t == 0:
-            gather_all(lambda a_, b_: c("wbm", a_, b_), 640, 0, 1536, 1920)
-            wcopy(1)
-        tt(sm(2), sm(1), c("dump", 0, 24), A.subtract)
-        if t:
-            ts(sm(8, 40), bank(5, 32, 40), -640.0, A.is_le, 640.0, A.mult)
-        tt(sm(3), bank(6, 128, 24), sm(1), A.add)
-        if t:
+            q_ = 10 * t
+            ts(c("act", 0, 40), bank(3, 0, 40), 0.5, A.is_ge, 512.0, A.mult)
+            scan(c("csr", q_, 40), c("act", q_, 40), c("one", q_, 40), 0.0, A.add, A.mult)
+            cp("v", c("pos16", 0, 24), bank(4, 256, 24))
+            scan(c("csr", 0, q_), c("act", 0, q_), c("one", 0, q_), c("csr", 39, 40), A.add, A.mult)
+            mm(bank(3, 64, 40), c("blk", 0, 128), c("csr", 0, 40), True, False)
+            mm(bank(3, 64, 40), c("trn2", 0, 128), c("act", 0, 40), False, True)
+            ts(sm(1), bank(4, 256, 24), 16.0, A.mult, 15.0 - 16 * S0, A.add)
+            ts(sm(8, 40), bank(3, 64, 40), -640.0, A.is_gt, 640.0, A.mult)
+            ts(sm(2), bank(4, 256, 24), -S0 - 127.5, A.add)
             tt(sm(9, 40), sm(8, 40), c("j40", 0, 40), A.add)
-        tt(sm(4), bank(6, 128, 24), sm(2), A.add)
-        if t:
+            tt(sm(3), sm(2), sm(2), A.mult)
             cp("v", c("wo16", 0, 40), sm(9, 40))
-        ts(sm(5), sm(3), 0.0, A.max, 255.0, A.min)
-        if t:
-            cp("s", c(wb, 0, 640), ind(c(wbo, 0, 1280), c("wo16", 0, 40)))
-            ts(c("wbm", 0, 640), ind(c(wbo, 0, 1280), c("wo16", 0, 40)), 1.0, A.min)
-            gather_all(lambda a_, b_: c("wbm", a_, b_), 640, 0, 0, 1920)
-            wraw()
-            wshift("s", 0)
-            wshift("s", 1)
-        tt(sm(6), sm(5), sm(3), A.is_equal)
-        tt(sm(7), sm(6), sm(4), A.mult)
-        tt(sm(0), sm(7), c("dump", 0, 24), A.add)
-        cp("v", c("pos16", 0, 24), sm(0))
-        if t == TR - 1:
-            for k, d in enumerate(others):
-                dma("y", c("so", 256 * k, 256 * k + 160), c(wb, 0, 640, p=blkp(d)), "pko%d" % d)
-            dma("y", ext(T.yw[32 * r:32 * r + 32, :]), c(wb, 0, 640, p=blkp(r)), "st")
-        if t == 0:
-            wcopy(2)
-            wcopy(3)
-            cp("v", c("pk", 0, 384), c("pkf", 0, 384))
-        cp("v", ind(c("lst", 0, 640), c("pos16", 0, 24)), c("pk", 0, 384))
-        if t:
-            for b in range(4):
-                wcopy(b)
-        ts(c("rx16", 0, 256), c("lst", 0, 256), 2.0 ** -12, A.mult)
-        if t:
-            wshift("v", 2)
-            wshift("v", 3)
-        ts(c("lo_i", 0, 256), c("lst", 0, 256), 4095, A.bitwise_and)
-        ts(sm(1), sm(0), 16.0, A.mult, 15.0, A.add)
+            ts(c("wm", 0, 640), ind(c(wo, 0, 1280), c("wo16", 0, 40)), 1.0, A.min)
+            cp("s", c(wn, 640, 1280), ind(c(wo, 0, 1280), c("wo16", 0, 40)))
+            w_window()
+            turn_dma(wn, 640, 640, "wr%d" % t)
+            if t == TR - 1:
+                for k, d in enumerate(others):
+                    dma("y", c("so", 256 * k, 256 * k + 160), c(wn, 640, 1280, p=blkp(d)), "pko%d" % d)
+                dma("y", ext(T.yw[32 * r:32 * r + 32, :]), c(wn, 640, 1280, p=blkp(r)), "st")
+                for k, d in enumerate(others):
+                    send(d, c("lo", 256 * r, 256 * r + 160), c("so", 256 * k, 256 * k + 160), "arw%d" % r)
+                for s in others[::-1]:
+                    dma("y", ext(T.yw[32 * s:32 * s + 32, :]), c("lo", 256 * s, 256 * s + 160), "st")
+        else:
+            cp("v", c("pos16", 0, 24), bank(4, 256, 24))
+            ts(sm(1), bank(4, 256, 24), 16.0, A.mult, 15.0 - 16 * S0, A.add)
+            ts(sm(2), bank(4, 256, 24), -S0 - 127.5, A.add)
+            tt(sm(3), sm(2), sm(2), A.mult)
+        cp("v", ind(c("lst", 0, 896), c("pos16", 0, 24)), c("pk", 0, 384))
+        ts(sm(4), sm(3), 16384.0, A.is_ge, 16384.0, A.mult)
+        ts(c("rx16", 0, 256), c("lst", S0, S0 + 256), 2.0 ** -12, A.mult)
+        ts(c("lo_i", 0, 256), c("lst", S0, S0 + 256), 4095, A.bitwise_and)
+        tt(sm(5), sm(4), sm(1), A.add)
         cp("v", c("ot16", 0, 256), c("lo_i", 0, 256))
+        tt(sm(6), sm(5), c("dump", 0, 24), A.min)
         for a_, b_ in CH1:
             cp("s", c("wg", 16 * a_, 16 * b_), ind(c("wm", 0, 2560), c("rx16", a_, b_)))
-        for x, (a_, b_) in enumerate(XCH):
-            cp("s", c("xg", 16 * a_, 16 * b_), ind(c("wr", 0, 2560), c("rx16", 80 + a_, 80 + b_)), 0.125)
-            if x < 2:
-                mm(bank(3 + x), c("agi", 512, 640), c("xg", 16 * a_ + 1, 16 * b_, 2))
-        ts(sm(2), sm(0), 3840.0, A.add)
+        for a_, b_ in XCH:
+            cp("s", c("xg", 16 * a_, 16 * b_), ind(c(wn, 640, 3200), c("rx16", 80 + a_, 80 + b_)), 0.125)
+            mm(c("ps", 8 * a_, 8 * b_), turn(0), c("xg", 16 * a_ + 1, 16 * b_, 2))
         if t:
-            tt(c("taum", 0, 384), ind(c("pm", 0, 640), c("pos16", 0, 24)), c("tau_o", 0, 384), A.mult)
-        products(*CH1[0])
-        tt(sm(3), sm(1), sm(2), A.min)
-        if t == 0:
-            tt(c("taum", 0, 384), ind(c("pm", 0, 640), c("pos16", 0, 24)), c("tau_o", 0, 384), A.mult)
-        cp("v", c("pe16", 0, 24), sm(3))
+            tt(c("taum", 0, 384), ind(c("pm", 0, 896), c("pos16", 0, 24)), c("tau_o", 0, 384), A.mult)
+        cp("v", c("pe16", 0, 24), sm(6))
+        products("ea", *CH1[0])
         for x in range(1, len(CH1)):
-            maxima(ec, *CH1[x - 1])
-            products(*CH1[x])
-        maxima(ec, *CH1[-1])
-        spread(ec, c("et", 0, 384))
-        mm(bank(7, 0, 384), c("agi", 512, 640), c("xg", 2049, 2816, 2))
-        gather_all(lambda a_, b_: c("et", a_, b_), 384, 0)
-        for x in range(2):
-            a_, b_ = XCH[x]
-            tt(c("y1", 4 * a_, 4 * b_), c("xg", 16 * a_, 16 * b_, 4), c("ps", 512 * (3 + x), 512 * (4 + x), 2), A.add)
-            tt(c("ps", 2560 + 4 * a_, 2560 + 4 * b_), c("xg", 16 * a_ + 2, 16 * b_, 4), c("ps", 512 * (3 + x) + 1, 512 * (4 + x), 2), A.add)
-        cp("s", c("ew", 0, 512), bank(0))
-        a_, b_ = XCH[2]
-        tt(c("y1", 4 * a_, 4 * b_), c("xg", 16 * a_, 16 * b_, 4), c("ps", 3584, 3968, 2), A.add)
-        tt(c("ps", 2560 + 4 * a_, 2560 + 4 * b_), c("xg", 16 * a_ + 2, 16 * b_, 4), c("ps", 3585, 3968, 2), A.add)
-        cp("s", c("ew", 512, 1024), bank(1))
-        cp("s", c("ew", 1024, 1536), bank(2))
-        tt(c("z1", 0, 352), c("y1", 0, 704, 2), c("ps", 2560, 3264, 2), A.add)
-        tt(bank(7, 0, 352), c("y1", 1, 704, 2), c("ps", 2561, 3264, 2), A.add)
-        tt(c("p1", 0, 176), c("z1", 0, 352, 2), c("ps", 3584, 3936, 2), A.add)
-        tt(bank(3, 0, 176), c("z1", 1, 352, 2), c("ps", 3585, 3936, 2), A.add)
-        tt(c("dw", 80, 256), c("p1", 0, 176), bank(3, 0, 176), A.subtract)
-        tt(c("ct", 0, 384), ind(c("dw", 0, 640), c("pos16", 0, 24)), c("co", 0, 384), A.add)
-        ts(c("co", 0, 384), c("ct", 0, 384), 0.125, A.max, 8.0, A.min)
-        nh = 16 * (256 - HY)
+            products("ea", *CH1[x])
+            maxima("ea", *CH1[x - 1])
+        if t == 0:
+            tt(c("taum", 0, 384), ind(c("pm", 0, 896), c("pos16", 0, 24)), c("tau_o", 0, 384), A.mult)
+        maxima("ea", *CH1[-1])
+        spread("ea", "eb")
+        e_window("eb")
+        e_out("eb", (1, 2, 3))
         for a_, b_ in CH3:
-            cp("s", c("eg", 16 * (a_ - HY), 16 * (b_ - HY)), ind(c("ew", 0, 1536), c("ot16", a_, b_)))
-        for o in range(0, nh, 512):
-            mm(c("ps", o, o + 512), c("agi", 512, 640), c("wg", 16 * HY + o, 16 * HY + o + 512))
-        if t < TR - 1:
-            gather_all(lambda a_, b_: c("co", a_, b_), 384, 4)
-            for b in range(3):
-                cp("s", c("cw", 512 * b, 512 * b + 512), bank(4 + b))
-        else:
-            for k, d in enumerate(others):
-                dma("y", c("so", 256 * k + 160, 256 * k + 256), c("co", 0, 384, p=blkp(d)), "pko%d" % d)
-            dma("y", ext(T.yc[32 * r:32 * r + 32, :]), c("co", 0, 384, p=blkp(r)), "st")
-            for k, d in enumerate(others):
-                send(d, c("lo", 256 * r, 256 * r + 256), c("so", 256 * k, 256 * k + 256), "aro%d" % r)
-            for s in others[::-1]:
-                dma("y", ext(T.yw[32 * s:32 * s + 32, :]), c("lo", 256 * s, 256 * s + 160), "st")
-                dma("y", ext(T.yc[32 * s:32 * s + 32, :]), c("lo", 256 * s + 160, 256 * s + 256), "st")
+            cp("s", c("eg", 16 * (a_ - HY), 16 * (b_ - HY)), ind(c("eb", 4096, 5632), c("ot16", a_, b_)))
+        tt(c("y1", 0, 704), c("xg", 0, 2816, 4), c("ps", 0, 1408, 2), A.add)
+        tt(c("ps", 1536, 2240), c("xg", 2, 2816, 4), c("ps", 1, 1408, 2), A.add)
+        tt(c("z1", 0, 352), c("y1", 0, 704, 2), c("ps", 1536, 2240, 2), A.add)
+        tt(bank(0, 0, 352), c("y1", 1, 704, 2), c("ps", 1537, 2240, 2), A.add)
+        tt(c("p1", 0, 176), c("z1", 0, 352, 2), c("ps", 0, 352, 2), A.add)
+        tt(bank(1, 0, 176), c("z1", 1, 352, 2), c("ps", 1, 352, 2), A.add)
+        tt(c("dw", 512, 688), c("p1", 0, 176), bank(1, 0, 176), A.subtract)
         if t == 0:
             cp("v", c("abi", 0, 80), c("kab", 640, 720))
-        for a_, b_ in CH2:
-            products(a_, b_)
-        for a_, b_ in CH2:
-            maxima(ec, a_, b_)
+        tt(c("ct", 0, 384), ind(c("dw", 0, 896), c("pos16", 0, 24)), c("cw", 0, 384), A.add)
+        products("eb", *CH2[0])
+        ts(c("cw", 0, 384), c("ct", 0, 384), 0.125, A.max, 8.0, A.min)
+        if t < TR - 1:
+            turn_dma("cw", 0, 384, "cg%d" % t)
+        else:
+            for k, d in enumerate(others):
+                dma("y", c("so", 256 * k + 160, 256 * k + 256), c("cw", 0, 384, p=blkp(d)), "pkc%d" % d)
+            dma("y", ext(T.yc[32 * r:32 * r + 32, :]), c("cw", 0, 384, p=blkp(r)), "st")
+            for k, d in enumerate(others):
+                send(d, c("lo", 256 * r + 160, 256 * r + 256), c("so", 256 * k + 160, 256 * k + 256), "aro%d" % r)
+            for s in others[::-1]:
+                dma("y", ext(T.yc[32 * s:32 * s + 32, :]), c("lo", 256 * s + 160, 256 * s + 256), "st")
+        last = CH2[0]
         for a_, b_ in CH3:
-            tt(c("prod", 16 * a_, 16 * b_), c("eg", 16 * (a_ - HY), 16 * (b_ - HY)), c("ps", 16 * (a_ - HY), 16 * (b_ - HY)), A.mult)
+            scan(c("prod", 16 * a_, 16 * b_), c("wg", 16 * a_, 16 * b_), c("eg", 16 * (a_ - HY), 16 * (b_ - HY)), 1.0, A.min, A.mult)
+            maxima("eb", *last)
+            last = (a_, b_)
         if t == 0:
             ts(c("abt", 0, 80), c("abi", 0, 80), 4, A.arith_shift_right)
             ts(c("abt", 80, 160), c("abi", 0, 80), 15, A.bitwise_and)
             cp("v", c("abd16", 0, 80), c("abt", 0, 80))
             cp("v", c("abm16", 0, 80), c("abt", 80, 160))
             cp("s", c("oh", 0, 1280), ind(c("idg", 0, 16), c("abm16", 0, 80)))
-        for a_, b_ in CH3:
-            maxima(ec, a_, b_)
-        spread(ec, c(ecn, 4096, 4480))
+        maxima("eb", *last)
+        spread("eb", "ea")
 
-    ef = "ec%d" % (TR % 2)
-    dma("y", ext(T.ye[32 * r:32 * r + 32, :]), c(ef, 4096, 4480, p=blkp(r)), "st")
     for k, d in enumerate(others):
         for u in range(4):
-            cp("vs"[u % 2], c("se", 96 * k, 96 * k + 96, p=blkp(u)), c(ef, 4096 + 96 * u, 4192 + 96 * u, p=blkp(d)))
+            cp("vs"[u % 2], c("se", 96 * k, 96 * k + 96, p=blkp(u)), c("ea", 4096 + 96 * u, 4192 + 96 * u, p=blkp(d)), 1.0 / LIFT)
         send(d, c("le", 96 * r, 96 * r + 96), c("se", 96 * k, 96 * k + 96), "are%d" % r)
+    cp("v", c("et", 0, 384, p=blkp(r)), c("ea", 4096, 4480, p=blkp(r)), 1.0 / LIFT)
+    dma("y", ext(T.ye[32 * r:32 * r + 32, :]), c("et", 0, 384, p=blkp(r)), "st")
     for s in others[::-1]:
         lands(c("le", 96 * s, 96 * s + 96), "are%d" % s, ne)
         for u in range(4):

@@ -1,39 +1,41 @@
 from concourse.mybir import AluOpType, ActivationFunctionType
 
 N, SO, RO, TR = 4, 384, 640, 4
-CH1 = [(0, 16), (16, 48), (48, 104), (104, 176), (176, 256)]
-CH2 = [(0, 48)]
-CH3 = [(48, 112), (112, 184), (184, 256)]
+CH1 = [(0, 32), (32, 96), (96, 176), (176, 256)]
+CH2 = [(0, 48), (48, 112), (112, 184), (184, 256)]
+HY = 48
 XCH = [(0, 64), (64, 128), (128, 176)]
-HY = CH3[0][0]
 LIFT = 2.0 ** 20
+KUP = 2.0 ** 15
 S0 = 432
+WA, WB = 288, 216
 F, B, I, U = "float32", "bfloat16", "int32", "uint16"
 SCRATCH = {
     "ps": ("psum", [128, 4096], F),
-    "sa": ("sbuf", [128, 3 * 384], F), "la": ("sbuf", [128, 4 * 384], F), "sab": ("sbuf", [128, 80], I), "sar": ("sbuf", [128, 160], F),
+    "sa": ("sbuf", [128, 3 * WA], F), "la": ("sbuf", [128, 4 * WA], F), "sab": ("sbuf", [128, 80], I), "sar": ("sbuf", [128, 160], F),
     "sb": ("sbuf", [128, 384], F), "si": ("sbuf", [128, 384], I), "sj": ("sbuf", [128, 384], I), "stau": ("sbuf", [128, 288], F),
-    "sk": ("sbuf", [128, 384], F), "sp": ("sbuf", [128, 288], F), "lb": ("sbuf", [128, 384], F), "lc": ("dram", [4, 128, 96], F),
-    "ea": ("sbuf", [128, 5640], F), "eb": ("sbuf", [128, 5640], F), "cw": ("sbuf", [128, 1536], F), "wm": ("sbuf", [128, 2560], F),
+    "sk": ("sbuf", [128, 384], F), "sp": ("sbuf", [128, 3 * WB], F), "lb": ("sbuf", [128, 4 * WB], F), "lc": ("dram", [4, 128, 96], F),
+    "ea": ("sbuf", [128, 5632], F), "eb": ("sbuf", [128, 5632], F), "cw": ("sbuf", [128, 1536], F), "wm": ("sbuf", [128, 2560], F),
     "w0": ("sbuf", [128, 3200], F), "w1": ("sbuf", [128, 3200], F),
-    "kab": ("sbuf", [128, 720], F), "tau_o": ("sbuf", [128, 384], F), "pk": ("sbuf", [128, 384], F),
-    "ct": ("sbuf", [128, 384], F), "wt": ("sbuf", [128, 640], F), "et": ("sbuf", [128, 384], F),
-    "dw": ("sbuf", [128, 896], F), "pm": ("sbuf", [128, 896], F), "taum": ("sbuf", [128, 384], F), "lst": ("sbuf", [128, 896], I),
+    "kab": ("sbuf", [128, 720], F), "tau_o": ("sbuf", [128, 384], F), "pk": ("sbuf", [128, 384], F), "ct": ("sbuf", [128, 384], F),
+    "wt": ("sbuf", [128, 640], F), "cb": ("sbuf", [128, 640], F), "et": ("sbuf", [128, 384], F), "thr": ("sbuf", [128, 384], F),
+    "dw": ("sbuf", [128, 896], F), "tz": ("sbuf", [128, 768], F), "taum": ("sbuf", [128, 384], F), "lst": ("sbuf", [128, 896], I),
     "lo_i": ("sbuf", [128, 256], I), "rx16": ("sbuf", [128, 256], U), "ot16": ("sbuf", [128, 256], U),
-    "wg": ("sbuf", [128, 4096], F), "prod": ("sbuf", [128, 4096], F), "msk": ("sbuf", [128, 1792], B), "eg": ("sbuf", [128, 16 * (256 - HY)], F),
-    "pe16": ("sbuf", [128, 24], U), "mz": ("sbuf", [128, 128], B),
+    "wg": ("sbuf", [128, 4096], F), "prod": ("sbuf", [128, 4096], F), "msk": ("sbuf", [128, 1280], B), "eg": ("sbuf", [128, 16 * (256 - HY)], F),
+    "pe16": ("sbuf", [128, 24], U), "tz16": ("sbuf", [128, 24], U), "mz": ("sbuf", [128, 128], B), "m0": ("sbuf", [128, 128], B),
     "xg": ("sbuf", [128, 2816], F), "y1": ("sbuf", [128, 704], F), "z1": ("sbuf", [128, 352], F), "p1": ("sbuf", [128, 176], F),
     "ind": ("sbuf", [128, 384], B), "nw": ("sbuf", [128, 96], B), "nr": ("sbuf", [128, 96], B), "ll": ("sbuf", [128, 128], B),
-    "xab": ("sbuf", [128, 1280], B), "oh": ("sbuf", [128, 1280], B), "act": ("sbuf", [128, 40], B), "csr": ("sbuf", [128, 40], B),
-    "css": ("sbuf", [128, 24], B), "sm": ("sbuf", [128, 10, 40], F), "wo16": ("sbuf", [128, 40], U), "pos16": ("sbuf", [128, 24], U),
-    "abi": ("sbuf", [128, 80], I), "abt": ("sbuf", [128, 160], I), "ab16": ("sbuf", [128, 80], U), "abd16": ("sbuf", [128, 80], U), "abm16": ("sbuf", [128, 80], U),
+    "xab": ("sbuf", [128, 1280], B), "xb": ("sbuf", [128, 640], B), "oh": ("sbuf", [128, 2240], B), "act": ("sbuf", [128, 40], B),
+    "csr": ("sbuf", [128, 40], B), "css": ("sbuf", [128, 24], B), "sm": ("sbuf", [128, 10, 40], F), "wo16": ("sbuf", [128, 40], U),
+    "pos16": ("sbuf", [128, 24], U), "abi": ("sbuf", [128, 80], I), "abt": ("sbuf", [128, 160], I), "ab16": ("sbuf", [128, 80], U),
+    "abd16": ("sbuf", [128, 160], U), "abm16": ("sbuf", [128, 80], U),
     "iv": ("sbuf", [128, 256], F), "agi": ("sbuf", [128, 256], F), "ma": ("sbuf", [128, 224], B), "mb": ("sbuf", [128, 224], B), "mt": ("sbuf", [128, 128], B),
     "we": ("sbuf", [128, 2048], B), "blk": ("sbuf", [128, 128], B), "trn": ("sbuf", [128, 128], B), "trn2": ("sbuf", [128, 128], B), "trn0": ("sbuf", [128, 128], B),
     "ci": ("sbuf", [128, 4], I), "cf": ("sbuf", [128, 8], F), "io2": ("sbuf", [128, 200], F), "g8": ("sbuf", [128, 8], B), "idg": ("sbuf", [128, 16], F),
     "j40": ("sbuf", [128, 40], F), "dump": ("sbuf", [128, 24], F), "k2": ("sbuf", [128, 96], F), "one": ("sbuf", [128, 40], B),
     "so": ("sbuf", [128, 3 * 256], F), "lo": ("sbuf", [128, 4 * 256], F), "se": ("sbuf", [128, 3 * 96], F), "le": ("sbuf", [128, 4 * 96], F),
 }
-SEMAPHORES = (["qv", "qs", "qp", "qg", "rl", "lco", "lbt", "ldb", "ldi", "ldab", "st"]
+SEMAPHORES = (["qv", "qs", "qp", "qg", "rl", "lco", "lbt", "ldb", "ldi", "ldab", "lde", "st"]
               + ["%s%d" % (n, k) for n in ("lda", "ara", "arb", "arc", "arn", "aro", "arw", "are", "pko", "pkc", "wr", "cg") for k in range(4)])
 SHAPES = {n: v[1] for n, v in SCRATCH.items()}
 A = AluOpType
@@ -170,6 +172,10 @@ def rank_program(g, core, T, topo):
             return op("s", lambda: g.scalar.activation(out["ap"], a_["ap"], ACT.Copy), [a_], [out])
         return op("s", lambda: g.scalar.activation(out["ap"], a_["ap"], ACT.Copy, scale=scale), [a_], [out])
 
+    def act(out, a_, func, scale, bias):
+        rd = [a_] + ([bias] if isinstance(bias, dict) else [])
+        return op("s", lambda: g.scalar.activation(out["ap"], a_["ap"], func, bias=sc_(bias), scale=scale), rd, [out])
+
     def ms(out, val):
         return op("v", lambda: g.vector.memset(out["ap"], val), [], [out])
 
@@ -203,28 +209,30 @@ def rank_program(g, core, T, topo):
     ne = len(engines((r + 1) % N))
     others = [(r + k) % N for k in (1, 2, 3)]
     for s in others:
-        lands(c("la", 384 * s, 384 * s + 384), "ara%d" % s, ne)
-        lands(c("lb", 96 * s, 96 * s + 96), "arb%d" % s, ne)
+        lands(c("la", WA * s, WA * s + WA), "ara%d" % s, ne)
+        lands(c("lb", WB * s, WB * s + WB), "arb%d" % s, ne)
         lands(ap("lc", s), "arc%d" % s, ne)
         lands(c("lo", 256 * s, 256 * s + 160), "arw%d" % s, ne)
         lands(c("lo", 256 * s + 160, 256 * s + 256), "aro%d" % s, ne)
-    for t in range(TR):
+    for t in range(1, TR):
         lands(c("nr", 24 * t, 24 * t + 24), "arn%d" % t, ne)
 
     def pack(d, a_, b_, p=None):
         k = others.index(d) if d != r else None
-        return c("la", 384 * r + a_, 384 * r + b_, p=p) if d == r else c("sa", 384 * k + a_, 384 * k + b_, p=p)
+        return c("la", WA * r + a_, WA * r + b_, p=p) if d == r else c("sa", WA * k + a_, WA * k + b_, p=p)
 
     dma("y", c("sab", 0, 40), ext(T.ra[:, :]), "ldab")
-    dma("s", c("sab", 40, 80), ext(T.rb[:, :]), "ldab")
+    dma("y", c("sab", 40, 80), ext(T.rb[:, :]), "ldab")
     for d in others + [r]:
         rows = slice(32 * d, 32 * d + 32)
-        dma("y", pack(d, 0, 384, blkp(0)), ext(T.ein[rows, :]), "lda%d" % d)
-        dma("s", pack(d, 0, 384, blkp(1)), ext(T.cin[rows, :]), "lda%d" % d)
-        dma("y", pack(d, 0, 384, blkp(2)), ext(T.kin[rows, 0:384]), "lda%d" % d)
-        dma("s", pack(d, 0, 256, blkp(3)), ext(T.kin[rows, 384:640]), "lda%d" % d)
+        dma("s", pack(d, 0, 288, blkp(0)), ext(T.cin[rows, 0:288]), "lda%d" % d)
+        dma("y", pack(d, 0, 96, blkp(1)), ext(T.cin[rows, 288:384]), "lda%d" % d)
+        dma("s", pack(d, 96, 160, blkp(1)), ext(T.kin[rows, 576:640]), "lda%d" % d)
+        dma("y", pack(d, 0, 288, blkp(2)), ext(T.kin[rows, 0:288]), "lda%d" % d)
+        dma("s", pack(d, 0, 288, blkp(3)), ext(T.kin[rows, 288:576]), "lda%d" % d)
     dma("y", c("si", 0, 384), ext(T.rx[:, :]), "ldi")
-    dma("s", c("sj", 0, 384), ext(T.ot[:, :]), "ldi")
+    dma("y", c("sj", 0, 384), ext(T.ot[:, :]), "ldi")
+    dma("y", c("et", 0, 384), ext(T.ein[:, :]), "lde")
     for k, d in enumerate(others):
         dma("y", c("stau", 96 * k, 96 * k + 96), ext(T.tau[32 * d:32 * d + 32, :]), "ldb")
     dma("y", ap("lc", r), ext(T.tau[32 * r:32 * r + 32, :]), "lco")
@@ -232,91 +240,116 @@ def rank_program(g, core, T, topo):
     iota(c("ci", 0, 1), [[0, 1]], 0, 1, False)
     iota(c("io2", 0, 128), [[16, 8], [0, 16]], 0, 0)
     iota(c("iv", 0, 256), [[0, 2], [-1, 128]], 0, 1)
+    iota(c("io2", 128, 144), [[1, 16]], 0, 0)
+    iota(c("io2", 144, 184), [[16, 40]], 0, 1)
     for d in others + [r]:
-        ms(pack(d, 336, 384, blkp(3)), 0.0)
+        ms(pack(d, 240, 288, blkp(1)), 0.0)
     ms(c("we", 0, 2048), 0.0)
     ts(c("ci", 1, 2), c("ci", 0, 1), 112, A.bitwise_and)
     ts(c("ci", 2, 3), c("ci", 0, 1), 15, A.bitwise_and)
     cp("v", c("cf", 0, 3), c("ci", 0, 3))
     kg16, pmod = c("cf", 1, 2), c("cf", 2, 3)
     ts(c("g8", 0, 8), c("io2", 0, 128, 16), kg16, A.is_equal)
-    for e in range(16):
-        cp("s", c("we", 128 * e + e, 128 * e + 128, 16), c("g8", 0, 8))
+    ts(c("agi", 0, 256), c("iv", 0, 256), 0.0, A.is_equal)
     ts(c("sar", 0, 80), c("sab", 0, 80), float(SO * r), A.is_lt, float(N * SO), A.mult)
     tt(c("sar", 80, 160), c("sar", 0, 80), c("sab", 0, 80), A.add)
     for d in others + [r]:
-        ts(pack(d, 256, 336, blkp(3)), c("sar", 80, 160, p=blkp(d)), -float(SO * r), A.add)
+        ts(pack(d, 160, 240, blkp(1)), c("sar", 80, 160, p=blkp(d)), -float(SO * r), A.add)
         if d != r:
-            send(d, c("la", 384 * r, 384 * r + 384), pack(d, 0, 384), "ara%d" % r)
-    ts(c("agi", 0, 256), c("iv", 0, 256), 0.0, A.is_equal)
+            send(d, c("la", WA * r, WA * r + WA), pack(d, 0, WA), "ara%d" % r)
+
+    for e in range(16):
+        cp("s", c("we", 128 * e + e, 128 * e + 128, 16), c("g8", 0, 8))
     ts(c("blk", 0, 128), c("io2", 0, 128), kg16, A.is_equal, 2.0 ** -9, A.mult)
     ts(c("trn0", 0, 128), c("io2", 0, 128), kg16, A.is_equal, -2.0 ** -9, A.mult)
     ms(c("mz", 0, 128), 0.0)
     cp("s", c("mt", 0, 128), c("agi", 0, 128), 2.0)
-    ms(c("lst", 0, 896), 0)
-    ms(c("dw", 0, 896), 0.0)
-    ts(bank(0, 0, 384), c("si", 0, 384), 4096.0, A.mult, -4096.0 * RO * r - SO * r, A.add)
-    ts(bank(1, 0, 384), c("si", 0, 384), float(RO * r), A.is_lt, 4096.0 * N * RO, A.mult)
-    ts(bank(2, 0, 384), c("sj", 0, 384), float(SO * r), A.is_lt, float(N * SO), A.mult)
-    tt(c("sk", 0, 384), c("sj", 0, 384), bank(0, 0, 384), A.add)
-    tt(c("sb", 0, 384), c("sk", 0, 384), bank(1, 0, 384), A.add)
-    tt(c("sk", 0, 384), c("sb", 0, 384), bank(2, 0, 384), A.add)
-    for k, d in enumerate(others):
-        for u in range(4):
-            cp("vs"[u % 2], c("sp", 96 * k, 96 * k + 96, p=blkp(u)), c("sk", 96 * u, 96 * u + 96, p=blkp(d)))
-        send(d, c("lb", 96 * r, 96 * r + 96), c("sp", 96 * k, 96 * k + 96), "arb%d" % r)
-    cp("s", c("pk", 0, 384, p=blkp(r)), c("sk", 0, 384, p=blkp(r)))
-
-    iota(c("io2", 128, 144), [[1, 16]], 0, 0)
-    iota(c("io2", 144, 184), [[16, 40]], 0, 1)
+    tt(c("m0", 0, 128), c("mt", 0, 128), c("agi", 16, 144), A.add)
+    for k in range(3):
+        ms(c("sp", WB * k + 192, WB * k + WB), 0.0)
+    cp("s", c("dw", 0, 896), c("we", 0, 896), 0.0)
+    asel(c("trn", 0, 128), c("trn0", 0, 128), [[-1, 128]], A.is_ge, 0.0, 0)
     asel(c("ma", 0, 128), c("mt", 0, 128), [[-32, 4], [1000, 2], [-1, 16]], A.not_equal, 1.0, -16)
     asel(c("mb", 0, 128), c("mz", 0, 128), [[-32, 4], [-1000, 2], [-1, 16]], A.not_equal, 1.0, 1000)
-    asel(c("trn", 0, 128), c("trn0", 0, 128), [[-1, 128]], A.is_ge, 0.0, 0)
     asel(c("trn2", 0, 128), c("trn", 0, 128), [[-1, 128]], A.not_equal, -2.0, 0)
-    cp("s", c("pm", 0, 896), c("dw", 0, 896))
-    ms(c("pm", S0, S0 + 256), LIFT)
-    ms(c("msk", 0, 1792), 1.0)
-    ms(c("msk", 0, 1792, 16), 0.0)
+    cp("s", c("tz", 384, 768), c("dw", 0, 384))
 
     def late_constants():
         ts(c("j40", 0, 40), c("io2", 144, 184), kg16, A.subtract)
-        ts(c("idg", 0, 16), c("io2", 128, 144), pmod, A.is_equal)
+        ts(c("idg", 0, 16), c("io2", 128, 144), pmod, A.is_equal, -1.0, A.mult)
         ms(c("one", 0, 40), 1.0)
+        ms(c("cf", 4, 5), -(0.125 * LIFT - 2.0 ** -7) * 2.0 ** 25)
+        ms(c("cf", 5, 6), 0.125 * LIFT)
         ts(c("dump", 0, 24), c("j40", 0, 24), 4096.0, A.add)
         for t in range(TR):
             ts(c("k2", 30 * t, 24 * t + 24), c("j40", 6 * t, 24), -1.0, A.mult, 511.0 + 96.0 * t, A.add)
             if t:
                 ts(c("k2", 24 * t, 30 * t), c("j40", 0, 6 * t), -1.0, A.mult, 127.0 + 96.0 * t, A.add)
-        cp("s", c("ma", 128, 224), c("ma", 0, 96))
-        cp("s", c("mb", 128, 224), c("mb", 0, 96))
 
-    for k, s in enumerate([r] + others[::-1]):
-        o = 384 * s
-        if k == 2:
-            late_constants()
-        cp("v", c("ea", 4096, 4480, p=blkp(s)), c("la", o, o + 384, p=blkp(0)), LIFT)
-        if k == 3:
-            ts(c("ind", 0, 384), c("ea", 4096, 4480), 0.125 * LIFT, A.is_ge)
-        cp("s", c("kab", 384, 720, p=blkp(s)), c("la", o, o + 336, p=blkp(3)))
+    def take_a(s):
+        o = WA * s
+        cp("v", c("kab", 640, 720, p=blkp(s)), c("la", o + 160, o + 240, p=blkp(1)))
+        cp("v", c("kab", 576, 640, p=blkp(s)), c("la", o + 96, o + 160, p=blkp(1)), KUP)
         for y in range(N):
             m = (s - y) % N
-            cp("vs"[y % 2], c("cw", 384 * m, 384 * m + 384, p=blkp(y)), c("la", o, o + 384, p=blkp(1)))
-        cp("s", c("kab", 0, 384, p=blkp(s)), c("la", o, o + 384, p=blkp(2)))
+            cp("vs"[y % 2], c("cw", 384 * m, 384 * m + 288, p=blkp(y)), c("la", o, o + 288, p=blkp(0)))
+            cp("s" if y < 3 else "v", c("cw", 384 * m + 288, 384 * m + 384, p=blkp(y)), c("la", o, o + 96, p=blkp(1)))
+        if s == others[0]:
+            cp("v", c("ab16", 0, 80), c("kab", 640, 720))
+        cp("s", c("kab", 0, 288, p=blkp(s)), c("la", o, o + 288, p=blkp(2)), KUP)
+        cp("v", c("kab", 288, 576, p=blkp(s)), c("la", o, o + 288, p=blkp(3)), KUP)
 
-    def turn_pe(buf, base, width, at, ms_):
-        for k, m in enumerate(ms_):
-            a_ = 0
-            while a_ < width:
-                o = at[k] + a_
-                b_ = min(width, a_ + 512 - o % 512)
-                mm(c("ps", o, o + b_ - a_), turn(m), c(buf, base + a_, base + b_))
-                a_ = b_
+    def take_lists(q, s):
+        cp(q, c("ll", 8, 32, p=blkp(s)), c("lb", WB * s + 192, WB * s + WB, p=blkp(0)))
+        for h in range(2):
+            cp(q, c("pk", 192 * h, 192 * h + 192, p=blkp(s)), c("lb", WB * s, WB * s + 192, p=blkp(h)))
 
-    def turn_out(q, buf, base, width, at, m):
-        cp(q, c(buf, base + m * width, base + (m + 1) * width), c("ps", at, at + width))
+    def take_e(q, s):
+        for h in range(2):
+            cp(q, c("ea", 4096 + 192 * h, 4288 + 192 * h, p=blkp(s)), c("lb", WB * s, WB * s + 192, p=blkp(2 + h)))
+
+    take_a(r)
+    cp("s", c("ea", 4096, 4480, p=blkp(r)), c("et", 0, 384, p=blkp(r)), LIFT)
+    for k, d in enumerate(others):
+        for h in range(2):
+            cp("s", c("sp", WB * k, WB * k + 192, p=blkp(2 + h)), c("et", 192 * h, 192 * h + 192, p=blkp(d)), LIFT)
+    ts(bank(0, 0, 384), c("si", 0, 384), 4096.0, A.mult, -4096.0 * RO * r - SO * r, A.add)
+    ts(bank(1, 0, 384), c("si", 0, 384), float(RO * r), A.is_lt, 4096.0 * N * RO, A.mult)
+    ts(bank(2, 0, 384), c("sj", 0, 384), float(SO * r), A.is_lt, float(N * SO), A.mult)
+    ts(c("ind", 0, 384), c("et", 0, 384), 0.125, A.is_ge)
+    for e in range(16):
+        mm(bank(4, 0, 24), c("we", 128 * e, 128 * e + 128), c("ind", e, 384, 16), e == 0, e == 15)
+    tt(c("sk", 0, 384), c("sj", 0, 384), bank(0, 0, 384), A.add)
+    cp("v", c("nw", 0, 24), bank(4, 0, 24))
+    mm(bank(5, 0, 24), c("m0", 0, 128), c("nw", 0, 24))
+    tt(c("sb", 0, 384), c("sk", 0, 384), bank(1, 0, 384), A.add)
+    for k, d in enumerate(others):
+        ts(c("sp", WB * k + 192, WB * k + WB, p=blkp(0)), c("ps", 2560, 2584, p=blkp(d)), 23.5, A.is_ge, 512.0, A.mult)
+    tt(c("sk", 0, 384), c("sb", 0, 384), bank(2, 0, 384), A.add)
+    for k, d in enumerate(others):
+        for h in range(2):
+            cp("vs"[h], c("sp", WB * k, WB * k + 192, p=blkp(h)), c("sk", 192 * h, 192 * h + 192, p=blkp(d)))
+        send(d, c("lb", WB * r, WB * r + WB), c("sp", WB * k, WB * k + WB), "arb%d" % r)
+    for k, d in enumerate(others):
+        send(d, ap("lc", r), c("stau", 96 * k, 96 * k + 96), "arc%d" % r)
+    iota(c("lst", 0, 896), [[0, 896]], 0, 0, False)
+    ts(c("ll", 8, 32, p=blkp(r)), c("ps", 2560, 2584, p=blkp(r)), 23.5, A.is_ge, 512.0, A.mult)
+    cp("s", c("pk", 0, 384, p=blkp(r)), c("sk", 0, 384, p=blkp(r)))
+    late_constants()
+    for s in others[::-1]:
+        take_a(s)
+        if s == others[2]:
+            ms(c("msk", 0, 1280), 1.0)
+        if s == others[1]:
+            ms(c("msk", 0, 1280, 16), 0.0)
 
     def turn_half(q, buf, base, width, h):
-        cp(q, c(buf, base + 2 * width, base + 3 * width, p=(64 * h, 64 * h + 64)), c(buf, base, base + width, p=(64 - 64 * h, 128 - 64 * h)))
+        out, in_ = c(buf, base + 2 * width, base + 3 * width, p=(64 * h, 64 * h + 64)), c(buf, base, base + width, p=(64 - 64 * h, 128 - 64 * h))
+        if q == "g":
+            wait("g", ("qg", cnt["qg"], {}))
+            asel(out, in_, [[0, width]], A.is_ge, 0.0, 0)
+        else:
+            cp(q, out, in_)
 
     def turn_dma(buf, base, width, sem):
         for m in (1, 2, 3):
@@ -324,19 +357,35 @@ def rank_program(g, core, T, topo):
             dma("y", c(buf, o, o + width, p=(0, 128 - 32 * m)), c(buf, base, base + width, p=(32 * m, 128)), sem)
             dma("y", c(buf, o, o + width, p=(128 - 32 * m, 128)), c(buf, base, base + width, p=(0, 32 * m)), sem)
 
-    def e_window(buf):
-        turn_pe(buf, 4096, 384, (2560, 3072, 3584), (1, 2, 3))
-
-    def e_out(buf, ms_):
+    def e_window(buf, ms_=(1, 2, 3)):
         for m in ms_:
-            turn_out("s", buf, 4096, 384, 2048 + 512 * m, m)
+            mm(bank(4 + m, 0, 384), turn(m), c(buf, 4096, 4480))
+
+    def e_out(buf, ms_=(1, 2, 3)):
+        for m in ms_:
+            cp("s", c(buf, 4096 + 384 * m, 4480 + 384 * m), bank(4 + m, 0, 384))
+
+    def w_window(between=None):
+        parts = [(m, h) for h in (0, 320) for m in (1, 3)]
+        for b, (m, h) in enumerate(parts):
+            mm(bank(b, 128, 320), turn(m), c("wm", h, h + 320))
+            if between and b == 0:
+                between()
+        turn_half("g", "wm", 0, 640, 0)
+        turn_half("s", "wm", 0, 640, 1)
+        for b, (m, h) in enumerate(parts):
+            cp("s", c("wm", 640 * m + h, 640 * m + h + 320), bank(b, 128, 320))
 
     def new_rates(out):
         tt(c("wt", 0, 640), ind(c("cw", 0, 1536), c("ab16", 0, 40)), c("kab", 0, 640), A.mult)
-        tt(out, ind(c("cw", 0, 1536), c("ab16", 40, 80)), c("wt", 0, 640), A.mult)
+        cp("s", c("cb", 0, 640), ind(c("cw", 0, 1536), c("ab16", 40, 80)), 1.0 / KUP)
+        scan(out, c("cb", 0, 640), c("wt", 0, 640), 1.0, A.min, A.mult)
 
-    def products(e_, a_, b_):
-        tt(c("prod", 16 * a_, 16 * b_), ind(c(e_, 4096, 5632), c("ot16", a_, b_)), c("wg", 16 * a_, 16 * b_), A.mult)
+    def products(e_, a_, b_, hy):
+        if a_ < hy:
+            tt(c("prod", 16 * a_, 16 * b_), ind(c(e_, 4096, 5632), c("ot16", a_, b_)), c("wg", 16 * a_, 16 * b_), A.mult)
+        else:
+            scan(c("prod", 16 * a_, 16 * b_), c("wg", 16 * a_, 16 * b_), c("eg", 16 * (a_ - HY), 16 * (b_ - HY)), 1.0, A.min, A.mult)
 
     def maxima(e_, a_, b_):
         scan(c(e_, 16 * a_, 16 * b_), c("msk", 0, 16 * (b_ - a_)), c("prod", 16 * a_, 16 * b_), 0.0, A.mult, A.max)
@@ -344,79 +393,78 @@ def rank_program(g, core, T, topo):
     def spread(e_, to):
         tt(c(to, 4096, 4480), ind(c(e_, 0, 4480), c("pe16", 0, 24)), c("taum", 0, 384), A.max)
 
+    def least():
+        cp("s", c("taum", 0, 384), ind(c("tz", 0, 768), c("tz16", 0, 24)))
+
+    def bound():
+        act(c("thr", 0, 384), c("taum", 0, 384), ACT.Relu, 2.0 ** 25, c("cf", 4, 5))
+        act(c("thr", 0, 384), c("thr", 0, 384), ACT.Identity, -1.0, c("cf", 5, 6))
+
     for t in range(TR):
         wn, wo = "w%d" % (t % 2), "w%d" % ((t + 1) % 2)
         nw, nr = c("nw", 24 * t, 24 * t + 24), c("nr", 24 * t, 24 * t + 24)
-        if t:
-            ts(c("ind", 0, 384), c("ea", 4096, 4480), 0.125 * LIFT, A.is_ge)
-        for e in range(16):
-            mm(bank(4, 0, 24), c("we", 128 * e, 128 * e + 128), c("ind", e, 384, 16), e == 0, e == 15)
-        if t == 0:
-            cp("v", c("ab16", 0, 80), c("kab", 640, 720))
-        cp("v", nw, bank(4, 0, 24))
-        send((r - 1) % N, nr, nw, "arn%d" % t)
-        e_window("ea")
-        if t == 0:
-            for x, d in enumerate(others):
-                send(d, ap("lc", r), c("stau", 96 * x, 96 * x + 96), "arc%d" % r)
-            new_rates(c(wn, 640, 1280))
-            for s in others[::-1]:
-                for u in range(4):
-                    cp("s", c("pk", 96 * u, 96 * u + 96, p=blkp(s)), c("lb", 96 * s, 96 * s + 96, p=blkp(u)))
-        else:
-            new_rates(c(wo, 0, 640))
-        e_out("ea", (1, 2, 3))
+        lw = c("ll", 32, 56) if t else c("ll", 8, 32)
+        p, q_ = 6 * t, 10 * t
+        pos = bank(4, 256, 24)
 
-        def w_window():
-            parts = [(m, h) for m in (1, 3) for h in (0, 320)]
-            for b, (m, h) in enumerate(parts):
-                mm(bank(b, 128, 320), turn(m), c("wm", h, h + 320))
-            turn_half("s", "wm", 0, 640, 0)
-            turn_half("s", "wm", 0, 640, 1)
-            for b, (m, h) in enumerate(parts):
-                cp("s", c("wm", 640 * m + h, 640 * m + h + 320), bank(b, 128, 320))
-        if t == 0:
-            ts(c("wm", 0, 640), c(wn, 640, 1280), 1.0, A.min)
-            w_window()
-            turn_dma(wn, 640, 640, "wr%d" % t)
-            dma("y", c("tau_o", 0, 384), ap("lc"), "lbt")
-        for m in ([0, 1, 2, 3] if t else [0]) + [-1]:
-            x = 32 * max(m, 0)
-            mm(bank(4, 64 + 24 * m, 24), c("ma", x, x + 128), nw, True, False)
-            mm(bank(4, 64 + 24 * m, 24), c("mb", x, x + 128), nr, False, True)
-        n = 120 if t else 48
-        ts(c("ll", 8, 8 + n), bank(4, 40, n), 23.5, A.is_ge, 512.0, A.mult)
-        lw = c("ll", 32, 56)
-        p = 6 * t
+        def places():
+            mm(pos, c("trn", 0, 128), lw, True, False)
+            mm(bank(4, 256 + p, 24 - p), c("blk", 0, 128), c("css", 0, 24 - p), False, False)
+            if p:
+                mm(bank(4, 256, p), c("blk", 0, 128), c("css", 24 - p, 24), False, False)
+            mm(pos, turn(0), sm(0), False, True)
+
+        def in_picks():
+            ts(sm(2), pos, -S0 - 127.5, A.add)
+            ts(sm(1), pos, 16.0, A.mult, 15.0 - 16 * S0, A.add)
+            tt(sm(3), sm(2), sm(2), A.mult)
         if t:
-            for h in range(2):
-                tt(c("xab", 640 * h, 640 * h + 640), ind(c("ll", 32, 128), c("abd16", 40 * h, 40 * h + 40)),
-                   c("oh", 640 * h, 640 * h + 640), A.mult)
-                for e in range(16):
-                    mm(bank(3, 0, 40), c("we", 128 * e, 128 * e + 128), c("xab", 640 * h + e, 640 * h + 640, 16),
-                       h == 0 and e == 0, h == 1 and e == 15)
+            tt(c("ind", 0, 384), ind(c("eb", 0, 4480), c("pe16", 0, 24)), c("thr", 0, 384), A.is_ge)
+            for e in range(16):
+                mm(bank(4, 0, 24), c("we", 128 * e, 128 * e + 128), c("ind", e, 384, 16), e == 0, e == 15)
+            spread("eb", "ea")
+            cp("v", nw, bank(4, 0, 24))
+            send((r - 1) % N, nr, nw, "arn%d" % t)
+            e_window("ea")
+            new_rates(c(wo, 0, 640))
+            e_out("ea")
+            for m in (0, 1, 2, 3, -1):
+                x = 32 * max(m, 0)
+                mm(bank(4, 64 + 24 * m, 24), c("ma", x, x + 128), nw, True, False)
+                mm(bank(4, 64 + 24 * m, 24), c("mb", x, x + 128), nr, False, True)
+            ts(c("ll", 8, 128), bank(4, 40, 120), 23.5, A.is_ge, 512.0, A.mult)
+            cp("s", c("xb", 0, 640), ind(c("ll", 32, 128), c("abd16", 80 + q_, 120 + q_)))
+            tt(c("xab", 0, 640), ind(c("ll", 32, 128), c("abd16", q_, 40 + q_)), c("oh", 16 * q_, 16 * q_ + 640), A.mult)
+            scan(c("xab", 640, 1280), c("xb", 0, 640), c("oh", 1120 + 16 * q_, 1760 + 16 * q_), 0.0, A.max, A.mult)
+            for x in range(32):
+                o = 640 * (x // 16)
+                mm(bank(3, 0, 40), c("we", 128 * (x % 16), 128 * (x % 16) + 128), c("xab", o + x % 16, o + 640, 16), x == 0, x == 31)
+        else:
+            new_rates(c(wn, 640, 1280))
+            for s in others[:0:-1]:
+                take_lists("s", s)
+                take_e("s", s)
+            ts(c("wm", 0, 640), c(wn, 640, 1280), 1.0, A.min)
+            take_lists("v", others[0])
         scan(c("css", 0, 24), c("ll", 8 + p, 32 + p), c("one", 0, 24), 0.0, A.add, A.mult)
         tt(sm(0), lw, c("k2", 24 * t, 24 * t + 24), A.max)
-        mm(bank(4, 256, 24), c("trn", 0, 128), lw, True, False)
-        mm(bank(4, 256 + p, 24 - p), c("blk", 0, 128), c("css", 0, 24 - p), False, False)
-        if p:
-            mm(bank(4, 256, p), c("blk", 0, 128), c("css", 24 - p, 24), False, False)
-        mm(bank(4, 256, 24), turn(0), sm(0), False, True)
         if t:
-            q_ = 10 * t
-            ts(c("act", 0, 40), bank(3, 0, 40), 0.5, A.is_ge, 512.0, A.mult)
-            scan(c("csr", q_, 40), c("act", q_, 40), c("one", q_, 40), 0.0, A.add, A.mult)
-            cp("v", c("pos16", 0, 24), bank(4, 256, 24))
-            scan(c("csr", 0, q_), c("act", 0, q_), c("one", 0, q_), c("csr", 39, 40), A.add, A.mult)
-            mm(bank(3, 64, 40), c("blk", 0, 128), c("csr", 0, 40), True, False)
-            mm(bank(3, 64, 40), c("trn2", 0, 128), c("act", 0, 40), False, True)
-            ts(sm(1), bank(4, 256, 24), 16.0, A.mult, 15.0 - 16 * S0, A.add)
+            places()
+            ts(c("act", 0, 40), bank(3, 0, 40), -0.5, A.is_le, 512.0, A.mult)
+            cp("v", c("pos16", 0, 24), pos)
+            scan(c("csr", 0, 40), c("act", 0, 40), c("one", 0, 40), 0.0, A.add, A.mult)
+            for o, a_, n in ((q_, 0, 40 - q_), (0, 40 - q_, q_)):
+                mm(bank(3, 64 + o, n), c("trn2", 0, 128), c("act", a_, a_ + n), True, False)
+                mm(bank(3, 64 + o, n), c("blk", 0, 128), c("csr", a_, a_ + n), False, True)
+            in_picks()
             ts(sm(8, 40), bank(3, 64, 40), -640.0, A.is_gt, 640.0, A.mult)
-            ts(sm(2), bank(4, 256, 24), -S0 - 127.5, A.add)
+            ts(sm(4), sm(3), 16384.0, A.is_ge, 16384.0, A.mult)
             tt(sm(9, 40), sm(8, 40), c("j40", 0, 40), A.add)
-            tt(sm(3), sm(2), sm(2), A.mult)
+            ts(sm(7), sm(3), 16384.0, A.is_ge, 384.0, A.mult)
             cp("v", c("wo16", 0, 40), sm(9, 40))
-            ts(c("wm", 0, 640), ind(c(wo, 0, 1280), c("wo16", 0, 40)), 1.0, A.min)
+            tt(sm(5), sm(4), sm(1), A.add)
+            for h in (0, 20):
+                ts(c("wm", 16 * h, 16 * h + 320), ind(c(wo, 0, 1280), c("wo16", h, h + 20)), 1.0, A.min)
             cp("s", c(wn, 640, 1280), ind(c(wo, 0, 1280), c("wo16", 0, 40)))
             w_window()
             turn_dma(wn, 640, 640, "wr%d" % t)
@@ -429,48 +477,70 @@ def rank_program(g, core, T, topo):
                 for s in others[::-1]:
                     dma("y", ext(T.yw[32 * s:32 * s + 32, :]), c("lo", 256 * s, 256 * s + 160), "st")
         else:
-            cp("v", c("pos16", 0, 24), bank(4, 256, 24))
-            ts(sm(1), bank(4, 256, 24), 16.0, A.mult, 15.0 - 16 * S0, A.add)
-            ts(sm(2), bank(4, 256, 24), -S0 - 127.5, A.add)
-            tt(sm(3), sm(2), sm(2), A.mult)
+            take_e("v", others[0])
+            w_window(places)
+            e_window("ea", (1, 3))
+            turn_dma(wn, 640, 640, "wr%d" % t)
+            dma("y", c("tau_o", 0, 384), ap("lc"), "lbt")
+            cp("v", c("pos16", 0, 24), pos)
+            in_picks()
         cp("v", ind(c("lst", 0, 896), c("pos16", 0, 24)), c("pk", 0, 384))
-        ts(sm(4), sm(3), 16384.0, A.is_ge, 16384.0, A.mult)
+        if t == 0:
+            ts(sm(4), sm(3), 16384.0, A.is_ge, 16384.0, A.mult)
+            ts(sm(7), sm(3), 16384.0, A.is_ge, 384.0, A.mult)
+            tt(sm(5), sm(4), sm(1), A.add)
+        tt(sm(2), sm(7), c("j40", 0, 24), A.add)
+        tt(sm(6), sm(5), c("dump", 0, 24), A.min)
         ts(c("rx16", 0, 256), c("lst", S0, S0 + 256), 2.0 ** -12, A.mult)
         ts(c("lo_i", 0, 256), c("lst", S0, S0 + 256), 4095, A.bitwise_and)
-        tt(sm(5), sm(4), sm(1), A.add)
+        cp("v", c("tz16", 0, 24), sm(2))
         cp("v", c("ot16", 0, 256), c("lo_i", 0, 256))
-        tt(sm(6), sm(5), c("dump", 0, 24), A.min)
-        for a_, b_ in CH1:
+        cp("v", c("pe16", 0, 24), sm(6))
+        if t == 0:
+            e_out("ea", (1, 3))
+        for a_, b_ in CH1[1:]:
             cp("s", c("wg", 16 * a_, 16 * b_), ind(c("wm", 0, 2560), c("rx16", a_, b_)))
+        if t:
+            least()
         for a_, b_ in XCH:
             cp("s", c("xg", 16 * a_, 16 * b_), ind(c(wn, 640, 3200), c("rx16", 80 + a_, 80 + b_)), 0.125)
             mm(c("ps", 8 * a_, 8 * b_), turn(0), c("xg", 16 * a_ + 1, 16 * b_, 2))
-        if t:
-            tt(c("taum", 0, 384), ind(c("pm", 0, 896), c("pos16", 0, 24)), c("tau_o", 0, 384), A.mult)
-        cp("v", c("pe16", 0, 24), sm(6))
-        products("ea", *CH1[0])
-        for x in range(1, len(CH1)):
-            products("ea", *CH1[x])
-            maxima("ea", *CH1[x - 1])
         if t == 0:
-            tt(c("taum", 0, 384), ind(c("pm", 0, 896), c("pos16", 0, 24)), c("tau_o", 0, 384), A.mult)
+            cp("s", c("tz", 0, 384), c("tau_o", 0, 384), LIFT)
+            least()
+            turn_half("v", "ea", 4096, 384, 0)
+            turn_half("v", "ea", 4096, 384, 1)
+        cp("v", c("wg", 0, 16 * CH1[0][1]), ind(c("wm", 0, 2560), c("rx16", *CH1[0])))
+        products("ea", *CH1[0], 256)
+        for x in range(1, len(CH1)):
+            products("ea", *CH1[x], 256)
+            maxima("ea", *CH1[x - 1])
         maxima("ea", *CH1[-1])
         spread("ea", "eb")
         e_window("eb")
-        e_out("eb", (1, 2, 3))
-        for a_, b_ in CH3:
+        e_out("eb")
+        for a_, b_ in CH2[1:]:
             cp("s", c("eg", 16 * (a_ - HY), 16 * (b_ - HY)), ind(c("eb", 4096, 5632), c("ot16", a_, b_)))
+        if t < TR - 1:
+            bound()
         tt(c("y1", 0, 704), c("xg", 0, 2816, 4), c("ps", 0, 1408, 2), A.add)
         tt(c("ps", 1536, 2240), c("xg", 2, 2816, 4), c("ps", 1, 1408, 2), A.add)
-        tt(c("z1", 0, 352), c("y1", 0, 704, 2), c("ps", 1536, 2240, 2), A.add)
-        tt(bank(0, 0, 352), c("y1", 1, 704, 2), c("ps", 1537, 2240, 2), A.add)
-        tt(c("p1", 0, 176), c("z1", 0, 352, 2), c("ps", 0, 352, 2), A.add)
-        tt(bank(1, 0, 176), c("z1", 1, 352, 2), c("ps", 1, 352, 2), A.add)
-        tt(c("dw", 512, 688), c("p1", 0, 176), bank(1, 0, 176), A.subtract)
         if t == 0:
             cp("v", c("abi", 0, 80), c("kab", 640, 720))
+        tt(c("z1", 0, 352), c("y1", 0, 704, 2), c("ps", 1536, 2240, 2), A.add)
+        tt(bank(0, 0, 352), c("y1", 1, 704, 2), c("ps", 1537, 2240, 2), A.add)
+        if t == 0:
+            ts(c("abt", 0, 80), c("abi", 0, 80), 4, A.arith_shift_right)
+            ts(c("abt", 80, 160), c("abi", 0, 80), 15, A.bitwise_and)
+        tt(c("p1", 0, 176), c("z1", 0, 352, 2), c("ps", 0, 352, 2), A.add)
+        tt(bank(1, 0, 176), c("z1", 1, 352, 2), c("ps", 1, 352, 2), A.add)
+        if t == 0:
+            cp("v", c("abm16", 0, 80), c("abt", 80, 160))
+        products("eb", *CH2[0], HY)
+        tt(c("dw", 512, 688), c("p1", 0, 176), bank(1, 0, 176), A.subtract)
+        maxima("eb", *CH2[0])
         tt(c("ct", 0, 384), ind(c("dw", 0, 896), c("pos16", 0, 24)), c("cw", 0, 384), A.add)
-        products("eb", *CH2[0])
+        products("eb", *CH2[1], HY)
         ts(c("cw", 0, 384), c("ct", 0, 384), 0.125, A.max, 8.0, A.min)
         if t < TR - 1:
             turn_dma("cw", 0, 384, "cg%d" % t)
@@ -482,30 +552,31 @@ def rank_program(g, core, T, topo):
                 send(d, c("lo", 256 * r + 160, 256 * r + 256), c("so", 256 * k + 160, 256 * k + 256), "aro%d" % r)
             for s in others[::-1]:
                 dma("y", ext(T.yc[32 * s:32 * s + 32, :]), c("lo", 256 * s + 160, 256 * s + 256), "st")
-        last = CH2[0]
-        for a_, b_ in CH3:
-            scan(c("prod", 16 * a_, 16 * b_), c("wg", 16 * a_, 16 * b_), c("eg", 16 * (a_ - HY), 16 * (b_ - HY)), 1.0, A.min, A.mult)
-            maxima("eb", *last)
-            last = (a_, b_)
+        for x in range(2, len(CH2)):
+            products("eb", *CH2[x], HY)
+            maxima("eb", *CH2[x - 1])
         if t == 0:
-            ts(c("abt", 0, 80), c("abi", 0, 80), 4, A.arith_shift_right)
-            ts(c("abt", 80, 160), c("abi", 0, 80), 15, A.bitwise_and)
-            cp("v", c("abd16", 0, 80), c("abt", 0, 80))
-            cp("v", c("abm16", 0, 80), c("abt", 80, 160))
-            cp("s", c("oh", 0, 1280), ind(c("idg", 0, 16), c("abm16", 0, 80)))
-        maxima("eb", *last)
-        spread("eb", "ea")
+            cp("s", c("ma", 128, 224), c("ma", 0, 96))
+            cp("s", c("mb", 128, 224), c("mb", 0, 96))
+            for h in range(2):
+                cp("v", c("abd16", 80 * h, 80 * h + 40), c("abt", 40 * h, 40 * h + 40))
+                cp("v", c("abd16", 80 * h + 40, 80 * h + 70), c("abt", 40 * h, 40 * h + 30))
+                cp("s", c("oh", 1120 * h, 1120 * h + 640), ind(c("idg", 0, 16), c("abm16", 40 * h, 40 * h + 40)))
+                cp("s", c("oh", 1120 * h + 640, 1120 * h + 1120), c("oh", 1120 * h, 1120 * h + 480))
+        maxima("eb", *CH2[-1])
+    spread("eb", "ea")
 
     for k, d in enumerate(others):
         for u in range(4):
             cp("vs"[u % 2], c("se", 96 * k, 96 * k + 96, p=blkp(u)), c("ea", 4096 + 96 * u, 4192 + 96 * u, p=blkp(d)), 1.0 / LIFT)
         send(d, c("le", 96 * r, 96 * r + 96), c("se", 96 * k, 96 * k + 96), "are%d" % r)
     cp("v", c("et", 0, 384, p=blkp(r)), c("ea", 4096, 4480, p=blkp(r)), 1.0 / LIFT)
-    dma("y", ext(T.ye[32 * r:32 * r + 32, :]), c("et", 0, 384, p=blkp(r)), "st")
     for s in others[::-1]:
         lands(c("le", 96 * s, 96 * s + 96), "are%d" % s, ne)
         for u in range(4):
             dma("ys"[u % 2], ext(T.ye[32 * s:32 * s + 32, 96 * u:96 * u + 96]), c("le", 96 * s, 96 * s + 96, p=blkp(u)), "st")
+        if s == others[2]:
+            dma("y", ext(T.ye[32 * r:32 * r + 32, :]), c("et", 0, 384, p=blkp(r)), "st")
     for sem in cnt:
         if cnt[sem]:
             wait("g", (sem, cnt[sem], {}))

@@ -2,23 +2,25 @@ from concourse.mybir import AluOpType, ActivationFunctionType
 
 N, SO, RO, TR = 4, 384, 640, 4
 CH1 = [(0, 32), (32, 96), (96, 176), (176, 256)]
-CH2 = [(0, 48), (48, 112), (112, 184), (184, 256)]
-HY = 48
+CH2 = [(0, 72), (72, 128), (128, 192), (192, 256)]
+NA = 64
+HY = 72
 XCH = [(0, 64), (64, 128), (128, 176)]
 LIFT = 2.0 ** 20
 KUP = 2.0 ** 15
 S0 = 432
-WA, WB = 288, 216
+WIDE = {"a": 96, "r": 200, "b": 192}
 F, B, I, U = "float32", "bfloat16", "int32", "uint16"
 SCRATCH = {
     "ps": ("psum", [128, 4096], F),
-    "sa": ("sbuf", [128, 3 * WA], F), "la": ("sbuf", [128, 4 * WA], F), "sab": ("sbuf", [128, 80], I), "sar": ("sbuf", [128, 160], F),
-    "sb": ("sbuf", [128, 384], F), "si": ("sbuf", [128, 384], I), "sj": ("sbuf", [128, 384], I), "stau": ("sbuf", [128, 288], F),
-    "sk": ("sbuf", [128, 384], F), "sp": ("sbuf", [128, 3 * WB], F), "lb": ("sbuf", [128, 4 * WB], F), "lc": ("dram", [4, 128, 96], F),
+    "sa": ("sbuf", [128, 3 * 96], F), "la": ("sbuf", [128, 4 * 96], F), "sr": ("sbuf", [128, 3 * 200], F), "lr": ("sbuf", [128, 4 * 200], F),
+    "sb": ("sbuf", [128, 3 * 192], F), "lb": ("sbuf", [128, 4 * 192], F), "stau": ("sbuf", [128, 288], F), "lc": ("dram", [4, 128, 96], F),
+    "sab": ("sbuf", [128, 80], I), "sar": ("sbuf", [128, 160], F), "si": ("sbuf", [128, 384], I), "sj": ("sbuf", [128, 384], I),
+    "sk": ("sbuf", [128, 384], F), "sl": ("sbuf", [128, 384], F),
     "ea": ("sbuf", [128, 5632], F), "eb": ("sbuf", [128, 5632], F), "cw": ("sbuf", [128, 1536], F), "wm": ("sbuf", [128, 2560], F),
     "w0": ("sbuf", [128, 3200], F), "w1": ("sbuf", [128, 3200], F),
     "kab": ("sbuf", [128, 720], F), "tau_o": ("sbuf", [128, 384], F), "pk": ("sbuf", [128, 384], F), "ct": ("sbuf", [128, 384], F),
-    "wt": ("sbuf", [128, 640], F), "cb": ("sbuf", [128, 640], F), "et": ("sbuf", [128, 384], F), "thr": ("sbuf", [128, 384], F),
+    "wt": ("sbuf", [128, 640], F), "ca": ("sbuf", [128, 640], F), "cb": ("sbuf", [128, 640], F), "et": ("sbuf", [128, 384], F), "thr": ("sbuf", [128, 384], F),
     "dw": ("sbuf", [128, 896], F), "tz": ("sbuf", [128, 768], F), "taum": ("sbuf", [128, 384], F), "lst": ("sbuf", [128, 896], I),
     "lo_i": ("sbuf", [128, 256], I), "rx16": ("sbuf", [128, 256], U), "ot16": ("sbuf", [128, 256], U),
     "wg": ("sbuf", [128, 4096], F), "prod": ("sbuf", [128, 4096], F), "msk": ("sbuf", [128, 1280], B), "eg": ("sbuf", [128, 16 * (256 - HY)], F),
@@ -30,13 +32,14 @@ SCRATCH = {
     "pos16": ("sbuf", [128, 24], U), "abi": ("sbuf", [128, 80], I), "abt": ("sbuf", [128, 160], I), "ab16": ("sbuf", [128, 80], U),
     "abd16": ("sbuf", [128, 160], U), "abm16": ("sbuf", [128, 80], U),
     "iv": ("sbuf", [128, 256], F), "agi": ("sbuf", [128, 256], F), "ma": ("sbuf", [128, 224], B), "mb": ("sbuf", [128, 224], B), "mt": ("sbuf", [128, 128], B),
-    "we": ("sbuf", [128, 2048], B), "blk": ("sbuf", [128, 128], B), "trn": ("sbuf", [128, 128], B), "trn2": ("sbuf", [128, 128], B), "trn0": ("sbuf", [128, 128], B),
-    "ci": ("sbuf", [128, 4], I), "cf": ("sbuf", [128, 8], F), "io2": ("sbuf", [128, 200], F), "g8": ("sbuf", [128, 8], B), "idg": ("sbuf", [128, 16], F),
+    "we": ("sbuf", [128, 144], B), "blk": ("sbuf", [128, 128], B), "trn": ("sbuf", [128, 128], B), "trn2": ("sbuf", [128, 128], B), "trn0": ("sbuf", [128, 128], B),
+    "ci": ("sbuf", [128, 4], I), "cf": ("sbuf", [128, 8], F), "io2": ("sbuf", [128, 200], F), "idg": ("sbuf", [128, 16], F),
     "j40": ("sbuf", [128, 40], F), "dump": ("sbuf", [128, 24], F), "k2": ("sbuf", [128, 96], F), "one": ("sbuf", [128, 40], B),
     "so": ("sbuf", [128, 3 * 256], F), "lo": ("sbuf", [128, 4 * 256], F), "se": ("sbuf", [128, 3 * 96], F), "le": ("sbuf", [128, 4 * 96], F),
 }
 SEMAPHORES = (["qv", "qs", "qp", "qg", "rl", "lco", "lbt", "ldb", "ldi", "ldab", "lde", "st"]
-              + ["%s%d" % (n, k) for n in ("lda", "ara", "arb", "arc", "arn", "aro", "arw", "are", "pko", "pkc", "wr", "cg") for k in range(4)])
+              + ["%s%d" % (n, k) for n in ("lda", "ldr", "ara", "arr", "arb", "arc", "arn", "aro", "arw", "are", "pko", "pkc", "wr", "cg")
+                 for k in range(4)])
 SHAPES = {n: v[1] for n, v in SCRATCH.items()}
 A = AluOpType
 ACT = ActivationFunctionType
@@ -164,6 +167,8 @@ def rank_program(g, core, T, topo):
         return op("v", lambda: g.vector.tensor_scalar(out["ap"], a_["ap"], sc_(s1), sc_(s2), o1, o2), rd, [out])
 
     def cp(q, out, a_, scale=None):
+        if q == "g":
+            return asel(out, a_, [[0, a_["regs"][0][4] - a_["regs"][0][3]]], A.is_ge, 0.0, 0)
         if q == "v":
             if scale is not None:
                 return ts(out, a_, scale, A.mult)
@@ -173,15 +178,13 @@ def rank_program(g, core, T, topo):
         return op("s", lambda: g.scalar.activation(out["ap"], a_["ap"], ACT.Copy, scale=scale), [a_], [out])
 
     def act(out, a_, func, scale, bias):
-        rd = [a_] + ([bias] if isinstance(bias, dict) else [])
-        return op("s", lambda: g.scalar.activation(out["ap"], a_["ap"], func, bias=sc_(bias), scale=scale), rd, [out])
+        return op("s", lambda: g.scalar.activation(out["ap"], a_["ap"], func, bias=bias["ap"], scale=scale), [a_, bias], [out])
 
     def ms(out, val):
         return op("v", lambda: g.vector.memset(out["ap"], val), [], [out])
 
     def scan(out, a_, b_, init, o1, o2):
-        rd = [a_, b_] + ([init] if isinstance(init, dict) else [])
-        return op("v", lambda: g.vector.tensor_tensor_scan(out["ap"], a_["ap"], b_["ap"], sc_(init), o1, o2), rd, [out])
+        return op("v", lambda: g.vector.tensor_tensor_scan(out["ap"], a_["ap"], b_["ap"], init, o1, o2), [a_, b_], [out])
 
     def mm(out, lhs, rhs, start=True, stop=True):
         return op("p", lambda: g.tensor.matmul(out["ap"], lhs["ap"], rhs["ap"], start, stop), [lhs, rhs], [out])
@@ -192,6 +195,7 @@ def rank_program(g, core, T, topo):
         return op("g", lambda: g.iota(out["ap"], pat, base, cm), [], [out])
 
     def asel(out, a_, pat, cmp_, fill, base):
+        wait("g", ("qg", cnt["qg"], {}))
         return op("g", lambda: g.affine_select(out["ap"], a_["ap"], pat, cmp_, fill, base, 1), [a_], [out])
 
     def blkp(q):
@@ -206,156 +210,160 @@ def rank_program(g, core, T, topo):
     def turn(m):
         return c("agi", 32 * m, 32 * m + 128)
 
+    def lane(e):
+        return c("we", 15 - e, 143 - e)
+
     ne = len(engines((r + 1) % N))
     others = [(r + k) % N for k in (1, 2, 3)]
     for s in others:
-        lands(c("la", WA * s, WA * s + WA), "ara%d" % s, ne)
-        lands(c("lb", WB * s, WB * s + WB), "arb%d" % s, ne)
+        for name, w in WIDE.items():
+            lands(c("l" + name, w * s, w * s + w), "ar%s%d" % (name, s), ne)
         lands(ap("lc", s), "arc%d" % s, ne)
         lands(c("lo", 256 * s, 256 * s + 160), "arw%d" % s, ne)
         lands(c("lo", 256 * s + 160, 256 * s + 256), "aro%d" % s, ne)
     for t in range(1, TR):
         lands(c("nr", 24 * t, 24 * t + 24), "arn%d" % t, ne)
 
-    def pack(d, a_, b_, p=None):
-        k = others.index(d) if d != r else None
-        return c("la", WA * r + a_, WA * r + b_, p=p) if d == r else c("sa", WA * k + a_, WA * k + b_, p=p)
+    def pack(name, d, a_, b_, p=None):
+        o = WIDE[name] * others.index(d)
+        return c("s" + name, o + a_, o + b_, p=p)
 
-    dma("y", c("sab", 0, 40), ext(T.ra[:, :]), "ldab")
-    dma("y", c("sab", 40, 80), ext(T.rb[:, :]), "ldab")
-    for d in others + [r]:
-        rows = slice(32 * d, 32 * d + 32)
-        dma("s", pack(d, 0, 288, blkp(0)), ext(T.cin[rows, 0:288]), "lda%d" % d)
-        dma("y", pack(d, 0, 96, blkp(1)), ext(T.cin[rows, 288:384]), "lda%d" % d)
-        dma("s", pack(d, 96, 160, blkp(1)), ext(T.kin[rows, 576:640]), "lda%d" % d)
-        dma("y", pack(d, 0, 288, blkp(2)), ext(T.kin[rows, 0:288]), "lda%d" % d)
-        dma("s", pack(d, 0, 288, blkp(3)), ext(T.kin[rows, 288:576]), "lda%d" % d)
-    dma("y", c("si", 0, 384), ext(T.rx[:, :]), "ldi")
-    dma("y", c("sj", 0, 384), ext(T.ot[:, :]), "ldi")
+    def landed(name, s, a_, b_, u):
+        return c("l" + name, WIDE[name] * s + a_, WIDE[name] * s + b_, p=blkp(u))
+
+    def post(name, d):
+        w = WIDE[name]
+        send(d, c("l" + name, w * r, w * r + w), pack(name, d, 0, w), "ar%s%d" % (name, r))
+
+    def load(name, w, src, d):
+        for u in range(4):
+            dma("ys"[u % 2], pack(name, d, 0, w, blkp(u)), ext(src[32 * d:32 * d + 32, w * u:w * u + w]), "ld%s%d" % (name, d))
+
+    def take(name, w, s, buf, qs, scale=None):
+        for u in range(4):
+            cp(qs[u], c(buf, w * u, w * u + w, p=blkp(s)), landed(name, s, 0, w, u), scale)
+
+    for d in others:
+        load("a", 96, T.cin, d)
     dma("y", c("et", 0, 384), ext(T.ein[:, :]), "lde")
-    for k, d in enumerate(others):
-        dma("y", c("stau", 96 * k, 96 * k + 96), ext(T.tau[32 * d:32 * d + 32, :]), "ldb")
-    dma("y", ap("lc", r), ext(T.tau[32 * r:32 * r + 32, :]), "lco")
+    dma("s", c("sab", 0, 40), ext(T.ra[:, :]), "ldab")
+    dma("s", c("sab", 40, 80), ext(T.rb[:, :]), "ldab")
+    for d in others:
+        load("r", 160, T.kin, d)
+    dma("y", c("si", 0, 384), ext(T.rx[:, :]), "ldi")
+    dma("s", c("sj", 0, 384), ext(T.ot[:, :]), "ldi")
+    dma("y", c("cw", 0, 384, p=blkp(r)), ext(T.cin[32 * r:32 * r + 32, :]), "lda%d" % r)
+    dma("s", c("wt", 0, 640, p=blkp(r)), ext(T.kin[32 * r:32 * r + 32, :]), "ldr%d" % r)
 
     iota(c("ci", 0, 1), [[0, 1]], 0, 1, False)
     iota(c("io2", 0, 128), [[16, 8], [0, 16]], 0, 0)
     iota(c("iv", 0, 256), [[0, 2], [-1, 128]], 0, 1)
     iota(c("io2", 128, 144), [[1, 16]], 0, 0)
     iota(c("io2", 144, 184), [[16, 40]], 0, 1)
-    for d in others + [r]:
-        ms(pack(d, 240, 288, blkp(1)), 0.0)
-    ms(c("we", 0, 2048), 0.0)
+    for d in others:
+        post("a", d)
+
+    for d in others:
+        ms(pack("r", d, 160, 200, (64, 128)), 0.0)
+    ms(c("we", 0, 144), 0.0)
     ts(c("ci", 1, 2), c("ci", 0, 1), 112, A.bitwise_and)
     ts(c("ci", 2, 3), c("ci", 0, 1), 15, A.bitwise_and)
     cp("v", c("cf", 0, 3), c("ci", 0, 3))
     kg16, pmod = c("cf", 1, 2), c("cf", 2, 3)
-    ts(c("g8", 0, 8), c("io2", 0, 128, 16), kg16, A.is_equal)
+    ts(c("we", 15, 143, 16), c("io2", 0, 128, 16), kg16, A.is_equal)
     ts(c("agi", 0, 256), c("iv", 0, 256), 0.0, A.is_equal)
-    ts(c("sar", 0, 80), c("sab", 0, 80), float(SO * r), A.is_lt, float(N * SO), A.mult)
-    tt(c("sar", 80, 160), c("sar", 0, 80), c("sab", 0, 80), A.add)
-    for d in others + [r]:
-        ts(pack(d, 160, 240, blkp(1)), c("sar", 80, 160, p=blkp(d)), -float(SO * r), A.add)
-        if d != r:
-            send(d, c("la", WA * r, WA * r + WA), pack(d, 0, WA), "ara%d" % r)
-
-    for e in range(16):
-        cp("s", c("we", 128 * e + e, 128 * e + 128, 16), c("g8", 0, 8))
     ts(c("blk", 0, 128), c("io2", 0, 128), kg16, A.is_equal, 2.0 ** -9, A.mult)
     ts(c("trn0", 0, 128), c("io2", 0, 128), kg16, A.is_equal, -2.0 ** -9, A.mult)
     ms(c("mz", 0, 128), 0.0)
     cp("s", c("mt", 0, 128), c("agi", 0, 128), 2.0)
     tt(c("m0", 0, 128), c("mt", 0, 128), c("agi", 16, 144), A.add)
-    for k in range(3):
-        ms(c("sp", WB * k + 192, WB * k + WB), 0.0)
-    cp("s", c("dw", 0, 896), c("we", 0, 896), 0.0)
-    asel(c("trn", 0, 128), c("trn0", 0, 128), [[-1, 128]], A.is_ge, 0.0, 0)
-    asel(c("ma", 0, 128), c("mt", 0, 128), [[-32, 4], [1000, 2], [-1, 16]], A.not_equal, 1.0, -16)
-    asel(c("mb", 0, 128), c("mz", 0, 128), [[-32, 4], [-1000, 2], [-1, 16]], A.not_equal, 1.0, 1000)
-    asel(c("trn2", 0, 128), c("trn", 0, 128), [[-1, 128]], A.not_equal, -2.0, 0)
+    for o in range(0, 896, 224):
+        cp("s", c("dw", o, o + 224), c("iv", 0, 224), 0.0)
     cp("s", c("tz", 384, 768), c("dw", 0, 384))
+    ts(c("j40", 0, 40), c("io2", 144, 184), kg16, A.subtract)
+    ts(c("idg", 0, 16), c("io2", 128, 144), pmod, A.is_equal, -1.0, A.mult)
+    ms(c("one", 0, 40), 1.0)
+    ms(c("cf", 4, 5), -(0.125 * LIFT - 2.0 ** -7) * 2.0 ** 25)
+    ms(c("cf", 5, 6), 0.125 * LIFT)
+    ts(c("dump", 0, 24), c("j40", 0, 24), 4096.0, A.add)
 
-    def late_constants():
-        ts(c("j40", 0, 40), c("io2", 144, 184), kg16, A.subtract)
-        ts(c("idg", 0, 16), c("io2", 128, 144), pmod, A.is_equal, -1.0, A.mult)
-        ms(c("one", 0, 40), 1.0)
-        ms(c("cf", 4, 5), -(0.125 * LIFT - 2.0 ** -7) * 2.0 ** 25)
-        ms(c("cf", 5, 6), 0.125 * LIFT)
-        ts(c("dump", 0, 24), c("j40", 0, 24), 4096.0, A.add)
-        for t in range(TR):
-            ts(c("k2", 30 * t, 24 * t + 24), c("j40", 6 * t, 24), -1.0, A.mult, 511.0 + 96.0 * t, A.add)
-            if t:
-                ts(c("k2", 24 * t, 30 * t), c("j40", 0, 6 * t), -1.0, A.mult, 127.0 + 96.0 * t, A.add)
+    def order_of(t):
+        ts(c("k2", 30 * t, 24 * t + 24), c("j40", 6 * t, 24), -1.0, A.mult, 511.0 + 96.0 * t, A.add)
+        if t:
+            ts(c("k2", 24 * t, 30 * t), c("j40", 0, 6 * t), -1.0, A.mult, 127.0 + 96.0 * t, A.add)
 
-    def take_a(s):
-        o = WA * s
-        cp("v", c("kab", 640, 720, p=blkp(s)), c("la", o + 160, o + 240, p=blkp(1)))
-        cp("v", c("kab", 576, 640, p=blkp(s)), c("la", o + 96, o + 160, p=blkp(1)), KUP)
-        for y in range(N):
-            m = (s - y) % N
-            cp("vs"[y % 2], c("cw", 384 * m, 384 * m + 288, p=blkp(y)), c("la", o, o + 288, p=blkp(0)))
-            cp("s" if y < 3 else "v", c("cw", 384 * m + 288, 384 * m + 384, p=blkp(y)), c("la", o, o + 96, p=blkp(1)))
-        if s == others[0]:
-            cp("v", c("ab16", 0, 80), c("kab", 640, 720))
-        cp("s", c("kab", 0, 288, p=blkp(s)), c("la", o, o + 288, p=blkp(2)), KUP)
-        cp("v", c("kab", 288, 576, p=blkp(s)), c("la", o, o + 288, p=blkp(3)), KUP)
-
-    def take_lists(q, s):
-        cp(q, c("ll", 8, 32, p=blkp(s)), c("lb", WB * s + 192, WB * s + WB, p=blkp(0)))
+    order_of(0)
+    ms(c("lst", S0, S0 + 256), 0)
+    ts(c("ind", 0, 384), c("et", 0, 384), 0.125, A.is_ge)
+    for e in range(16):
+        mm(bank(4, 0, 24), lane(e), c("ind", e, 384, 16), e == 0, e == 15)
+    ts(c("sar", 0, 80), c("sab", 0, 80), float(SO * r), A.is_lt, float(N * SO), A.mult)
+    ms(c("msk", 0, 1280), 1.0)
+    cp("v", c("nw", 0, 24), bank(4, 0, 24))
+    mm(bank(5, 0, 24), c("m0", 0, 128), c("nw", 0, 24))
+    tt(c("sar", 80, 160), c("sar", 0, 80), c("sab", 0, 80), A.add)
+    for d in others:
+        ts(pack("r", d, 160, 184, blkp(2)), c("ps", 2560, 2584, p=blkp(d)), 23.5, A.is_ge, 512.0, A.mult)
         for h in range(2):
-            cp(q, c("pk", 192 * h, 192 * h + 192, p=blkp(s)), c("lb", WB * s, WB * s + 192, p=blkp(h)))
-
-    def take_e(q, s):
+            ts(pack("r", d, 160, 200, blkp(h)), c("sar", 80 + 40 * h, 120 + 40 * h, p=blkp(d)), -float(SO * r), A.add)
+        post("r", d)
+    ms(c("msk", 0, 1280, 16), 0.0)
+    ts(c("kab", 640, 720, p=blkp(r)), c("sar", 80, 160, p=blkp(r)), -float(SO * r), A.add)
+    ts(c("ll", 8, 32, p=blkp(r)), c("ps", 2560, 2584, p=blkp(r)), 23.5, A.is_ge, 512.0, A.mult)
+    for d in others:
         for h in range(2):
-            cp(q, c("ea", 4096 + 192 * h, 4288 + 192 * h, p=blkp(s)), c("lb", WB * s, WB * s + 192, p=blkp(2 + h)))
-
-    take_a(r)
+            cp("s", pack("b", d, 0, 192, blkp(2 + h)), c("et", 192 * h, 192 * h + 192, p=blkp(d)), LIFT)
     cp("s", c("ea", 4096, 4480, p=blkp(r)), c("et", 0, 384, p=blkp(r)), LIFT)
-    for k, d in enumerate(others):
-        for h in range(2):
-            cp("s", c("sp", WB * k, WB * k + 192, p=blkp(2 + h)), c("et", 192 * h, 192 * h + 192, p=blkp(d)), LIFT)
+    cp("s", c("kab", 0, 640, p=blkp(r)), c("wt", 0, 640, p=blkp(r)), KUP)
     ts(bank(0, 0, 384), c("si", 0, 384), 4096.0, A.mult, -4096.0 * RO * r - SO * r, A.add)
     ts(bank(1, 0, 384), c("si", 0, 384), float(RO * r), A.is_lt, 4096.0 * N * RO, A.mult)
     ts(bank(2, 0, 384), c("sj", 0, 384), float(SO * r), A.is_lt, float(N * SO), A.mult)
-    ts(c("ind", 0, 384), c("et", 0, 384), 0.125, A.is_ge)
-    for e in range(16):
-        mm(bank(4, 0, 24), c("we", 128 * e, 128 * e + 128), c("ind", e, 384, 16), e == 0, e == 15)
     tt(c("sk", 0, 384), c("sj", 0, 384), bank(0, 0, 384), A.add)
-    cp("v", c("nw", 0, 24), bank(4, 0, 24))
-    mm(bank(5, 0, 24), c("m0", 0, 128), c("nw", 0, 24))
-    tt(c("sb", 0, 384), c("sk", 0, 384), bank(1, 0, 384), A.add)
+    wait("y", ("qv", cnt["qv"], {}))
     for k, d in enumerate(others):
-        ts(c("sp", WB * k + 192, WB * k + WB, p=blkp(0)), c("ps", 2560, 2584, p=blkp(d)), 23.5, A.is_ge, 512.0, A.mult)
-    tt(c("sk", 0, 384), c("sb", 0, 384), bank(2, 0, 384), A.add)
-    for k, d in enumerate(others):
+        dma("y", c("stau", 96 * k, 96 * k + 96), ext(T.tau[32 * d:32 * d + 32, :]), "ldb")
+    dma("y", ap("lc", r), ext(T.tau[32 * r:32 * r + 32, :]), "lco")
+    for s in others[::-1]:
+        take("a", 96, s, "cw", "ssss")
+    tt(c("sl", 0, 384), c("sk", 0, 384), bank(1, 0, 384), A.add)
+    for m in (1, 2, 3):
+        mm(bank(4 + m, 0, 384), turn(m), c("cw", 0, 384))
+    tt(c("sk", 0, 384), c("sl", 0, 384), bank(2, 0, 384), A.add)
+    for d in others:
         for h in range(2):
-            cp("vs"[h], c("sp", WB * k, WB * k + 192, p=blkp(h)), c("sk", 192 * h, 192 * h + 192, p=blkp(d)))
-        send(d, c("lb", WB * r, WB * r + WB), c("sp", WB * k, WB * k + WB), "arb%d" % r)
+            cp("v", pack("b", d, 0, 192, blkp(h)), c("sk", 192 * h, 192 * h + 192, p=blkp(d)))
+        post("b", d)
+    cp("v", c("pk", 0, 384, p=blkp(r)), c("sk", 0, 384, p=blkp(r)))
+    for m in (1, 2, 3):
+        cp("s", c("cw", 384 * m, 384 * m + 384), bank(4 + m, 0, 384))
+    asel(c("trn", 0, 128), c("trn0", 0, 128), [[-1, 128]], A.is_ge, 0.0, 0)
     for k, d in enumerate(others):
         send(d, ap("lc", r), c("stau", 96 * k, 96 * k + 96), "arc%d" % r)
-    iota(c("lst", 0, 896), [[0, 896]], 0, 0, False)
-    ts(c("ll", 8, 32, p=blkp(r)), c("ps", 2560, 2584, p=blkp(r)), 23.5, A.is_ge, 512.0, A.mult)
-    cp("s", c("pk", 0, 384, p=blkp(r)), c("sk", 0, 384, p=blkp(r)))
-    late_constants()
     for s in others[::-1]:
-        take_a(s)
-        if s == others[2]:
-            ms(c("msk", 0, 1280), 1.0)
-        if s == others[1]:
-            ms(c("msk", 0, 1280, 16), 0.0)
+        for h in range(2):
+            cp("v", c("kab", 640 + 40 * h, 680 + 40 * h, p=blkp(s)), landed("r", s, 160, 200, h))
+        cp("v", c("ll", 8, 32, p=blkp(s)), landed("r", s, 160, 184, 2))
+        if s == others[0]:
+            cp("v", c("ab16", 0, 80), c("kab", 640, 720))
+        take("r", 160, s, "kab", "vsvs" if s == others[0] else "vvvv", KUP)
+
+    def take_b(q, s, buf, base, u):
+        for h in range(2):
+            cp(q, c(buf, base + 192 * h, base + 192 * h + 192, p=blkp(s)), landed("b", s, 0, 192, u + h))
+
+    def swap(q, buf, a_, to, width, h):
+        cp(q, c(buf, to, to + width, p=(64 * h, 64 * h + 64)), c(buf, a_, a_ + width, p=(64 - 64 * h, 128 - 64 * h)))
 
     def turn_half(q, buf, base, width, h):
-        out, in_ = c(buf, base + 2 * width, base + 3 * width, p=(64 * h, 64 * h + 64)), c(buf, base, base + width, p=(64 - 64 * h, 128 - 64 * h))
-        if q == "g":
-            wait("g", ("qg", cnt["qg"], {}))
-            asel(out, in_, [[0, width]], A.is_ge, 0.0, 0)
-        else:
-            cp(q, out, in_)
+        swap(q, buf, base, base + 2 * width, width, h)
 
     def turn_dma(buf, base, width, sem):
-        for m in (1, 2, 3):
+        for m in (1, 3):
             o = base + m * width
             dma("y", c(buf, o, o + width, p=(0, 128 - 32 * m)), c(buf, base, base + width, p=(32 * m, 128)), sem)
             dma("y", c(buf, o, o + width, p=(128 - 32 * m, 128)), c(buf, base, base + width, p=(0, 32 * m)), sem)
+        for h in range(2):
+            turn_half("g", buf, base, width, h)
 
     def e_window(buf, ms_=(1, 2, 3)):
         for m in ms_:
@@ -365,20 +373,26 @@ def rank_program(g, core, T, topo):
         for m in ms_:
             cp("s", c(buf, 4096 + 384 * m, 4480 + 384 * m), bank(4 + m, 0, 384))
 
-    def w_window(between=None):
-        parts = [(m, h) for h in (0, 320) for m in (1, 3)]
+    def w_window(q):
+        parts = [(1, 0), (1, 320), (3, 320)] + ([(3, 0)] if q == "v" else [])
         for b, (m, h) in enumerate(parts):
             mm(bank(b, 128, 320), turn(m), c("wm", h, h + 320))
-            if between and b == 0:
-                between()
-        turn_half("g", "wm", 0, 640, 0)
-        turn_half("s", "wm", 0, 640, 1)
+        for h, n in ((0, 320), (320, 320)) if q == "g" else ((0, 640),):
+            swap(q, "wm", h, 1280 + h, n, 0)
+        swap("s", "wm", 0, 1280, 640, 1)
         for b, (m, h) in enumerate(parts):
             cp("s", c("wm", 640 * m + h, 640 * m + h + 320), bank(b, 128, 320))
+            if b == 0 and q == "g":
+                swap("g", "wm", 640, 1920, 320, 0)
+                swap("s", "wm", 640, 1920, 320, 1)
 
-    def new_rates(out):
-        tt(c("wt", 0, 640), ind(c("cw", 0, 1536), c("ab16", 0, 40)), c("kab", 0, 640), A.mult)
-        cp("s", c("cb", 0, 640), ind(c("cw", 0, 1536), c("ab16", 40, 80)), 1.0 / KUP)
+    def new_rates(out, t):
+        if t == 0:
+            tt(c("wt", 0, 640), ind(c("cw", 0, 1536), c("ab16", 0, 40)), c("kab", 0, 640), A.mult)
+            cp("s", c("cb", 0, 640), ind(c("cw", 0, 1536), c("ab16", 40, 80)), 1.0 / KUP)
+        else:
+            scan(c("wt", 0, 640), c("ca", 0, 640), c("kab", 0, 640), 8.0, A.min, A.mult)
+            order_of(t)
         scan(out, c("cb", 0, 640), c("wt", 0, 640), 1.0, A.min, A.mult)
 
     def products(e_, a_, b_, hy):
@@ -407,6 +421,10 @@ def rank_program(g, core, T, topo):
         p, q_ = 6 * t, 10 * t
         pos = bank(4, 256, 24)
 
+        def counts():
+            scan(c("css", 0, 24), c("ll", 8 + p, 32 + p), c("one", 0, 24), 0.0, A.add, A.mult)
+            tt(sm(0), lw, c("k2", 24 * t, 24 * t + 24), A.max)
+
         def places():
             mm(pos, c("trn", 0, 128), lw, True, False)
             mm(bank(4, 256 + p, 24 - p), c("blk", 0, 128), c("css", 0, 24 - p), False, False)
@@ -421,52 +439,53 @@ def rank_program(g, core, T, topo):
         if t:
             tt(c("ind", 0, 384), ind(c("eb", 0, 4480), c("pe16", 0, 24)), c("thr", 0, 384), A.is_ge)
             for e in range(16):
-                mm(bank(4, 0, 24), c("we", 128 * e, 128 * e + 128), c("ind", e, 384, 16), e == 0, e == 15)
+                mm(bank(4, 0, 24), lane(e), c("ind", e, 384, 16), e == 0, e == 15)
             spread("eb", "ea")
-            cp("v", nw, bank(4, 0, 24))
+            cp("s" if t > 1 else "v", nw, bank(4, 0, 24))
             send((r - 1) % N, nr, nw, "arn%d" % t)
-            e_window("ea")
-            new_rates(c(wo, 0, 640))
-            e_out("ea")
-            for m in (0, 1, 2, 3, -1):
-                x = 32 * max(m, 0)
-                mm(bank(4, 64 + 24 * m, 24), c("ma", x, x + 128), nw, True, False)
-                mm(bank(4, 64 + 24 * m, 24), c("mb", x, x + 128), nr, False, True)
+            e_window("ea", (1, 3))
+            turn_half("g", "ea", 4096, 384, 0)
+            turn_half("s", "ea", 4096, 384, 1)
+            new_rates(c(wo, 0, 640), t)
+            if t == 1:
+                cp("v", c("abd16", 40, 70), c("abt", 0, 30))
+                cp("v", c("abd16", 80, 120), c("abt", 40, 80))
+                cp("v", c("abd16", 120, 150), c("abt", 40, 70))
+            e_out("ea", (1, 3))
+            for k, (sel, n_) in enumerate((("ma", nw), ("mb", nr))):
+                for m in (0, 1, 2, 3, -1):
+                    x = 32 * max(m, 0)
+                    mm(bank(4, 64 + 24 * m, 24), c(sel, x, x + 128), n_, k == 0 and m == 0, k == 1 and m == -1)
             ts(c("ll", 8, 128), bank(4, 40, 120), 23.5, A.is_ge, 512.0, A.mult)
             cp("s", c("xb", 0, 640), ind(c("ll", 32, 128), c("abd16", 80 + q_, 120 + q_)))
             tt(c("xab", 0, 640), ind(c("ll", 32, 128), c("abd16", q_, 40 + q_)), c("oh", 16 * q_, 16 * q_ + 640), A.mult)
+            counts()
             scan(c("xab", 640, 1280), c("xb", 0, 640), c("oh", 1120 + 16 * q_, 1760 + 16 * q_), 0.0, A.max, A.mult)
             for x in range(32):
                 o = 640 * (x // 16)
-                mm(bank(3, 0, 40), c("we", 128 * (x % 16), 128 * (x % 16) + 128), c("xab", o + x % 16, o + 640, 16), x == 0, x == 31)
-        else:
-            new_rates(c(wn, 640, 1280))
-            for s in others[:0:-1]:
-                take_lists("s", s)
-                take_e("s", s)
-            ts(c("wm", 0, 640), c(wn, 640, 1280), 1.0, A.min)
-            take_lists("v", others[0])
-        scan(c("css", 0, 24), c("ll", 8 + p, 32 + p), c("one", 0, 24), 0.0, A.add, A.mult)
-        tt(sm(0), lw, c("k2", 24 * t, 24 * t + 24), A.max)
-        if t:
-            places()
-            ts(c("act", 0, 40), bank(3, 0, 40), -0.5, A.is_le, 512.0, A.mult)
+                if x == 16:
+                    places()
+                mm(bank(3, 0, 40), lane(x % 16), c("xab", o + x % 16, o + 640, 16), x == 0, x == 31)
             cp("v", c("pos16", 0, 24), pos)
+            in_picks()
+            ts(c("act", 0, 40), bank(3, 0, 40), -0.5, A.is_le, 512.0, A.mult)
+            ts(sm(4), sm(3), 16384.0, A.is_ge, 16384.0, A.mult)
             scan(c("csr", 0, 40), c("act", 0, 40), c("one", 0, 40), 0.0, A.add, A.mult)
             for o, a_, n in ((q_, 0, 40 - q_), (0, 40 - q_, q_)):
                 mm(bank(3, 64 + o, n), c("trn2", 0, 128), c("act", a_, a_ + n), True, False)
                 mm(bank(3, 64 + o, n), c("blk", 0, 128), c("csr", a_, a_ + n), False, True)
-            in_picks()
-            ts(sm(8, 40), bank(3, 64, 40), -640.0, A.is_gt, 640.0, A.mult)
-            ts(sm(4), sm(3), 16384.0, A.is_ge, 16384.0, A.mult)
-            tt(sm(9, 40), sm(8, 40), c("j40", 0, 40), A.add)
             ts(sm(7), sm(3), 16384.0, A.is_ge, 384.0, A.mult)
-            cp("v", c("wo16", 0, 40), sm(9, 40))
             tt(sm(5), sm(4), sm(1), A.add)
+            tt(sm(2), sm(7), c("j40", 0, 24), A.add)
+            ts(sm(8, 40), bank(3, 64, 40), -640.0, A.is_gt, 640.0, A.mult)
+            tt(sm(6), sm(5), c("dump", 0, 24), A.min)
+            tt(sm(9, 40), sm(8, 40), c("j40", 0, 40), A.add)
+            cp("v", c("tz16", 0, 24), sm(2))
+            cp("v", c("wo16", 0, 40), sm(9, 40))
             for h in (0, 20):
                 ts(c("wm", 16 * h, 16 * h + 320), ind(c(wo, 0, 1280), c("wo16", h, h + 20)), 1.0, A.min)
             cp("s", c(wn, 640, 1280), ind(c(wo, 0, 1280), c("wo16", 0, 40)))
-            w_window()
+            w_window("g")
             turn_dma(wn, 640, 640, "wr%d" % t)
             if t == TR - 1:
                 for k, d in enumerate(others):
@@ -477,71 +496,88 @@ def rank_program(g, core, T, topo):
                 for s in others[::-1]:
                     dma("y", ext(T.yw[32 * s:32 * s + 32, :]), c("lo", 256 * s, 256 * s + 160), "st")
         else:
-            take_e("v", others[0])
-            w_window(places)
-            e_window("ea", (1, 3))
-            turn_dma(wn, 640, 640, "wr%d" % t)
-            dma("y", c("tau_o", 0, 384), ap("lc"), "lbt")
+            counts()
+            places()
+            new_rates(c(wn, 640, 1280), t)
+            take_b("s", others[2], "pk", 0, 0)
+            take_b("s", others[1], "pk", 0, 0)
             cp("v", c("pos16", 0, 24), pos)
+            ts(c("wm", 0, 640), c(wn, 640, 1280), 1.0, A.min)
             in_picks()
-        cp("v", ind(c("lst", 0, 896), c("pos16", 0, 24)), c("pk", 0, 384))
-        if t == 0:
+            take_b("g", others[2], "ea", 4096, 2)
+            w_window("v")
+            take_b("g", others[1], "ea", 4096, 2)
             ts(sm(4), sm(3), 16384.0, A.is_ge, 16384.0, A.mult)
             ts(sm(7), sm(3), 16384.0, A.is_ge, 384.0, A.mult)
             tt(sm(5), sm(4), sm(1), A.add)
-        tt(sm(2), sm(7), c("j40", 0, 24), A.add)
-        tt(sm(6), sm(5), c("dump", 0, 24), A.min)
-        ts(c("rx16", 0, 256), c("lst", S0, S0 + 256), 2.0 ** -12, A.mult)
-        ts(c("lo_i", 0, 256), c("lst", S0, S0 + 256), 4095, A.bitwise_and)
-        cp("v", c("tz16", 0, 24), sm(2))
-        cp("v", c("ot16", 0, 256), c("lo_i", 0, 256))
-        cp("v", c("pe16", 0, 24), sm(6))
+            take_b("g", others[0], "ea", 4096, 2)
+            take_b("v", others[0], "pk", 0, 0)
+            e_window("ea", (1, 3))
+            turn_half("g", "ea", 4096, 384, 0)
+            turn_dma(wn, 640, 640, "wr%d" % t)
+            dma("y", c("tau_o", 0, 384), ap("lc"), "lbt")
+        cp("v", ind(c("lst", 0, 896), c("pos16", 0, 24)), c("pk", 0, 384))
         if t == 0:
+            tt(sm(2), sm(7), c("j40", 0, 24), A.add)
+            tt(sm(6), sm(5), c("dump", 0, 24), A.min)
+        ts(c("lo_i", 0, 256), c("lst", S0, S0 + 256), 4095, A.bitwise_and)
+        ts(c("rx16", 0, 256), c("lst", S0, S0 + 256), 2.0 ** -12, A.mult)
+        if t == 0:
+            cp("v", c("tz16", 0, 24), sm(2))
+        cp("v", c("ot16", 0, 256), c("lo_i", 0, 256))
+        if t == 0:
+            turn_half("s", "ea", 4096, 384, 1)
             e_out("ea", (1, 3))
         for a_, b_ in CH1[1:]:
             cp("s", c("wg", 16 * a_, 16 * b_), ind(c("wm", 0, 2560), c("rx16", a_, b_)))
-        if t:
-            least()
         for a_, b_ in XCH:
             cp("s", c("xg", 16 * a_, 16 * b_), ind(c(wn, 640, 3200), c("rx16", 80 + a_, 80 + b_)), 0.125)
-            mm(c("ps", 8 * a_, 8 * b_), turn(0), c("xg", 16 * a_ + 1, 16 * b_, 2))
+            for e in ((0, 1) if a_ < NA else ()):
+                mm(c("ps", 4 * a_, 4 * b_), turn(0), c("xg", 16 * a_ + e, 16 * b_, 4), e == 0, e == 1)
+            for e in (2, 3):
+                mm(c("ps", 1536 + 4 * a_, 1536 + 4 * b_), turn(0), c("xg", 16 * a_ + e, 16 * b_, 4), e == 2, e == 3)
         if t == 0:
             cp("s", c("tz", 0, 384), c("tau_o", 0, 384), LIFT)
-            least()
-            turn_half("v", "ea", 4096, 384, 0)
-            turn_half("v", "ea", 4096, 384, 1)
+        least()
+        cp("s", bank(1, 0, 704 - 4 * NA), c("xg", 16 * NA + 1, 2816, 4))
+        cp("s", c("y1", 0, 4 * NA), bank(0, 0, 4 * NA))
         cp("v", c("wg", 0, 16 * CH1[0][1]), ind(c("wm", 0, 2560), c("rx16", *CH1[0])))
+        cp("v", c("pe16", 0, 24), sm(6))
         products("ea", *CH1[0], 256)
         for x in range(1, len(CH1)):
             products("ea", *CH1[x], 256)
             maxima("ea", *CH1[x - 1])
         maxima("ea", *CH1[-1])
         spread("ea", "eb")
-        e_window("eb")
-        e_out("eb")
-        for a_, b_ in CH2[1:]:
-            cp("s", c("eg", 16 * (a_ - HY), 16 * (b_ - HY)), ind(c("eb", 4096, 5632), c("ot16", a_, b_)))
-        if t < TR - 1:
-            bound()
-        tt(c("y1", 0, 704), c("xg", 0, 2816, 4), c("ps", 0, 1408, 2), A.add)
-        tt(c("ps", 1536, 2240), c("xg", 2, 2816, 4), c("ps", 1, 1408, 2), A.add)
+        e_window("eb", (1, 3))
+        turn_half("g", "eb", 4096, 384, 0)
+        turn_half("s", "eb", 4096, 384, 1)
+        e_out("eb", (1, 3))
+        tt(c("y1", 4 * NA, 704), c("xg", 16 * NA, 2816, 4), bank(1, 0, 704 - 4 * NA), A.add)
         if t == 0:
             cp("v", c("abi", 0, 80), c("kab", 640, 720))
         tt(c("z1", 0, 352), c("y1", 0, 704, 2), c("ps", 1536, 2240, 2), A.add)
         tt(bank(0, 0, 352), c("y1", 1, 704, 2), c("ps", 1537, 2240, 2), A.add)
         if t == 0:
-            ts(c("abt", 0, 80), c("abi", 0, 80), 4, A.arith_shift_right)
             ts(c("abt", 80, 160), c("abi", 0, 80), 15, A.bitwise_and)
         tt(c("p1", 0, 176), c("z1", 0, 352, 2), c("ps", 0, 352, 2), A.add)
         tt(bank(1, 0, 176), c("z1", 1, 352, 2), c("ps", 1, 352, 2), A.add)
         if t == 0:
             cp("v", c("abm16", 0, 80), c("abt", 80, 160))
-        products("eb", *CH2[0], HY)
         tt(c("dw", 512, 688), c("p1", 0, 176), bank(1, 0, 176), A.subtract)
+        cp("s", c("ct", 0, 384), ind(c("dw", 0, 896), c("pos16", 0, 24)))
+        mm(bank(2, 0, 384), turn(0), c("cw", 0, 384), True, False)
+        mm(bank(2, 0, 384), turn(0), c("ct", 0, 384), False, True)
+        for a_, b_ in CH2[1:]:
+            cp("s", c("eg", 16 * (a_ - HY), 16 * (b_ - HY)), ind(c("eb", 4096, 5632), c("ot16", a_, b_)))
+        if t < TR - 1:
+            bound()
+        products("eb", *CH2[0], HY)
+        if t == 0:
+            ts(c("abt", 0, 80), c("abi", 0, 80), 4, A.arith_shift_right)
         maxima("eb", *CH2[0])
-        tt(c("ct", 0, 384), ind(c("dw", 0, 896), c("pos16", 0, 24)), c("cw", 0, 384), A.add)
         products("eb", *CH2[1], HY)
-        ts(c("cw", 0, 384), c("ct", 0, 384), 0.125, A.max, 8.0, A.min)
+        ts(c("cw", 0, 384), bank(2, 0, 384), 0.125, A.max, 8.0, A.min)
         if t < TR - 1:
             turn_dma("cw", 0, 384, "cg%d" % t)
         else:
@@ -555,15 +591,21 @@ def rank_program(g, core, T, topo):
         for x in range(2, len(CH2)):
             products("eb", *CH2[x], HY)
             maxima("eb", *CH2[x - 1])
+        if t < TR - 1:
+            cp("s", c("ca", 0, 640), ind(c("cw", 0, 1536), c("ab16", 0, 40)))
+            cp("s", c("cb", 0, 640), ind(c("cw", 0, 1536), c("ab16", 40, 80)), 1.0 / KUP)
         if t == 0:
+            asel(c("ma", 0, 128), c("mt", 0, 128), [[-32, 4], [1000, 2], [-1, 16]], A.not_equal, 1.0, -16)
+            asel(c("mb", 0, 128), c("mz", 0, 128), [[-32, 4], [-1000, 2], [-1, 16]], A.not_equal, 1.0, 1000)
+            asel(c("trn2", 0, 128), c("trn", 0, 128), [[-1, 128]], A.not_equal, -2.0, 0)
             cp("s", c("ma", 128, 224), c("ma", 0, 96))
             cp("s", c("mb", 128, 224), c("mb", 0, 96))
             for h in range(2):
-                cp("v", c("abd16", 80 * h, 80 * h + 40), c("abt", 40 * h, 40 * h + 40))
-                cp("v", c("abd16", 80 * h + 40, 80 * h + 70), c("abt", 40 * h, 40 * h + 30))
                 cp("s", c("oh", 1120 * h, 1120 * h + 640), ind(c("idg", 0, 16), c("abm16", 40 * h, 40 * h + 40)))
                 cp("s", c("oh", 1120 * h + 640, 1120 * h + 1120), c("oh", 1120 * h, 1120 * h + 480))
         maxima("eb", *CH2[-1])
+        if t == 0:
+            cp("v", c("abd16", 0, 40), c("abt", 0, 40))
     spread("eb", "ea")
 
     for k, d in enumerate(others):

from concourse.mybir import AluOpType, ActivationFunctionType

N, SO, RO, TR = 4, 384, 640, 4
CH1 = [(0, 32), (32, 96), (96, 176), (176, 256)]
CH2 = [(0, 72), (72, 128), (128, 192), (192, 256)]
NA = 64
HY = 72
XCH = [(0, 64), (64, 128), (128, 176)]
LIFT = 2.0 ** 20
KUP = 2.0 ** 15
S0 = 432
WIDE = {"a": 96, "r": 200, "b": 192}
F, B, I, U = "float32", "bfloat16", "int32", "uint16"
SCRATCH = {
    "ps": ("psum", [128, 4096], F),
    "sa": ("sbuf", [128, 3 * 96], F), "la": ("sbuf", [128, 4 * 96], F), "sr": ("sbuf", [128, 3 * 200], F), "lr": ("sbuf", [128, 4 * 200], F),
    "sb": ("sbuf", [128, 3 * 192], F), "lb": ("sbuf", [128, 4 * 192], F), "stau": ("sbuf", [128, 288], F), "lc": ("dram", [4, 128, 96], F),
    "sab": ("sbuf", [128, 80], I), "sar": ("sbuf", [128, 160], F), "si": ("sbuf", [128, 384], I), "sj": ("sbuf", [128, 384], I),
    "sk": ("sbuf", [128, 384], F), "sl": ("sbuf", [128, 384], F),
    "ea": ("sbuf", [128, 5632], F), "eb": ("sbuf", [128, 5632], F), "cw": ("sbuf", [128, 1536], F), "wm": ("sbuf", [128, 2560], F),
    "w0": ("sbuf", [128, 3200], F), "w1": ("sbuf", [128, 3200], F),
    "kab": ("sbuf", [128, 720], F), "tau_o": ("sbuf", [128, 384], F), "pk": ("sbuf", [128, 384], F), "ct": ("sbuf", [128, 384], F),
    "wt": ("sbuf", [128, 640], F), "ca": ("sbuf", [128, 640], F), "cb": ("sbuf", [128, 640], F), "et": ("sbuf", [128, 384], F), "thr": ("sbuf", [128, 384], F),
    "dw": ("sbuf", [128, 896], F), "tz": ("sbuf", [128, 768], F), "taum": ("sbuf", [128, 384], F), "lst": ("sbuf", [128, 896], I),
    "lo_i": ("sbuf", [128, 256], I), "rx16": ("sbuf", [128, 256], U), "ot16": ("sbuf", [128, 256], U),
    "wg": ("sbuf", [128, 4096], F), "prod": ("sbuf", [128, 4096], F), "msk": ("sbuf", [128, 1280], B), "eg": ("sbuf", [128, 16 * (256 - HY)], F),
    "pe16": ("sbuf", [128, 24], U), "tz16": ("sbuf", [128, 24], U), "mz": ("sbuf", [128, 128], B), "m0": ("sbuf", [128, 128], B),
    "xg": ("sbuf", [128, 2816], F), "y1": ("sbuf", [128, 704], F), "z1": ("sbuf", [128, 352], F), "p1": ("sbuf", [128, 176], F),
    "ind": ("sbuf", [128, 384], B), "nw": ("sbuf", [128, 96], B), "nr": ("sbuf", [128, 96], B), "ll": ("sbuf", [128, 128], B),
    "xab": ("sbuf", [128, 1280], B), "xb": ("sbuf", [128, 640], B), "oh": ("sbuf", [128, 2240], B), "act": ("sbuf", [128, 40], B),
    "csr": ("sbuf", [128, 40], B), "css": ("sbuf", [128, 24], B), "sm": ("sbuf", [128, 10, 40], F), "wo16": ("sbuf", [128, 40], U),
    "pos16": ("sbuf", [128, 24], U), "abi": ("sbuf", [128, 80], I), "abt": ("sbuf", [128, 160], I), "ab16": ("sbuf", [128, 80], U),
    "abd16": ("sbuf", [128, 160], U), "abm16": ("sbuf", [128, 80], U),
    "iv": ("sbuf", [128, 256], F), "agi": ("sbuf", [128, 256], F), "ma": ("sbuf", [128, 224], B), "mb": ("sbuf", [128, 224], B), "mt": ("sbuf", [128, 128], B),
    "we": ("sbuf", [128, 144], B), "blk": ("sbuf", [128, 128], B), "trn": ("sbuf", [128, 128], B), "trn2": ("sbuf", [128, 128], B), "trn0": ("sbuf", [128, 128], B),
    "ci": ("sbuf", [128, 4], I), "cf": ("sbuf", [128, 8], F), "io2": ("sbuf", [128, 200], F), "idg": ("sbuf", [128, 16], F),
    "j40": ("sbuf", [128, 40], F), "dump": ("sbuf", [128, 24], F), "k2": ("sbuf", [128, 96], F), "one": ("sbuf", [128, 40], B),
    "so": ("sbuf", [128, 3 * 256], F), "lo": ("sbuf", [128, 4 * 256], F), "se": ("sbuf", [128, 3 * 96], F), "le": ("sbuf", [128, 4 * 96], F),
}
SEMAPHORES = (["qv", "qs", "qp", "qg", "rl", "lco", "lbt", "ldb", "ldi", "ldab", "lde", "st"]
              + ["%s%d" % (n, k) for n in ("lda", "ldr", "ara", "arr", "arb", "arc", "arn", "aro", "arw", "are", "pko", "pkc", "wr", "cg")
                 for k in range(4)])
SHAPES = {n: v[1] for n, v in SCRATCH.items()}
A = AluOpType
ACT = ActivationFunctionType


def rank_program(g, core, T, topo):
    r = T.rank_of(core)
    if r is None:
        return
    Q = {"g": g, "v": g.vector, "s": g.scalar, "p": g.tensor, "y": g.sync}
    cnt = {"qv": 0, "qs": 0, "qp": 0, "qg": 0}
    known = {q: {} for q in Q}
    log = {}

    def ap(name, *idx):
        shape = SHAPES[name]
        idx = list(idx) + [slice(None)] * (len(shape) - len(idx))
        lo, hi, stride, rng = 0, 0, 1, []
        for k in range(len(shape) - 1, -1, -1):
            ix = idx[k]
            rr = range(shape[k])[ix] if isinstance(ix, slice) else range(ix, ix + 1)
            if k == 0:
                rng = [rr[0], rr[-1] + 1]
            else:
                lo += rr[0] * stride
                hi += rr[-1] * stride
                stride *= shape[k]
        if name == "ps":
            reg = (name, 0, 128, lo // 512 * 512, hi // 512 * 512 + 512, (lo, hi + 1))
        elif SCRATCH[name][0] == "dram":
            reg = (name, rng[0], rng[1], 0, 1, (0, 1))
        else:
            reg = (name, rng[0], rng[1], lo, hi + 1, (lo, hi + 1))
        return {"ap": T[name][tuple(idx)], "regs": [reg], "offs": []}

    def c(name, a, b, step=None, p=None):
        ps_ = slice(None) if p is None else slice(p[0], p[1])
        return ap(name, ps_, slice(a, b, step))

    def ind(win, off):
        return {"ap": win["ap"].indirect(off["ap"]), "regs": win["regs"], "offs": off["regs"]}

    def wait(q, tok):
        sem, val, clock = tok
        if val is None:
            val = cnt[sem]
        if known[q].get(sem, 0) >= val:
            return
        Q[q].wait_ge(T.sem[sem], val)
        for s_, v_ in list(clock.items()) + [(sem, val)]:
            if known[q].get(s_, 0) < v_:
                known[q][s_] = v_

    def order(q, reads, writes, tok_of):
        acc = [(x, False) for a_ in reads for x in a_["regs"] + a_["offs"]]
        acc += [(x, True) for a_ in writes for x in a_["regs"]] + [(x, False) for a_ in writes for x in a_["offs"]]
        need = []
        for (name, p0, p1, c0, c1, p0x), wr in acc:
            for e in log.get(name, []):
                if e[0] < p1 and p0 < e[1] and e[2] < c1 and c0 < e[3]:
                    if name != "ps":
                        if wr or e[4]:
                            need.append(e[6])
                    elif e[5] != q:
                        need.append(e[6])
                    elif q != "p" and (wr or e[4]) and e[0] < p1 and e[7] < p0x[1] and p0x[0] < e[8]:
                        need.append(e[6])
        need.sort(key=lambda t_: -(t_[1] or 0))
        for t_ in need:
            wait(q, t_)
        tok = tok_of()
        for (name, p0, p1, c0, c1, p0x), wr in acc:
            old = log.get(name, [])
            if name == "ps":
                old = [e for e in old if not (c0 <= e[2] and e[3] <= c1 and (e[5] != q or q == "p"))]
            elif wr:
                old = [e for e in old if not (p0 <= e[0] and e[1] <= p1 and c0 <= e[2] and e[3] <= c1)]
            log[name] = old + [[p0, p1, c0, c1, wr, q, tok, p0x[0], p0x[1]]]
        return tok

    def op(q, fn, reads, writes):
        def emit():
            sem = "q" + q
            fn().then_inc(T.sem[sem], 1)
            cnt[sem] += 1
            return (sem, cnt[sem], dict(known[q]))
        return order(q, reads, writes, emit)

    def dma(q, out, in_, sem):
        def emit():
            Q[q].dma_start(out["ap"], in_["ap"]).then_inc(T.sem[sem], 16)
            cnt[sem] = cnt.get(sem, 0) + 16
            return (sem, None, dict(known[q]))
        return order(q, [in_], [out], emit)

    def ext(a_):
        return {"ap": a_, "regs": [], "offs": []}

    def engines(d):
        return topo.engines(core, T.cores[d])

    def send(d, out, in_, sem):
        def emit():
            rid, pid = topo.addr(T.cores[d], core)
            g.remote_dma(out["ap"], in_["ap"], T.sem[sem], T.sem.rl, pid, rid, topo.mask(core, T.cores[d]))
            cnt["rl"] = cnt.get("rl", 0) + len(engines(d))
            return ("rl", None, {})
        return order("g", [in_], [], emit)

    def lands(a_, sem, n):
        cnt[sem] = n
        for name, p0, p1, c0, c1, _ in a_["regs"]:
            log.setdefault(name, []).append([p0, p1, c0, c1, True, "far", (sem, n, {}), c0, c1])

    def sc_(x):
        return x["ap"] if isinstance(x, dict) else x

    def tt(out, a_, b_, o):
        return op("v", lambda: g.vector.tensor_tensor(out["ap"], a_["ap"], b_["ap"], o), [a_, b_], [out])

    def ts(out, a_, s1, o1, s2=None, o2=None):
        rd = [a_] + [x for x in (s1, s2) if isinstance(x, dict)]
        if o2 is None:
            return op("v", lambda: g.vector.tensor_scalar(out["ap"], a_["ap"], sc_(s1), None, o1), rd, [out])
        return op("v", lambda: g.vector.tensor_scalar(out["ap"], a_["ap"], sc_(s1), sc_(s2), o1, o2), rd, [out])

    def cp(q, out, a_, scale=None):
        if q == "g":
            return asel(out, a_, [[0, a_["regs"][0][4] - a_["regs"][0][3]]], A.is_ge, 0.0, 0)
        if q == "v":
            if scale is not None:
                return ts(out, a_, scale, A.mult)
            return op("v", lambda: g.vector.tensor_copy(out["ap"], a_["ap"]), [a_], [out])
        if scale is None:
            return op("s", lambda: g.scalar.activation(out["ap"], a_["ap"], ACT.Copy), [a_], [out])
        return op("s", lambda: g.scalar.activation(out["ap"], a_["ap"], ACT.Copy, scale=scale), [a_], [out])

    def act(out, a_, func, scale, bias):
        return op("s", lambda: g.scalar.activation(out["ap"], a_["ap"], func, bias=bias["ap"], scale=scale), [a_, bias], [out])

    def ms(out, val):
        return op("v", lambda: g.vector.memset(out["ap"], val), [], [out])

    def scan(out, a_, b_, init, o1, o2):
        return op("v", lambda: g.vector.tensor_tensor_scan(out["ap"], a_["ap"], b_["ap"], init, o1, o2), [a_, b_], [out])

    def mm(out, lhs, rhs, start=True, stop=True):
        return op("p", lambda: g.tensor.matmul(out["ap"], lhs["ap"], rhs["ap"], start, stop), [lhs, rhs], [out])

    def iota(out, pat, base, cm, flt=True):
        if flt:
            return op("g", lambda: g.iota(out["ap"], pat, base, cm, allow_small_or_imprecise_dtypes=True), [], [out])
        return op("g", lambda: g.iota(out["ap"], pat, base, cm), [], [out])

    def asel(out, a_, pat, cmp_, fill, base):
        wait("g", ("qg", cnt["qg"], {}))
        return op("g", lambda: g.affine_select(out["ap"], a_["ap"], pat, cmp_, fill, base, 1), [a_], [out])

    def blkp(q):
        return (32 * q, 32 * q + 32)

    def bank(b, a_=0, n=512):
        return c("ps", 512 * b + a_, 512 * b + a_ + n)

    def sm(k, n=24):
        return ap("sm", slice(None), k, slice(0, n))

    def turn(m):
        return c("agi", 32 * m, 32 * m + 128)

    def lane(e):
        return c("we", 15 - e, 143 - e)

    ne = len(engines((r + 1) % N))
    others = [(r + k) % N for k in (1, 2, 3)]
    for s in others:
        for name, w in WIDE.items():
            lands(c("l" + name, w * s, w * s + w), "ar%s%d" % (name, s), ne)
        lands(ap("lc", s), "arc%d" % s, ne)
        lands(c("lo", 256 * s, 256 * s + 160), "arw%d" % s, ne)
        lands(c("lo", 256 * s + 160, 256 * s + 256), "aro%d" % s, ne)
    for t in range(1, TR):
        lands(c("nr", 24 * t, 24 * t + 24), "arn%d" % t, ne)

    def pack(name, d, a_, b_, p=None):
        o = WIDE[name] * others.index(d)
        return c("s" + name, o + a_, o + b_, p=p)

    def landed(name, s, a_, b_, u):
        return c("l" + name, WIDE[name] * s + a_, WIDE[name] * s + b_, p=blkp(u))

    def post(name, d):
        w = WIDE[name]
        send(d, c("l" + name, w * r, w * r + w), pack(name, d, 0, w), "ar%s%d" % (name, r))

    def load(name, w, src, d):
        for u in range(4):
            dma("ys"[u % 2], pack(name, d, 0, w, blkp(u)), ext(src[32 * d:32 * d + 32, w * u:w * u + w]), "ld%s%d" % (name, d))

    def take(name, w, s, buf, qs, scale=None):
        for u in range(4):
            cp(qs[u], c(buf, w * u, w * u + w, p=blkp(s)), landed(name, s, 0, w, u), scale)

    for d in others:
        load("a", 96, T.cin, d)
    dma("y", c("et", 0, 384), ext(T.ein[:, :]), "lde")
    dma("s", c("sab", 0, 40), ext(T.ra[:, :]), "ldab")
    dma("s", c("sab", 40, 80), ext(T.rb[:, :]), "ldab")
    for d in others:
        load("r", 160, T.kin, d)
    dma("y", c("si", 0, 384), ext(T.rx[:, :]), "ldi")
    dma("s", c("sj", 0, 384), ext(T.ot[:, :]), "ldi")
    dma("y", c("cw", 0, 384, p=blkp(r)), ext(T.cin[32 * r:32 * r + 32, :]), "lda%d" % r)
    dma("s", c("wt", 0, 640, p=blkp(r)), ext(T.kin[32 * r:32 * r + 32, :]), "ldr%d" % r)

    iota(c("ci", 0, 1), [[0, 1]], 0, 1, False)
    iota(c("io2", 0, 128), [[16, 8], [0, 16]], 0, 0)
    iota(c("iv", 0, 256), [[0, 2], [-1, 128]], 0, 1)
    iota(c("io2", 128, 144), [[1, 16]], 0, 0)
    iota(c("io2", 144, 184), [[16, 40]], 0, 1)
    for d in others:
        post("a", d)

    for d in others:
        ms(pack("r", d, 160, 200, (64, 128)), 0.0)
    ms(c("we", 0, 144), 0.0)
    ts(c("ci", 1, 2), c("ci", 0, 1), 112, A.bitwise_and)
    ts(c("ci", 2, 3), c("ci", 0, 1), 15, A.bitwise_and)
    cp("v", c("cf", 0, 3), c("ci", 0, 3))
    kg16, pmod = c("cf", 1, 2), c("cf", 2, 3)
    ts(c("we", 15, 143, 16), c("io2", 0, 128, 16), kg16, A.is_equal)
    ts(c("agi", 0, 256), c("iv", 0, 256), 0.0, A.is_equal)
    ts(c("blk", 0, 128), c("io2", 0, 128), kg16, A.is_equal, 2.0 ** -9, A.mult)
    ts(c("trn0", 0, 128), c("io2", 0, 128), kg16, A.is_equal, -2.0 ** -9, A.mult)
    ms(c("mz", 0, 128), 0.0)
    cp("s", c("mt", 0, 128), c("agi", 0, 128), 2.0)
    tt(c("m0", 0, 128), c("mt", 0, 128), c("agi", 16, 144), A.add)
    for o in range(0, 896, 224):
        cp("s", c("dw", o, o + 224), c("iv", 0, 224), 0.0)
    cp("s", c("tz", 384, 768), c("dw", 0, 384))
    ts(c("j40", 0, 40), c("io2", 144, 184), kg16, A.subtract)
    ts(c("idg", 0, 16), c("io2", 128, 144), pmod, A.is_equal, -1.0, A.mult)
    ms(c("one", 0, 40), 1.0)
    ms(c("cf", 4, 5), -(0.125 * LIFT - 2.0 ** -7) * 2.0 ** 25)
    ms(c("cf", 5, 6), 0.125 * LIFT)
    ts(c("dump", 0, 24), c("j40", 0, 24), 4096.0, A.add)

    def order_of(t):
        ts(c("k2", 30 * t, 24 * t + 24), c("j40", 6 * t, 24), -1.0, A.mult, 511.0 + 96.0 * t, A.add)
        if t:
            ts(c("k2", 24 * t, 30 * t), c("j40", 0, 6 * t), -1.0, A.mult, 127.0 + 96.0 * t, A.add)

    order_of(0)
    ms(c("lst", S0, S0 + 256), 0)
    ts(c("ind", 0, 384), c("et", 0, 384), 0.125, A.is_ge)
    for e in range(16):
        mm(bank(4, 0, 24), lane(e), c("ind", e, 384, 16), e == 0, e == 15)
    ts(c("sar", 0, 80), c("sab", 0, 80), float(SO * r), A.is_lt, float(N * SO), A.mult)
    ms(c("msk", 0, 1280), 1.0)
    cp("v", c("nw", 0, 24), bank(4, 0, 24))
    mm(bank(5, 0, 24), c("m0", 0, 128), c("nw", 0, 24))
    tt(c("sar", 80, 160), c("sar", 0, 80), c("sab", 0, 80), A.add)
    for d in others:
        ts(pack("r", d, 160, 184, blkp(2)), c("ps", 2560, 2584, p=blkp(d)), 23.5, A.is_ge, 512.0, A.mult)
        for h in range(2):
            ts(pack("r", d, 160, 200, blkp(h)), c("sar", 80 + 40 * h, 120 + 40 * h, p=blkp(d)), -float(SO * r), A.add)
        post("r", d)
    ms(c("msk", 0, 1280, 16), 0.0)
    ts(c("kab", 640, 720, p=blkp(r)), c("sar", 80, 160, p=blkp(r)), -float(SO * r), A.add)
    ts(c("ll", 8, 32, p=blkp(r)), c("ps", 2560, 2584, p=blkp(r)), 23.5, A.is_ge, 512.0, A.mult)
    for d in others:
        for h in range(2):
            cp("s", pack("b", d, 0, 192, blkp(2 + h)), c("et", 192 * h, 192 * h + 192, p=blkp(d)), LIFT)
    cp("s", c("ea", 4096, 4480, p=blkp(r)), c("et", 0, 384, p=blkp(r)), LIFT)
    cp("s", c("kab", 0, 640, p=blkp(r)), c("wt", 0, 640, p=blkp(r)), KUP)
    ts(bank(0, 0, 384), c("si", 0, 384), 4096.0, A.mult, -4096.0 * RO * r - SO * r, A.add)
    ts(bank(1, 0, 384), c("si", 0, 384), float(RO * r), A.is_lt, 4096.0 * N * RO, A.mult)
    ts(bank(2, 0, 384), c("sj", 0, 384), float(SO * r), A.is_lt, float(N * SO), A.mult)
    tt(c("sk", 0, 384), c("sj", 0, 384), bank(0, 0, 384), A.add)
    wait("y", ("qv", cnt["qv"], {}))
    for k, d in enumerate(others):
        dma("y", c("stau", 96 * k, 96 * k + 96), ext(T.tau[32 * d:32 * d + 32, :]), "ldb")
    dma("y", ap("lc", r), ext(T.tau[32 * r:32 * r + 32, :]), "lco")
    for s in others[::-1]:
        take("a", 96, s, "cw", "ssss")
    tt(c("sl", 0, 384), c("sk", 0, 384), bank(1, 0, 384), A.add)
    for m in (1, 2, 3):
        mm(bank(4 + m, 0, 384), turn(m), c("cw", 0, 384))
    tt(c("sk", 0, 384), c("sl", 0, 384), bank(2, 0, 384), A.add)
    for d in others:
        for h in range(2):
            cp("v", pack("b", d, 0, 192, blkp(h)), c("sk", 192 * h, 192 * h + 192, p=blkp(d)))
        post("b", d)
    cp("v", c("pk", 0, 384, p=blkp(r)), c("sk", 0, 384, p=blkp(r)))
    for m in (1, 2, 3):
        cp("s", c("cw", 384 * m, 384 * m + 384), bank(4 + m, 0, 384))
    asel(c("trn", 0, 128), c("trn0", 0, 128), [[-1, 128]], A.is_ge, 0.0, 0)
    for k, d in enumerate(others):
        send(d, ap("lc", r), c("stau", 96 * k, 96 * k + 96), "arc%d" % r)
    for s in others[::-1]:
        for h in range(2):
            cp("v", c("kab", 640 + 40 * h, 680 + 40 * h, p=blkp(s)), landed("r", s, 160, 200, h))
        cp("v", c("ll", 8, 32, p=blkp(s)), landed("r", s, 160, 184, 2))
        if s == others[0]:
            cp("v", c("ab16", 0, 80), c("kab", 640, 720))
        take("r", 160, s, "kab", "vsvs" if s == others[0] else "vvvv", KUP)

    def take_b(q, s, buf, base, u):
        for h in range(2):
            cp(q, c(buf, base + 192 * h, base + 192 * h + 192, p=blkp(s)), landed("b", s, 0, 192, u + h))

    def swap(q, buf, a_, to, width, h):
        cp(q, c(buf, to, to + width, p=(64 * h, 64 * h + 64)), c(buf, a_, a_ + width, p=(64 - 64 * h, 128 - 64 * h)))

    def turn_half(q, buf, base, width, h):
        swap(q, buf, base, base + 2 * width, width, h)

    def turn_dma(buf, base, width, sem):
        for m in (1, 3):
            o = base + m * width
            dma("y", c(buf, o, o + width, p=(0, 128 - 32 * m)), c(buf, base, base + width, p=(32 * m, 128)), sem)
            dma("y", c(buf, o, o + width, p=(128 - 32 * m, 128)), c(buf, base, base + width, p=(0, 32 * m)), sem)
        for h in range(2):
            turn_half("g", buf, base, width, h)

    def e_window(buf, ms_=(1, 2, 3)):
        for m in ms_:
            mm(bank(4 + m, 0, 384), turn(m), c(buf, 4096, 4480))

    def e_out(buf, ms_=(1, 2, 3)):
        for m in ms_:
            cp("s", c(buf, 4096 + 384 * m, 4480 + 384 * m), bank(4 + m, 0, 384))

    def w_window(q):
        parts = [(1, 0), (1, 320), (3, 320)] + ([(3, 0)] if q == "v" else [])
        for b, (m, h) in enumerate(parts):
            mm(bank(b, 128, 320), turn(m), c("wm", h, h + 320))
        for h, n in ((0, 320), (320, 320)) if q == "g" else ((0, 640),):
            swap(q, "wm", h, 1280 + h, n, 0)
        swap("s", "wm", 0, 1280, 640, 1)
        for b, (m, h) in enumerate(parts):
            cp("s", c("wm", 640 * m + h, 640 * m + h + 320), bank(b, 128, 320))
            if b == 0 and q == "g":
                swap("g", "wm", 640, 1920, 320, 0)
                swap("s", "wm", 640, 1920, 320, 1)

    def new_rates(out, t):
        if t == 0:
            tt(c("wt", 0, 640), ind(c("cw", 0, 1536), c("ab16", 0, 40)), c("kab", 0, 640), A.mult)
            cp("s", c("cb", 0, 640), ind(c("cw", 0, 1536), c("ab16", 40, 80)), 1.0 / KUP)
        else:
            scan(c("wt", 0, 640), c("ca", 0, 640), c("kab", 0, 640), 8.0, A.min, A.mult)
            order_of(t)
        scan(out, c("cb", 0, 640), c("wt", 0, 640), 1.0, A.min, A.mult)

    def products(e_, a_, b_, hy):
        if a_ < hy:
            tt(c("prod", 16 * a_, 16 * b_), ind(c(e_, 4096, 5632), c("ot16", a_, b_)), c("wg", 16 * a_, 16 * b_), A.mult)
        else:
            scan(c("prod", 16 * a_, 16 * b_), c("wg", 16 * a_, 16 * b_), c("eg", 16 * (a_ - HY), 16 * (b_ - HY)), 1.0, A.min, A.mult)

    def maxima(e_, a_, b_):
        scan(c(e_, 16 * a_, 16 * b_), c("msk", 0, 16 * (b_ - a_)), c("prod", 16 * a_, 16 * b_), 0.0, A.mult, A.max)

    def spread(e_, to):
        tt(c(to, 4096, 4480), ind(c(e_, 0, 4480), c("pe16", 0, 24)), c("taum", 0, 384), A.max)

    def least():
        cp("s", c("taum", 0, 384), ind(c("tz", 0, 768), c("tz16", 0, 24)))

    def bound():
        act(c("thr", 0, 384), c("taum", 0, 384), ACT.Relu, 2.0 ** 25, c("cf", 4, 5))
        act(c("thr", 0, 384), c("thr", 0, 384), ACT.Identity, -1.0, c("cf", 5, 6))

    for t in range(TR):
        wn, wo = "w%d" % (t % 2), "w%d" % ((t + 1) % 2)
        nw, nr = c("nw", 24 * t, 24 * t + 24), c("nr", 24 * t, 24 * t + 24)
        lw = c("ll", 32, 56) if t else c("ll", 8, 32)
        p, q_ = 6 * t, 10 * t
        pos = bank(4, 256, 24)

        def counts():
            scan(c("css", 0, 24), c("ll", 8 + p, 32 + p), c("one", 0, 24), 0.0, A.add, A.mult)
            tt(sm(0), lw, c("k2", 24 * t, 24 * t + 24), A.max)

        def places():
            mm(pos, c("trn", 0, 128), lw, True, False)
            mm(bank(4, 256 + p, 24 - p), c("blk", 0, 128), c("css", 0, 24 - p), False, False)
            if p:
                mm(bank(4, 256, p), c("blk", 0, 128), c("css", 24 - p, 24), False, False)
            mm(pos, turn(0), sm(0), False, True)

        def in_picks():
            ts(sm(2), pos, -S0 - 127.5, A.add)
            ts(sm(1), pos, 16.0, A.mult, 15.0 - 16 * S0, A.add)
            tt(sm(3), sm(2), sm(2), A.mult)
        if t:
            tt(c("ind", 0, 384), ind(c("eb", 0, 4480), c("pe16", 0, 24)), c("thr", 0, 384), A.is_ge)
            for e in range(16):
                mm(bank(4, 0, 24), lane(e), c("ind", e, 384, 16), e == 0, e == 15)
            spread("eb", "ea")
            cp("s" if t > 1 else "v", nw, bank(4, 0, 24))
            send((r - 1) % N, nr, nw, "arn%d" % t)
            e_window("ea", (1, 3))
            turn_half("g", "ea", 4096, 384, 0)
            turn_half("s", "ea", 4096, 384, 1)
            new_rates(c(wo, 0, 640), t)
            if t == 1:
                cp("v", c("abd16", 40, 70), c("abt", 0, 30))
                cp("v", c("abd16", 80, 120), c("abt", 40, 80))
                cp("v", c("abd16", 120, 150), c("abt", 40, 70))
            e_out("ea", (1, 3))
            for k, (sel, n_) in enumerate((("ma", nw), ("mb", nr))):
                for m in (0, 1, 2, 3, -1):
                    x = 32 * max(m, 0)
                    mm(bank(4, 64 + 24 * m, 24), c(sel, x, x + 128), n_, k == 0 and m == 0, k == 1 and m == -1)
            ts(c("ll", 8, 128), bank(4, 40, 120), 23.5, A.is_ge, 512.0, A.mult)
            cp("s", c("xb", 0, 640), ind(c("ll", 32, 128), c("abd16", 80 + q_, 120 + q_)))
            tt(c("xab", 0, 640), ind(c("ll", 32, 128), c("abd16", q_, 40 + q_)), c("oh", 16 * q_, 16 * q_ + 640), A.mult)
            counts()
            scan(c("xab", 640, 1280), c("xb", 0, 640), c("oh", 1120 + 16 * q_, 1760 + 16 * q_), 0.0, A.max, A.mult)
            for x in range(32):
                o = 640 * (x // 16)
                if x == 16:
                    places()
                mm(bank(3, 0, 40), lane(x % 16), c("xab", o + x % 16, o + 640, 16), x == 0, x == 31)
            cp("v", c("pos16", 0, 24), pos)
            in_picks()
            ts(c("act", 0, 40), bank(3, 0, 40), -0.5, A.is_le, 512.0, A.mult)
            ts(sm(4), sm(3), 16384.0, A.is_ge, 16384.0, A.mult)
            scan(c("csr", 0, 40), c("act", 0, 40), c("one", 0, 40), 0.0, A.add, A.mult)
            for o, a_, n in ((q_, 0, 40 - q_), (0, 40 - q_, q_)):
                mm(bank(3, 64 + o, n), c("trn2", 0, 128), c("act", a_, a_ + n), True, False)
                mm(bank(3, 64 + o, n), c("blk", 0, 128), c("csr", a_, a_ + n), False, True)
            ts(sm(7), sm(3), 16384.0, A.is_ge, 384.0, A.mult)
            tt(sm(5), sm(4), sm(1), A.add)
            tt(sm(2), sm(7), c("j40", 0, 24), A.add)
            ts(sm(8, 40), bank(3, 64, 40), -640.0, A.is_gt, 640.0, A.mult)
            tt(sm(6), sm(5), c("dump", 0, 24), A.min)
            tt(sm(9, 40), sm(8, 40), c("j40", 0, 40), A.add)
            cp("v", c("tz16", 0, 24), sm(2))
            cp("v", c("wo16", 0, 40), sm(9, 40))
            for h in (0, 20):
                ts(c("wm", 16 * h, 16 * h + 320), ind(c(wo, 0, 1280), c("wo16", h, h + 20)), 1.0, A.min)
            cp("s", c(wn, 640, 1280), ind(c(wo, 0, 1280), c("wo16", 0, 40)))
            w_window("g")
            turn_dma(wn, 640, 640, "wr%d" % t)
            if t == TR - 1:
                for k, d in enumerate(others):
                    dma("y", c("so", 256 * k, 256 * k + 160), c(wn, 640, 1280, p=blkp(d)), "pko%d" % d)
                dma("y", ext(T.yw[32 * r:32 * r + 32, :]), c(wn, 640, 1280, p=blkp(r)), "st")
                for k, d in enumerate(others):
                    send(d, c("lo", 256 * r, 256 * r + 160), c("so", 256 * k, 256 * k + 160), "arw%d" % r)
                for s in others[::-1]:
                    dma("y", ext(T.yw[32 * s:32 * s + 32, :]), c("lo", 256 * s, 256 * s + 160), "st")
        else:
            counts()
            places()
            new_rates(c(wn, 640, 1280), t)
            take_b("s", others[2], "pk", 0, 0)
            take_b("s", others[1], "pk", 0, 0)
            cp("v", c("pos16", 0, 24), pos)
            ts(c("wm", 0, 640), c(wn, 640, 1280), 1.0, A.min)
            in_picks()
            take_b("g", others[2], "ea", 4096, 2)
            w_window("v")
            take_b("g", others[1], "ea", 4096, 2)
            ts(sm(4), sm(3), 16384.0, A.is_ge, 16384.0, A.mult)
            ts(sm(7), sm(3), 16384.0, A.is_ge, 384.0, A.mult)
            tt(sm(5), sm(4), sm(1), A.add)
            take_b("g", others[0], "ea", 4096, 2)
            take_b("v", others[0], "pk", 0, 0)
            e_window("ea", (1, 3))
            turn_half("g", "ea", 4096, 384, 0)
            turn_dma(wn, 640, 640, "wr%d" % t)
            dma("y", c("tau_o", 0, 384), ap("lc"), "lbt")
        cp("v", ind(c("lst", 0, 896), c("pos16", 0, 24)), c("pk", 0, 384))
        if t == 0:
            tt(sm(2), sm(7), c("j40", 0, 24), A.add)
            tt(sm(6), sm(5), c("dump", 0, 24), A.min)
        ts(c("lo_i", 0, 256), c("lst", S0, S0 + 256), 4095, A.bitwise_and)
        ts(c("rx16", 0, 256), c("lst", S0, S0 + 256), 2.0 ** -12, A.mult)
        if t == 0:
            cp("v", c("tz16", 0, 24), sm(2))
        cp("v", c("ot16", 0, 256), c("lo_i", 0, 256))
        if t == 0:
            turn_half("s", "ea", 4096, 384, 1)
            e_out("ea", (1, 3))
        for a_, b_ in CH1[1:]:
            cp("s", c("wg", 16 * a_, 16 * b_), ind(c("wm", 0, 2560), c("rx16", a_, b_)))
        for a_, b_ in XCH:
            cp("s", c("xg", 16 * a_, 16 * b_), ind(c(wn, 640, 3200), c("rx16", 80 + a_, 80 + b_)), 0.125)
            for e in ((0, 1) if a_ < NA else ()):
                mm(c("ps", 4 * a_, 4 * b_), turn(0), c("xg", 16 * a_ + e, 16 * b_, 4), e == 0, e == 1)
            for e in (2, 3):
                mm(c("ps", 1536 + 4 * a_, 1536 + 4 * b_), turn(0), c("xg", 16 * a_ + e, 16 * b_, 4), e == 2, e == 3)
        if t == 0:
            cp("s", c("tz", 0, 384), c("tau_o", 0, 384), LIFT)
        least()
        cp("s", bank(1, 0, 704 - 4 * NA), c("xg", 16 * NA + 1, 2816, 4))
        cp("s", c("y1", 0, 4 * NA), bank(0, 0, 4 * NA))
        cp("v", c("wg", 0, 16 * CH1[0][1]), ind(c("wm", 0, 2560), c("rx16", *CH1[0])))
        cp("v", c("pe16", 0, 24), sm(6))
        products("ea", *CH1[0], 256)
        for x in range(1, len(CH1)):
            products("ea", *CH1[x], 256)
            maxima("ea", *CH1[x - 1])
        maxima("ea", *CH1[-1])
        spread("ea", "eb")
        e_window("eb", (1, 3))
        turn_half("g", "eb", 4096, 384, 0)
        turn_half("s", "eb", 4096, 384, 1)
        e_out("eb", (1, 3))
        tt(c("y1", 4 * NA, 704), c("xg", 16 * NA, 2816, 4), bank(1, 0, 704 - 4 * NA), A.add)
        if t == 0:
            cp("v", c("abi", 0, 80), c("kab", 640, 720))
        tt(c("z1", 0, 352), c("y1", 0, 704, 2), c("ps", 1536, 2240, 2), A.add)
        tt(bank(0, 0, 352), c("y1", 1, 704, 2), c("ps", 1537, 2240, 2), A.add)
        if t == 0:
            ts(c("abt", 80, 160), c("abi", 0, 80), 15, A.bitwise_and)
        tt(c("p1", 0, 176), c("z1", 0, 352, 2), c("ps", 0, 352, 2), A.add)
        tt(bank(1, 0, 176), c("z1", 1, 352, 2), c("ps", 1, 352, 2), A.add)
        if t == 0:
            cp("v", c("abm16", 0, 80), c("abt", 80, 160))
        tt(c("dw", 512, 688), c("p1", 0, 176), bank(1, 0, 176), A.subtract)
        cp("s", c("ct", 0, 384), ind(c("dw", 0, 896), c("pos16", 0, 24)))
        mm(bank(2, 0, 384), turn(0), c("cw", 0, 384), True, False)
        mm(bank(2, 0, 384), turn(0), c("ct", 0, 384), False, True)
        for a_, b_ in CH2[1:]:
            cp("s", c("eg", 16 * (a_ - HY), 16 * (b_ - HY)), ind(c("eb", 4096, 5632), c("ot16", a_, b_)))
        if t < TR - 1:
            bound()
        products("eb", *CH2[0], HY)
        if t == 0:
            ts(c("abt", 0, 80), c("abi", 0, 80), 4, A.arith_shift_right)
        maxima("eb", *CH2[0])
        products("eb", *CH2[1], HY)
        ts(c("cw", 0, 384), bank(2, 0, 384), 0.125, A.max, 8.0, A.min)
        if t < TR - 1:
            turn_dma("cw", 0, 384, "cg%d" % t)
        else:
            for k, d in enumerate(others):
                dma("y", c("so", 256 * k + 160, 256 * k + 256), c("cw", 0, 384, p=blkp(d)), "pkc%d" % d)
            dma("y", ext(T.yc[32 * r:32 * r + 32, :]), c("cw", 0, 384, p=blkp(r)), "st")
            for k, d in enumerate(others):
                send(d, c("lo", 256 * r + 160, 256 * r + 256), c("so", 256 * k + 160, 256 * k + 256), "aro%d" % r)
            for s in others[::-1]:
                dma("y", ext(T.yc[32 * s:32 * s + 32, :]), c("lo", 256 * s + 160, 256 * s + 256), "st")
        for x in range(2, len(CH2)):
            products("eb", *CH2[x], HY)
            maxima("eb", *CH2[x - 1])
        if t < TR - 1:
            cp("s", c("ca", 0, 640), ind(c("cw", 0, 1536), c("ab16", 0, 40)))
            cp("s", c("cb", 0, 640), ind(c("cw", 0, 1536), c("ab16", 40, 80)), 1.0 / KUP)
        if t == 0:
            asel(c("ma", 0, 128), c("mt", 0, 128), [[-32, 4], [1000, 2], [-1, 16]], A.not_equal, 1.0, -16)
            asel(c("mb", 0, 128), c("mz", 0, 128), [[-32, 4], [-1000, 2], [-1, 16]], A.not_equal, 1.0, 1000)
            asel(c("trn2", 0, 128), c("trn", 0, 128), [[-1, 128]], A.not_equal, -2.0, 0)
            cp("s", c("ma", 128, 224), c("ma", 0, 96))
            cp("s", c("mb", 128, 224), c("mb", 0, 96))
            for h in range(2):
                cp("s", c("oh", 1120 * h, 1120 * h + 640), ind(c("idg", 0, 16), c("abm16", 40 * h, 40 * h + 40)))
                cp("s", c("oh", 1120 * h + 640, 1120 * h + 1120), c("oh", 1120 * h, 1120 * h + 480))
        maxima("eb", *CH2[-1])
        if t == 0:
            cp("v", c("abd16", 0, 40), c("abt", 0, 40))
    spread("eb", "ea")

    for k, d in enumerate(others):
        for u in range(4):
            cp("vs"[u % 2], c("se", 96 * k, 96 * k + 96, p=blkp(u)), c("ea", 4096 + 96 * u, 4192 + 96 * u, p=blkp(d)), 1.0 / LIFT)
        send(d, c("le", 96 * r, 96 * r + 96), c("se", 96 * k, 96 * k + 96), "are%d" % r)
    cp("v", c("et", 0, 384, p=blkp(r)), c("ea", 4096, 4480, p=blkp(r)), 1.0 / LIFT)
    for s in others[::-1]:
        lands(c("le", 96 * s, 96 * s + 96), "are%d" % s, ne)
        for u in range(4):
            dma("ys"[u % 2], ext(T.ye[32 * s:32 * s + 32, 96 * u:96 * u + 96]), c("le", 96 * s, 96 * s + 96, p=blkp(u)), "st")
        if s == others[2]:
            dma("y", ext(T.ye[32 * r:32 * r + 32, :]), c("et", 0, 384, p=blkp(r)), "st")
    for sem in cnt:
        if cnt[sem]:
            wait("g", (sem, cnt[sem], {}))
